import numpy as np, ml_dtypes
CORES = [6,15,38,47]
N = 4
import mx_ref
BF = ml_dtypes.bfloat16
def gentries(a):
    return np.ascontiguousarray(a.reshape(8, 16, -1).transpose(0, 2, 1)).reshape(8, -1)
def gtable(e):
    e = np.asarray(e); return np.ascontiguousarray(e.reshape(8, -1, 16).transpose(0, 2, 1)).reshape(128, -1).astype(np.int32)
def gcols(t, e):
    v = np.concatenate([t.reshape(8, 16, -1, 4), np.zeros((8, 16, 1, 4), BF)], axis=2)
    return np.ascontiguousarray(np.stack([v[g][:, e[g]] for g in range(8)])).reshape(128, -1)
def tile(rs):
    return np.stack(rs, axis=2).reshape(128, -1).astype(BF)
def pick(q, e):
    c = np.concatenate([q[0].reshape(128, -1, 4), np.zeros((128, 1, 4), np.uint8)], axis=1); s = np.concatenate([q[1], np.ones((16, 1), np.uint8)], axis=1)
    return (np.ascontiguousarray(c[:, e].reshape(128, -1)), np.ascontiguousarray(s[:, e]))
def join(*qs):
    return (np.concatenate([q[0] for q in qs], axis=1), np.concatenate([q[1] for q in qs], axis=1))
def put(q, e, v):
    c, s = q[0].reshape(128, -1, 4).copy(), q[1].copy(); c[:, e] = v[0].reshape(128, -1, 4); s[:, e] = v[1]
    return (c.reshape(128, -1), s)
def pk(c, s):
    return (np.ascontiguousarray(c), mx_ref.live(s))
def emit(q):
    return q[0], q[1]
def packed(v, rng):
    q = [mx_ref.quantize(np.ascontiguousarray(v[r])) for r in range(N)]
    return np.stack([a for a, b in q]), np.stack([mx_ref.plane(b, rng) for a, b in q])
def values_of_codes():
    e, c = np.zeros((128, 128, 4), np.float32), np.zeros((128, 2, 4), np.uint8)
    e[np.arange(128), np.arange(128), 0] = 1
    c[:127, :, 0] = np.arange(256).reshape(2, 128).T[:127]
    return mx_ref.matmul(mx_ref.quantize(e.reshape(128, 512).astype(BF)), (c.reshape(128, 8), np.full((16, 2), 127, np.uint8))).T.reshape(-1).astype(np.float64)
CODE_VALUE, SCALE_VALUE = values_of_codes(), 2.0 ** (np.arange(256) - 127.0)
def decode(q):
    return (CODE_VALUE[q[0]].reshape(16, 8, -1, 4) * SCALE_VALUE[q[1]][:, None, :, None] + 0.0).reshape(128, -1).astype(np.float32)
def f(rng, *shape):
    return mx_ref.flush((rng.standard_normal(shape, dtype=np.float32) * np.exp2(rng.integers(-2, 3, shape[:-1] + (1,)))).astype(BF))
def wide(rng, *shape, cols=0):
    v = rng.standard_normal(shape, dtype=np.float32) * np.exp2(rng.integers(-12, 13, shape)).astype(np.float32)
    if cols: v *= np.repeat(np.exp2(rng.integers(-cols, cols + 1, shape[:-2] + (1, shape[-1] // 4))) * (rng.random(shape[:-2] + (1, shape[-1] // 4)) > 0.0625), 4, axis=-1).astype(np.float32)
    return mx_ref.flush(v.astype(BF))
C, S, R = 288, 48, 3
L = 3 * C + 2 * S
def flipped(t, pos):
    h, a = np.arange(3 * C), t[:, :3 * C]
    o = np.where(a < 3 * C, a, h) // 3
    low = np.minimum(a, h)
    wants = np.take_along_axis(pos, o, axis=1) != np.repeat(pos, 3, axis=1)
    least = np.min(np.where(wants, low, L).reshape(8, C, 3), axis=2)
    go = wants & (h < a) & (low == np.repeat(least, 3, axis=1)) & (low == np.take_along_axis(least, o, axis=1))
    g, i = np.nonzero(go)
    j = a[g, i]
    i1, i2 = i // 3 * 3 + (i + 1) % 3, i // 3 * 3 + (i + 2) % 3
    j1, j2 = j // 3 * 3 + (j + 1) % 3, j // 3 * 3 + (j + 2) % 3
    phi = np.tile(np.arange(L), (8, 1))
    phi[g, i2] = i1
    phi[g, j1] = i2
    phi[g, j2] = j1
    phi[g, i1] = j2
    new = np.zeros_like(t)
    np.put_along_axis(new, phi, np.take_along_axis(phi, t, axis=1), axis=1)
    return new
def anyhow(rng):
    return np.argsort(rng.random((N, 8, 3 * C)), axis=2)
def strip(rng, q):
    return np.concatenate([rng.permutation(3 * q + 2), np.stack([3 * q + 1, 3 * np.roll(q, -1)], axis=1).reshape(-1)])
def pairs(rng):
    q = rng.permutation(C).reshape(2, C // 2)
    k = np.argsort(rng.random((C // 2, 3)), axis=1)
    e = np.stack([3 * q[0][:, None] + np.arange(3), 3 * q[1][:, None] + k], axis=2)
    kept = np.ones((C // 2, 3), bool)
    kept[rng.permutation(C // 2)[:S], rng.integers(0, 3, S)] = False
    return np.concatenate([rng.permutation(e[~kept].reshape(-1)), e[kept].reshape(-1)]), q[0], q[1]
def joined(p):
    s = np.broadcast_to(3 * C + np.arange(2 * S), (N, 8, 2 * S))
    a = np.concatenate([p[:, :, :2 * S], p[:, :, 2 * S::2]], axis=2)
    b = np.concatenate([s, p[:, :, 2 * S + 1::2]], axis=2)
    e = np.zeros((N, 8, L), np.int64)
    np.put_along_axis(e, a, b, axis=2)
    np.put_along_axis(e, b, a, axis=2)
    return np.stack([gtable(k) for k in e])
def drawn(rng, x, p, u, v, w):
    c, s = packed(w, rng)
    return {"x": x, "tw": joined(p), "u": u, "v": v, "wc": c, "ws": s}
def setup_inputs(rng):
    return drawn(rng, np.array(f(rng, N, 128, 4 * C)), anyhow(rng), np.array(f(rng, N, 128, 512)), np.array(f(rng, N, 128, 512)), np.array(f(rng, N, 128, 2048)))
def setup_inputs_near(rng):
    p = anyhow(rng)
    o = rng.permutation(N)
    c = rng.integers(-1, 2, (N, 8, R, C)).astype(np.float32)
    for r in range(N):
        if o[r] == 0:
            for g in range(8): p[r, g] = strip(rng, np.arange(C))
            c[r, :, 0] = -np.abs(c[r, :, 0])
            c[r, :, 0, ::2] = 1
        if o[r] == 1: c[r] = -np.abs(c[r])
        if o[r] == 2: c[r] = 1
        if o[r] == 3:
            for g in rng.permutation(8)[:4]:
                p[r, g], a, b = pairs(rng)
                c[r, g, 0] = -np.abs(c[r, g, 0])
                c[r, g, 0, a] = 1
    x = np.array(f(rng, N, 128, 4 * C)).astype(np.float32).reshape(N, 8, 16, C, 4)
    x[:, :, :8] = 0
    x[:, :, :R, :, 0] = c * np.exp2(np.array([-30.0, -12.0, 0.0, 10.0]))[rng.integers(0, 4, (N, 8, 1, C))]
    k = np.where(rng.permutation(N) < N // 2, 2.0 ** -30, 1.0).astype(np.float32).astype(BF)
    u = np.array(f(rng, N, 128, 512)).reshape(N, 128, 128, 4)
    for g in range(8):
        for i in range(16 * g, 16 * g + R):
            u[:, :, i] = 0
            u[:, i, i, 0] = k
    w = np.array(f(rng, N, 128, 2048)).reshape(N, 8, 16, 4, 8, 16, 4)
    w[:, :, :8] = 0
    w[:, :, :, :, :, :8] = 0
    return drawn(rng, x.reshape(N, 128, 4 * C).astype(BF), p, u.reshape(N, 128, 512), np.array(f(rng, N, 128, 512)), w.reshape(N, 128, 2048))
def setup_inputs_loops(rng):
    p = anyhow(rng)
    o = rng.permutation(N)
    n = (2 * S + 5) // 6 * 2
    three = np.arange(3)
    x = np.array(f(rng, N, 128, 4 * C)).reshape(N, 128, C, 4)
    for r in range(N):
        if o[r] % 3 == 2: x[r, :, ::C - 1] = BF(-2.0 ** 26)
        for g in range(8):
            q = rng.permutation(C)
            if o[r] % 3 == 0: p[r, g] = (3 * q[:, None] + three).reshape(-1)
            if o[r] % 3 == 1:
                a, b = q[n::2], q[n + 1::2]
                k = np.argsort(rng.random((len(a), 3)), axis=1)
                e = np.stack([3 * a[:, None] + three, 3 * b[:, None] + k], axis=2)
                p[r, g] = np.concatenate([(3 * q[:n, None] + three).reshape(-1), e.reshape(-1)])
            if o[r] % 3 == 2: p[r, g] = strip(rng, q)
    return drawn(rng, x.reshape(N, 128, 4 * C), p, np.array(f(rng, N, 128, 512)), np.array(f(rng, N, 128, 512)), np.array(f(rng, N, 128, 2048)))
def setup_inputs_huge(rng):
    o = rng.permutation(N)
    x = -2.0 ** 30 * np.where(rng.random((N, 128, 4 * C)) < 0.75, 1.0, 0.5 + 0.4 * rng.random((N, 128, 4 * C)))
    x[:, 15::16] = 2.0 ** 30 * np.where(rng.random((N, 8, 4 * C)) < 0.75, -1.0, 0.5)
    s = np.argsort(rng.random((N, 128, 128)), axis=1) % 2 * 2.0 - 1.0
    s[o == 0] = 1
    s[o == 1] = -1
    u = 2.0 ** 30 * (0.75 + 0.25 * rng.random((N, 128, 128, 4))) * s[:, :, :, None]
    w = np.zeros((N, 128, 4, 128, 4), np.float32)
    i = np.arange(128)
    for b in range(4): w[:, i, b, i, b] = np.where(i % 16 == 15, -8, -24)
    return drawn(rng, x.astype(np.float32).astype(BF), anyhow(rng), u.astype(np.float32).reshape(N, 128, 512).astype(BF), np.array(f(rng, N, 128, 512)), w.reshape(N, 128, 2048).astype(BF))
def setup_inputs_spread(rng):
    d = setup_inputs(rng)
    d["x"] = np.array(wide(rng, N, 128, 4 * C, cols=6))
    return d
def check_inputs(d):
    b = []
    for k in ("x", "u", "v"):
        a = np.abs(d[k].astype(np.float32))
        if not (np.isfinite(a).all() and ((a == 0) | (a >= 2.0 ** -30) & (a <= 2.0 ** 30)).all()): b.append("a value of " + k)
    for r in range(N):
        t = gentries(d["tw"][r]).astype(np.int64)
        if ((t < 0) | (t >= L)).any(): b.append("an entry of tw")
        t = np.clip(t, 0, L - 1)
        if (np.take_along_axis(t, t, axis=1) != np.arange(L)).any(): b.append("tw: a twin's twin")
        if (t == np.arange(L)).any(): b.append("tw: a number is its own twin")
        if (t[:, 3 * C:] >= 3 * C).any(): b.append("tw: a slot's twin is a slot")
    return b
def reference(x, tw, u, v, wc, ws):
    qu = [mx_ref.quantize(u[r]) for r in range(N)]
    lay = [pk(wc[r], ws[r]) for r in range(N)]
    now = [x[r] for r in range(N)]
    twin = [gentries(tw[r]).astype(np.int64) for r in range(N)]
    for t in range(R):
        held, right, left = [], [], []
        for r in range(N):
            q = mx_ref.quantize(now[r])
            twin[r] = flipped(twin[r], mx_ref.matmul(qu[r], q)[t::16] > 0)
            held.append(decode(q))
            e = twin[r][:, 3 * C:] // 3
            right.append(mx_ref.quantize(gcols(now[r], e[:, :S])))
            left.append(mx_ref.quantize(gcols(now[r], e[:, S:])))
        for r in range(N):
            came = decode(join(left[(r + 1) % N], right[(r - 1) % N]))
            z = np.concatenate([held[r], came], axis=1).astype(BF)
            a = twin[r][:, :3 * C]
            e = np.where(a < 3 * C, a // 3, a - 2 * C)
            p = [gcols(z, e[:, k::3]).astype(np.float32) for k in range(3)]
            q = mx_ref.quantize(np.maximum(np.maximum(p[0], p[1]), p[2]).astype(BF))
            now[r] = tile([held[r][:, b::4] + np.maximum(mx_ref.matmul(pick(lay[r], np.arange(128 * b, 128 * b + 128)), q), np.float32(0.0)) * np.float32(0.015625) for b in range(4)])
    y, ot = np.zeros((N, 128, C), np.float32), np.zeros((N, 8, L), np.float32)
    oc, osc = np.zeros((N, 128, 4 * C), np.uint8), np.zeros((N, 16, C), np.uint8)
    for r in range(N):
        q = mx_ref.quantize(now[r])
        y[r] = mx_ref.matmul(mx_ref.quantize(v[r]), q)
        ot[r] = twin[r]
        oc[r], osc[r] = emit(q)
    return {"y": y, "ot": ot, "oc": oc, "osc": osc}

@@ -1,0 +1,543 @@
+from concourse.bass import DstId, RemoteDMATransfer
+from concourse.mybir import dt, AluOpType, ActivationFunctionType
+
+C, S, R = 288, 48, 3
+FP8 = "float8_e4m3fn_x4"
+BIG = float(2 ** 32)
+NONE = 1536
+NOWHERE = 2047 * 4096.0
+EARLY = 1
+
+SCRATCH = {"ps": ("psum", [128, 4096], "float32")}
+for _d, _bufs in (
+    ("bfloat16", {"xin": 4 * C, "xt": 4 * C, "mt": 4 * C, "ub": 512, "vb": 512, "eb": 520, "ones": 128, "ident": 128,
+                  "cm": 1152, "sb": 1152, "bits": 1248, "dw": 4 * 384, "dn": 4 * 576, "g0": 2 * C, "g1": 2 * C,
+                  "gi": 4 * C, "go": 4 * C, "two": 2 * C}),
+    ("float32", {"c0": 16, "c1": 16, "col": 8, "vw": 18, "base4": 384, "inttab": 960, "itab": 1540, "ntab": 1540,
+                 "otab": 1536, "tfn": 960, "otf": 960, "so": 960, "pw": 72, "w": 54, "wp": 54, "pr": 54, "hb": 54,
+                 "hc": 54, "kb": 42, "af": C, "nf": 384, "pf": 384, "inf": 384, "zf": 384, "gf": 864, "rl": 4 * C,
+                 "yb": C}),
+    ("int32", {"twb": 64, "r16": 16, "r16b": 16, "coli": 8, "c16": 18, "uoi": 24, "key": 216, "k1": 72, "best": 72,
+               "tb": 90, "hs": 54, "th": 36, "lb": 60, "xb": 60, "mb": 60, "db": 60, "ib": 60, "lo": 60, "t1": 60,
+               "t2": 60, "t3": 60, "idx": 18, "aq": 24, "xz": 18}),
+    ("uint16", {"tw16": 64, "uoff": 24, "offn": 18, "offp": 18, "e2": 54, "e54": 54, "esl": 6, "oto": 60, "esend": 24}),
+    (FP8, {"wq": 512, "uq": 128, "uq2": 384, "vq": 128, "eq": 512, "mq": C}),
+    ("uint8", {"wsc": 512, "us": 128, "us2": 384, "vs": 128, "es": 512, "ms": C}),
+):
+    for _n in _bufs:
+        SCRATCH[_n] = ("sbuf", [128, _bufs[_n]], _d)
+for _t in range(R + 1):
+    SCRATCH["qx%d" % _t] = ("sbuf", [128, C], FP8)
+    SCRATCH["sx%d" % _t] = ("sbuf", [128, C], "uint8")
+for _t in range(R):
+    SCRATCH["lq%d" % _t] = ("sbuf", [128, 2 * C], FP8)
+    SCRATCH["ls%d" % _t] = ("sbuf", [128, 2 * C], "uint8")
+    SCRATCH["lst%d" % _t] = ("sbuf", [128, 8], "uint16")
+
+POOL = {"v": 48, "s": 36, "t": 24, "g": 10}
+NDMA = 16
+SEMAPHORES = (["%s%d" % (q, i) for q in POOL for i in range(POOL[q])] + ["d%d" % i for i in range(NDMA)]
+              + ["%s%d" % (n, t) for n in ("fp", "fn", "lst") for t in range(R)] + ["sent"])
+
+A = AluOpType
+F = ActivationFunctionType
+
+
+def meet(a, b):
+    if a[0] != b[0] or a[2] <= b[1] or b[2] <= a[1]:
+        return False
+    return not (a[3] > 1 and a[3] == b[3] and (a[1] - b[1]) % a[3] != 0)
+
+
+def emit(g, T, ops):
+    Q = {"v": g.vector, "s": g.scalar, "t": g.tensor, "g": g, "y": g.sync}
+    n = len(ops)
+    known = {q: set() for q in Q}
+    closure, waits, first, before, prev = [], [], {}, {}, {}
+    for i in range(n):
+        q, rd, wr = ops[i]["q"], ops[i]["r"], ops[i]["w"]
+        need = set()
+        k = known[q]
+        for j in range(i):
+            o = ops[j]
+            if o["kind"] == "remote" or j in k:
+                continue
+            hit = any(meet(a, b) for a in rd + wr for b in o["w"]) or any(meet(a, b) for a in wr for b in o["r"])
+            if not hit and o["q"] != q:
+                hit = any(a[0] == "ps" and meet(a, b) for a in rd for b in o["r"])
+            if hit:
+                need.add(j)
+        keep = [j for j in need if not any(j in closure[x] for x in need if x != j)]
+        for j in keep:
+            k |= closure[j]
+            k.add(j)
+            first.setdefault(j, i)
+        waits.append(sorted(keep))
+        closure.append(set(k))
+        before[i] = prev.get(q)
+        prev[q] = i
+    group = {}
+    for i in sorted(first):
+        j = before[i]
+        if ops[i]["kind"] == "op" and j in group and ops[j]["kind"] == "op" and first[j] == first[i]:
+            group[i] = group[j]
+            group[i].append(i)
+        else:
+            group[i] = [i]
+    known = {q: set() for q in Q}
+    closure = []
+    last = {q: [None] * POOL[q] for q in POOL}
+    count = {q: [0] * POOL[q] for q in POOL}
+    tag, ndma, stores = {}, [0], []
+
+    def learn(k, j):
+        for x in group[j]:
+            k |= closure[x]
+            k.add(x)
+
+    for i in range(n):
+        o = ops[i]
+        q = o["q"]
+        k = known[q]
+        ws = []
+        for j in waits[i]:
+            if j not in k:
+                ws.append(j)
+                learn(k, j)
+        if o["kind"] == "dma":
+            tag[i] = ("d%d" % ndma[0], 16)
+            ndma[0] += 1
+            if i not in first:
+                stores.append((q, tag[i]))
+        elif i in first and group[i][0] == i:
+            free = [s for s in range(POOL[q]) if last[q][s] is None or last[q][s] in k]
+            if free:
+                s = min(free, key=lambda z: -1 if last[q][z] is None else last[q][z])
+            else:
+                s = min(range(POOL[q]), key=lambda z: last[q][z])
+                ws.append(last[q][s])
+                learn(k, last[q][s])
+            last[q][s] = group[i][-1]
+            count[q][s] += len(group[i])
+            for x in group[i]:
+                tag[x] = ("%s%d" % (q, s), count[q][s])
+        for name, val in o["pre"]:
+            Q[q].wait_ge(T.sem[name], val)
+        for j in ws:
+            Q[q].wait_ge(T.sem[tag[j][0]], tag[j][1])
+        closure.append(set(k))
+        ins = o["fn"](Q[q])
+        if i in tag:
+            ins.then_inc(T.sem[tag[i][0]], 16 if o["kind"] == "dma" else 1)
+    for q, (name, val) in stores:
+        Q[q].wait_ge(T.sem[name], val)
+
+
+def rank_program(g, core, T, topo):
+    rank = T.rank_of(core)
+    if rank is None:
+        return
+    nr = len(T.cores)
+    nxt, prv = T.cores[(rank + 1) % nr], T.cores[(rank - 1) % nr]
+    ops = []
+    sent = [0]
+
+    def a(name, lo=0, hi=None, st=1):
+        if hi is None:
+            hi = SCRATCH[name][1][1]
+        ap = T[name][:, lo:hi] if st == 1 else T[name][:, lo:hi:st]
+        if name == "ps":
+            return (ap, [("ps", lo // 512 * 512, lo // 512 * 512 + 512, 1)])
+        return (ap, [(name, lo, hi, st)])
+
+    def bank(b, n=C):
+        return a("ps", 512 * b, 512 * b + n)
+
+    def ind(win, off):
+        return (win[0].indirect(off[0]), win[1] + off[1])
+
+    def rec(q, fn, rd, wr, kind="op", pre=()):
+        r = []
+        for x in rd:
+            if isinstance(x, tuple):
+                r += x[1]
+        w = []
+        for x in wr:
+            w += x[1]
+        ops.append({"q": q, "fn": fn, "r": r, "w": w, "kind": kind, "pre": list(pre)})
+
+    def val(x):
+        return x[0] if isinstance(x, tuple) else x
+
+    def tt(o, x, y, op):
+        rec("v", lambda e: e.tensor_tensor(o[0], x[0], y[0], op), [x, y], [o])
+
+    def ts(o, x, s1, op0, s2=None, op1=None):
+        if op1 is None:
+            rec("v", lambda e: e.tensor_scalar(o[0], x[0], val(s1), None, op0), [x, s1], [o])
+        else:
+            rec("v", lambda e: e.tensor_scalar(o[0], x[0], val(s1), val(s2), op0, op1), [x, s1, s2], [o])
+
+    def cp(o, x):
+        rec("v", lambda e: e.tensor_copy(o[0], x[0]), [x], [o])
+
+    def ms(o, c):
+        rec("v", lambda e: e.memset(o[0], c), [], [o])
+
+    def scan(o, x):
+        n = len(range(x[1][0][1], x[1][0][2], x[1][0][3]))
+        m = a("cm", 0, n)
+        rec("v", lambda e: e.tensor_tensor_scan(o[0], m[0], x[0], 0.0, A.mult, A.add), [m, x], [o])
+
+    def sc(o, x, pre=()):
+        rec("s", lambda e: e.activation(o[0], x[0], F.Copy), [x], [o], pre=pre)
+
+    def act(o, x, func, bias, scale):
+        rec("s", lambda e: e.activation(o[0], x[0], func, bias=bias, scale=scale), [x], [o])
+
+    def quant(q, s, x):
+        rec("v", lambda e: e.quantize_mx(q[0], s[0], x[0]), [x], [q, s])
+
+    def mm(o, wq, wsc, xq, xs, pre=()):
+        rec("t", lambda e: e.matmul_mx(o[0], wq[0], wsc[0], xq[0], xs[0], True, True), [wq, wsc, xq, xs], [o], pre=pre)
+
+    def dma(q, o, x, rd=(), wr=()):
+        rec(q, lambda e: e.dma_start(o, x), list(rd), list(wr), kind="dma")
+
+    def iota(o, pattern, base, cmul, small=False):
+        if small:
+            rec("g", lambda e: e.iota(o[0], pattern, base, cmul, allow_small_or_imprecise_dtypes=True), [], [o])
+        else:
+            rec("g", lambda e: e.iota(o[0], pattern, base, cmul), [], [o])
+
+    def part(src, dst, which):
+        en = topo.engines(src, dst)
+        return en if which == "all" else en[:len(en) // 2] if which == "low" else en[len(en) // 2:]
+
+    def send(pieces, rd):
+        tr = []
+        for dst, which, sem, s_, d_ in pieces:
+            rid, pid = topo.addr(dst)[:2]
+            en = part(core, dst, which)
+            sent[0] += len(en)
+            tr.append(RemoteDMATransfer(dst_ids=[DstId(rid=rid, pnc=pid)], dma_engine_mask=sum(1 << e for e in en),
+                                        remote_sem=T.sem[sem], src=s_, dst=d_))
+        rec("g", lambda e: e.remote_dma_fused(tr, local_sem=T.sem.sent), rd, [], kind="remote")
+
+    from_prv = len(part(prv, core, "all")) + len(part(prv, core, "low"))
+    from_nxt = len(part(nxt, core, "all")) + len(part(nxt, core, "high"))
+    lists_in = len(part(prv, core, "low")) + len(part(nxt, core, "high"))
+
+    def column(o, x, shift=0.0):
+        ts(o, x, shift - 1.5, A.add, 0.25, A.mult)
+
+    s_num, s_hi, s_thr, s_pm, s_tri = a("col", 0, 1), a("col", 1, 2), a("col", 2, 3), a("col", 3, 4), a("col", 5, 6)
+
+    def priorities():
+        tt(a("t1", 0, 54), a("hb"), a("tb", 0, 54), A.min)
+        ts(a("lo", 0, 54), a("tb", 0, 54), float(4 * C), A.is_ge, 4096.0, A.mult)
+        tt(a("t3", 0, 54), a("t1", 0, 54), a("lo", 0, 54), A.add)
+        ts(a("pr"), a("t3", 0, 54), -4096.0, A.mult, (4 * C + 1) * 4096.0, A.add)
+
+    def pick_codes(lo, hi):
+        o = a("uoff", lo // 16, hi // 16)
+        rec("v", lambda e: e.tensor_copy(T.uq2[:, lo:hi].bitcast(dt.uint32), T.uq[:, 0:128].bitcast(dt.uint32).indirect(o[0])),
+            [a("uq"), o], [a("uq2", lo, hi)])
+
+    def pick_scales(lo, hi):
+        sc(a("us2", lo, hi), ind(a("us"), a("uoff", lo // 16, hi // 16)))
+
+    def signs(t):
+        src, h = "xt" if t else "xin", C // 2
+        for i in range(2):
+            q_, s_ = a("qx%d" % t, h * i, h * i + h), a("sx%d" % t, h * i, h * i + h)
+            quant(q_, s_, a(src, 4 * h * i, 4 * h * i + 4 * h))
+            mm(bank(4 + i, h), a("uq2", 128 * t, 128 * t + 128), a("us2", 128 * t, 128 * t + 128), q_, s_)
+        act(a("bits", 864, 864 + h), bank(4, h), F.Sign, 0.0, 1.0)
+
+    def signs_rest():
+        ts(a("bits", 864 + C // 2, 1152), bank(5, C // 2), 0.0, A.is_gt)
+
+    dma("y", T.xin[:], T.x[:], wr=[a("xin")])
+    dma("s", T.twb[:, 0:60], T.tw[:], wr=[a("twb")])
+    dma("s", T.ub[:], T.u[:], wr=[a("ub")])
+    dma("y", T.wq[:].bitcast(dt.uint8), T.wc[:], wr=[a("wq")])
+    dma("y", T.wsc[:], T.ws[:], wr=[a("wsc")])
+    dma("y", T.vb[:], T.v[:], wr=[a("vb")])
+    ms(a("ones"), 1.0)
+    iota(a("r16"), [[1, 16]], 128, -1)
+    iota(a("base4"), [[4, 384]], 0, 0, True)
+    rec("g", lambda e: e.affine_select(T.ident[:], T.ones[:], [[-1, 128]], A.is_equal, 0.0, 0, 1), [a("ones")], [a("ident")])
+    iota(a("uoi"), [[1, 3], [16, 8]], 0, 0)
+    iota(a("c16"), [[16, 18]], 0, 0)
+    for name, c in (("nf", NOWHERE), ("inf", NOWHERE), ("pf", 0.0)):
+        act(a(name, C, 384), a("ones", 0, 96), F.Identity, 0.0, c)
+    act(a("bits", 1152, 1248), a("ones", 0, 96), F.Identity, 0.0, 0.0)
+    iota(a("itab", 0, 768), [[1, 768]], 0, 0, True)
+    ms(a("eb"), 0.0)
+    ts(a("r16b"), a("r16"), 15, A.bitwise_and)
+    ts(a("coli", 0, 1), a("r16", 0, 1), -1.0, A.mult, 128.0, A.add)
+    for k in range(3):
+        act(a("inttab", k, 3 * C, 3), a("base4", 0, C), F.Identity, float(k), 1.0)
+    sc(a("inttab", 3 * C, 960), a("base4", C, 384))
+    ms(a("ntab", 1536, 1540), NOWHERE)
+    ts(a("c0"), a("r16b"), 0.0, A.not_equal)
+    ts(a("c1"), a("r16b"), 1.0, A.is_equal, BIG, A.mult)
+    ts(a("col", 4, 5), a("r16b", 0, 1), 1.0, A.is_equal)
+    ts(a("coli", 1, 2), a("coli", 0, 1), 15, A.bitwise_and)
+    tt(a("cm", 0, 16), a("c0"), a("c1"), A.max)
+    ts(s_num, a("col", 4, 5), 1.0, A.mult, 1.0 / BIG, A.add)
+    ts(s_thr, a("col", 4, 5), -BIG / 2, A.mult, BIG / 2, A.add)
+    cp(a("cm", 16, 32), a("cm", 0, 16))
+    cp(s_pm, a("coli", 1, 2))
+    ts(s_hi, s_num, 1.0 / 4096, A.mult)
+    cp(a("cm", 32, 64), a("cm", 0, 32))
+    ts(s_tri, s_num, 1.0 / 16384, A.mult)
+    cp(a("cm", 64, 128), a("cm", 0, 64))
+    cp(a("eb", 3, 515, 4), a("ident"))
+    cp(a("cm", 128, 256), a("cm", 0, 128))
+    cp(a("cm", 256, 288), a("cm", 0, 32))
+    for b in range(4):
+        quant(a("eq", 128 * b, 128 * b + 128), a("es", 128 * b, 128 * b + 128), a("eb", 3 - b, 515 - b))
+    cp(a("tw16", 0, 60), a("twb", 0, 60))
+    cp(a("uoff"), a("uoi"))
+    ts(a("vw"), a("c16"), s_pm, A.add)
+    sc(a("tfn", 128, 960), ind(a("inttab"), a("tw16", 8, 60)))
+    cp(a("cm", 288, 576), a("cm", 0, 288))
+    cp(a("tfn", 0, 128), ind(a("inttab"), a("tw16", 0, 8)))
+    cp(a("cm", 576, 1152), a("cm", 0, 576))
+    quant(a("uq"), a("us"), a("ub"))
+    pick_codes(0, 128)
+    pick_scales(0, 128)
+    signs(0)
+    for k in range(3):
+        scan(a("so", C * k, C * k + C), a("tfn", k, 3 * C, 3))
+    scan(a("so", 3 * C, 960), a("tfn", 3 * C, 960))
+    signs_rest()
+    ts(a("lb"), a("so", 15, 960, 16), s_num, A.mult)
+    ts(a("tb", 0, 54), a("so", 15, 864, 16), s_num, A.mult)
+    column(a("e54"), a("lb", 0, 54))
+    for k in range(3):
+        act(a("hb", 18 * k, 18 * k + 18), a("vw"), F.Identity, float(k), 4.0)
+
+    for t in range(R):
+        more = t < R - 1
+        qx, sx = a("qx%d" % t), a("sx%d" % t)
+        lq, ls, lst, fp, fn = "lq%d" % t, "ls%d" % t, "lst%d" % t, "fp%d" % t, "fn%d" % t
+        u8 = qx[0].bitcast(dt.uint8)
+        send([(nxt, "all", fp, u8, T[lq][:, C:2 * C].bitcast(dt.uint8))], [qx])
+        send([(nxt, "low", fp, sx[0], T[ls][:, C:2 * C]), (prv, "high", fn, sx[0], T[ls][:, 0:C])], [sx])
+        send([(prv, "all", fn, u8, T[lq][:, 0:C].bitcast(dt.uint8))], [qx])
+        if t == 0:
+            iota(a("itab", 768, 1540), [[1, 772]], 768, 0, True)
+
+        def unpack(b, bk, q_, s_, pre=()):
+            mm(bank(bk), a("eq", 128 * b, 128 * b + 128), a("es", 128 * b, 128 * b + 128), q_, s_, pre)
+
+        def far(h, planes):
+            for b in planes:
+                unpack(b, 4 + b, a(lq, C * h, C * h + C), a(ls, C * h, C * h + C),
+                       [(fp, from_prv) if h else (fn, from_nxt)] if b == 0 else ())
+                sc(a("dn", 576 * b + C * h, 576 * b + C * h + C), bank(4 + b))
+
+        pos = a("bits", 864, 1248)
+        sc(a("bits", 448, 864), ind(pos, a("e54", 28, 54)))
+        cp(a("bits", 0, 448), ind(pos, a("e54", 0, 28)))
+        if t == 0:
+            for k in range(4):
+                act(a("ntab", k, 1536, 4), a("base4"), F.Identity, 4096.0 * ((k + 1) % 3), 4096.0)
+        for b in range(4):
+            unpack(b, b, qx, sx)
+            sc(a("dw", 384 * b, 384 * b + C), bank(b))
+        scan(a("sb"), a("bits", 0, 1152))
+        if t == 0:
+            priorities()
+            cp(a("tb", 54, 90), a("lb", 0, 36))
+        ts(a("pw"), a("sb", 15, 1152, 16), s_thr, A.is_gt)
+        for k in range(3):
+            tt(a("w", 18 * k, 18 * k + 18), a("pw", 18 * k, 18 * k + 18), a("pw", 54, 72), A.not_equal)
+        if t:
+            tt(a("aq", 18, 24), a("lb", 54, 60), a("t2", 54, 60), A.add)
+        else:
+            cp(a("aq", 18, 24), a("lb", 54, 60))
+        tt(a("wp"), a("w"), a("pr"), A.mult)
+        column(a("esl"), a("lb", 54, 60))
+        ts(a("wp", 0, 18), a("wp", 0, 18), 2048.0, A.max)
+        if t:
+            tt(a("lb", 54, 60), a("lb", 54, 60), a("t2", 54, 60), A.add)
+        else:
+            cp(a("kb", 36, 42), a("lb", 54, 60))
+        for s_ in range(3):
+            tt(a("key", s_, 216, 4), a("wp"), a("tb", 18 * s_, 18 * s_ + 54), A.add)
+        tt(a("key", 3, 216, 4), a("wp"), a("hb"), A.add)
+        tt(a("k1"), a("key", 0, 72), a("key", 72, 144), A.max)
+        tt(a("best"), a("k1"), a("key", 144, 216), A.max)
+        ts(a("idx"), a("best", 0, 72, 4), 4095, A.bitwise_and)
+        ts(a("lb", 18, 36), a("best", 1, 72, 4), 2047, A.bitwise_and)
+        ts(a("lb", 0, 18), a("best", 0, 72, 4), 2047, A.bitwise_and)
+        ts(a("offn"), a("idx"), float(NONE), A.min)
+        cp(a("offp"), a("lb", 18, 36))
+        column(a("e2", 0, 18), a("lb", 0, 18))
+        sc(a("nf", 0, C), ind(a("ntab"), a("offn")))
+        cp(a("af"), ind(a("itab"), a("offn")))
+        sc(a("pf", 0, C), ind(a("itab"), a("offp")))
+        ts(a("lb", 36, 54), a("best", 2, 72, 4), 2047, A.bitwise_and)
+        tt(a("inf", 0, C), ind(a("nf"), a("e2", 0, 18)), a("af"), A.add)
+        if t == 0:
+            sc(a("kb", 0, 18), a("vw"))
+            sc(a("kb", 18, 36), a("vw"))
+        tt(a("db", 18, 36), a("lb", 36, 54), a("lb", 18, 36), A.subtract)
+        sc(a("zf", C, 384), ind(a("inf"), a("esl")))
+        tt(a("zf", 0, C), ind(a("pf"), a("e2", 0, 18)), a("inf", 0, C), A.add)
+        sc(a("gf", 0, C), ind(a("inf"), a("e2", 0, 18)))
+        if t == 0:
+            act(a("two", 0, 2 * C, 2), a("base4", 0, C), F.Identity, -1e29, 0.0)
+            act(a("two", 1, 2 * C, 2), a("base4", 0, C), F.Identity, 0.0, 0.0)
+            for k, c in enumerate((0.0, 4.0, 2.0)):
+                act(a("hc", 18 * k, 18 * k + 18), a("vw"), F.Identity, c, 0.0)
+        far(1, range(EARLY))
+        tt(a("aq", 0, 18), a("lb", 36, 54), a("lb", 0, 18), A.add)
+        scan(a("so", 0, 384), a("zf"))
+        ts(a("xz"), a("best", 3, 72, 4), 3, A.bitwise_and)
+        ts(a("ib", 36, 60), a("so", 15, 384, 16), s_num, A.mult)
+        ts(a("xb", 54, 60), a("so", C + 15, 384, 16), s_hi, A.mult, -0.49, A.add)
+        ts(a("xb", 18, 36), a("so", 15, C, 16), s_tri, A.mult, -0.49, A.add)
+        ts(a("xb", 36, 54), a("so", 15, C, 16), s_tri, A.mult, -0.49, A.add)
+        ts(a("lo", 36, 60), a("ib", 36, 60), 4095, A.bitwise_and)
+        tt(a("mb", 18, 60), a("xb", 18, 60), a("kb"), A.is_equal)
+        tt(a("db", 36, 60), a("lo", 36, 60), a("aq"), A.subtract)
+        if more:
+            ts(a("hs", 0, 18), a("best", 3, 72, 4), 2047, A.bitwise_and)
+        tt(a("t1", 18, 60), a("mb", 18, 60), a("db", 18, 60), A.mult)
+        if more:
+            ts(a("th", 0, 18), a("xz"), -3.0, A.mult, -3.0, A.min)
+        tt(a("lb", 18, 60), a("lb", 18, 60), a("t1", 18, 60), A.add)
+        if more:
+            ts(a("th", 18, 36), a("xz"), -3.0, A.mult, -3.0, A.max)
+        ea, eb_ = a("esend", 8 * t, 8 * t + 3), a("esend", 8 * t + 4, 8 * t + 7)
+        column(ea, a("lb", 54, 57), 4.0 * C)
+        column(eb_, a("lb", 57, 60))
+        send([(nxt, "low", lst, ea[0], T[lst][:, 3:6]), (prv, "high", lst, eb_[0], T[lst][:, 0:3])], [ea, eb_])
+        if t == 0:
+            iota(a("otab", 0, 4 * C), [[3, C], [1, 4]], 0, 0, True)
+            iota(a("otab", 4 * C, 1536), [[1, 2 * S], [0, 4]], 3 * C, 0, True)
+        column(a("e2", 18, 54), a("lb", 18, 54))
+        ts(a("t2", 0, 54), a("lb", 0, 54), 4097.0, A.mult)
+        sc(a("gf", 2 * C, 3 * C), ind(a("inf"), a("e2", 36, 54)))
+        cp(a("gf", C, 2 * C), ind(a("inf"), a("e2", 18, 36)))
+        far(1, range(EARLY, 4))
+        far(0, range(4))
+        scan(a("so", 0, 864), a("gf"))
+        if more:
+            tt(a("hs", 18, 36), a("hs", 0, 18), a("th", 0, 18), A.add)
+        ts(a("ib", 0, 54), a("so", 15, 864, 16), s_num, A.mult)
+        ts(a("xb", 0, 54), a("so", 15, 864, 16), s_hi, A.mult, -0.49, A.add)
+        tt(a("db", 0, 54), a("ib", 0, 54), a("t2", 0, 54), A.subtract)
+        tt(a("mb", 0, 54), a("xb", 0, 54), a("lb", 0, 54), A.is_equal)
+        if more:
+            tt(a("hs", 36, 54), a("hs", 0, 18), a("th", 18, 36), A.add)
+        tt(a("t1", 0, 54), a("mb", 0, 54), a("db", 0, 54), A.mult)
+        if more:
+            tt(a("hb"), a("hs"), a("hc"), A.add)
+        tt(a("lb", 0, 54), a("lb", 0, 54), a("t1", 0, 54), A.add)
+        column(a("e54"), a("lb", 0, 54))
+
+        def plane(b):
+            return a("dw", 384 * b, 384 * b + 384)
+
+        def border(b):
+            sc(a("dw", 384 * b + C, 384 * b + 384), ind(a("dn", 576 * b, 576 * b + 576), a(lst, 0, 6)),
+               [(lst, lists_in)] if b == 0 else ())
+
+        def both(b):
+            for k in range(2):
+                sc(a("gi", 2 * C * (b - 2) + k, 2 * C * (b - 1), 2), ind(plane(b), a("e54", 18 * k, 18 * k + 18)))
+
+        border(0)
+        border(1)
+        border(2)
+        sc(a("g0", C, 2 * C), ind(plane(1), a("e54", 0, 18)))
+        border(3)
+        both(2)
+        both(3)
+        if t == 0:
+            pick_scales(128, 384)
+        ts(a("t1"), a("lb"), 3, A.bitwise_and)
+        ts(a("t2"), a("t1"), 0.0, A.is_equal, 3.0, A.mult)
+        ts(a("t3"), a("t2"), -1.0, A.add)
+        tt(a("t1"), a("lb"), a("t3"), A.add)
+        tt(a("t2"), a("t1"), a("xb"), A.is_equal)
+        tt(a("t1"), a("t2"), a("mb"), A.max)
+        tt(a("t2"), a("t1"), a("t3"), A.mult)
+        if not more:
+            tt(a("tb", 0, 54), a("lb", 0, 54), a("t2", 0, 54), A.add)
+            tt(a("tb", 54, 90), a("lb", 0, 36), a("t2", 0, 36), A.add)
+
+        def p1(b):
+            tt(a("g1", C * b, C * b + C), ind(plane(b), a("e54", 18, 36)), a("g0", C * b, C * b + C), A.max)
+
+        def p2(b):
+            tt(a("mt", b, 4 * C, 4), ind(plane(b), a("e54", 36, 54)), a("g1", C * b, C * b + C), A.max)
+
+        def p3(b):
+            lo, hi = 2 * C * (b - 2), 2 * C * (b - 1)
+            o, x, m = a("go", lo, hi), a("gi", lo, hi), a("two")
+            rec("v", lambda e: e.tensor_tensor_scan(o[0], m[0], x[0], 0.0, A.add, A.max), [m, x], [o])
+
+        def p4(b):
+            tt(a("mt", b, 4 * C, 4), ind(plane(b), a("e54", 36, 54)), a("go", 2 * C * (b - 2) + 1, 2 * C * (b - 1), 2), A.max)
+
+        cp(a("g0", 0, C), ind(plane(0), a("e54", 0, 18)))
+        p1(0)
+        p1(1)
+        p2(0)
+        p2(1)
+        p3(2)
+        p4(2)
+        p3(3)
+        p4(3)
+        quant(a("mq"), a("ms"), a("mt"))
+        for b in range(4):
+            mm(bank(4 + b), a("wq", 128 * b, 128 * b + 128), a("wsc", 128 * b, 128 * b + 128), a("mq"), a("ms"))
+            act(a("rl", C * b, C * b + C), bank(4 + b), F.Relu, 0.0, 0.015625)
+        if more:
+            tt(a("tb", 0, 54), a("lb", 0, 54), a("t2", 0, 54), A.add)
+            if t == 0:
+                pick_codes(128, 384)
+            else:
+                quant(a("vq"), a("vs"), a("vb"))
+            priorities()
+        else:
+            for j in range(3):
+                ts(a("wp", 18 * j, 18 * j + 18), a("xz"), float((3 - j) % 3), A.is_equal, 4096.0, A.mult)
+            tt(a("lb", 54, 60), a("lb", 54, 60), a("t2", 54, 60), A.add)
+            for s_ in range(3):
+                tt(a("key", s_, 162, 3), a("wp"), a("tb", 18 * s_, 18 * s_ + 54), A.add)
+            cp(a("oto", 54, 60), a("lb", 54, 60))
+            tt(a("k1", 0, 54), a("key", 0, 54), a("key", 54, 108), A.max)
+            tt(a("best", 0, 54), a("k1", 0, 54), a("key", 108, 162), A.max)
+            for s_ in range(3):
+                ts(a("oto", 18 * s_, 18 * s_ + 18), a("best", s_, 54, 3), -4096.0, A.add)
+        for b in range(4):
+            tt(a("xt", b, 4 * C, 4), bank(b), a("rl", C * b, C * b + C), A.add)
+        if more:
+            signs(t + 1)
+            tt(a("tb", 54, 90), a("lb", 0, 36), a("t2", 0, 36), A.add)
+            tt(a("kb", 36, 42), a("lb", 54, 60), a("t2", 54, 60), A.add)
+            signs_rest()
+        else:
+            quant(a("qx%d" % R), a("sx%d" % R), a("xt"))
+
+    qx, sx = a("qx%d" % R), a("sx%d" % R)
+    for k in range(3):
+        sc(a("otf", k, 3 * C, 3), ind(a("otab"), a("oto", 18 * k, 18 * k + 18)))
+    mm(bank(4), a("vq"), a("vs"), qx, sx)
+    dma("y", T.oc[:], qx[0].bitcast(dt.uint8), rd=[qx])
+    for k in range(4):
+        dma("y", T.osc[4 * k:4 * k + 4, :], T["sx%d" % R][32 * k:32 * k + 4, :], rd=[sx])
+    cp(a("otf", 3 * C, 960), ind(a("otab"), a("oto", 54, 60)))
+    cp(a("yb"), bank(4))
+    dma("y", T.y[:], T.yb[:], rd=[a("yb")])
+    dma("s", T.ot[:], T.otf[0:128:16, :], rd=[a("otf")])
+    emit(g, T, ops)
+    g.wait_ge(T.sem.sent, sent[0])

@@ -6,7 +6,7 @@ FP8 = "float8_e4m3fn_x4"
 BIG = float(2 ** 32)
 NONE = 1536
 NOWHERE = 2047 * 4096.0
-EARLY = 1
+WAKE, TOL, LAG_A, LAG_B, LAG_L = 200, 60, 6000, 8000, 3000
 
 SCRATCH = {"ps": ("psum", [128, 4096], "float32")}
 for _d, _bufs in (
@@ -16,10 +16,10 @@ for _d, _bufs in (
     ("float32", {"c0": 16, "c1": 16, "col": 8, "vw": 18, "base4": 384, "inttab": 960, "itab": 1540, "ntab": 1540,
                  "otab": 1536, "tfn": 960, "otf": 960, "so": 960, "pw": 72, "w": 54, "wp": 54, "pr": 54, "hb": 54,
                  "hc": 54, "kb": 42, "af": C, "nf": 384, "pf": 384, "inf": 384, "zf": 384, "gf": 864, "rl": 4 * C,
-                 "yb": C}),
-    ("int32", {"twb": 64, "r16": 16, "r16b": 16, "coli": 8, "c16": 18, "uoi": 24, "key": 216, "k1": 72, "best": 72,
-               "tb": 90, "hs": 54, "th": 36, "lb": 60, "xb": 60, "mb": 60, "db": 60, "ib": 60, "lo": 60, "t1": 60,
-               "t2": 60, "t3": 60, "idx": 18, "aq": 24, "xz": 18}),
+                 "yb": C, "kk": 216, "dfl": 72, "f0": 120, "f1": 120, "fo": 120, "uu": 24, "u2": 54}),
+    ("int32", {"twb": 64, "r16": 16, "r16b": 16, "coli": 8, "c16": 18, "uoi": 24, "key": 216, "k1": 72, "k2": 72,
+               "best": 72, "tb": 90, "hs": 54, "th": 36, "lb": 60, "xb": 60, "ib": 60, "p1": 54, "p2": 54, "p3": 54,
+               "t1": 60, "t2": 60, "t3": 60, "t4": 60, "t5": 60, "t6": 60, "t7": 60, "idx": 18, "aq": 36, "xz": 18}),
     ("uint16", {"tw16": 64, "uoff": 24, "offn": 18, "offp": 18, "e2": 54, "e54": 54, "esl": 6, "oto": 60, "esend": 24}),
     (FP8, {"wq": 512, "uq": 128, "uq2": 384, "vq": 128, "eq": 512, "mq": C}),
     ("uint8", {"wsc": 512, "us": 128, "us2": 384, "vs": 128, "es": 512, "ms": C}),
@@ -49,30 +49,66 @@ def meet(a, b):
     return not (a[3] > 1 and a[3] == b[3] and (a[1] - b[1]) % a[3] != 0)
 
 
+def clash(x, o):
+    if o["kind"] == "remote":
+        return False
+    if any(meet(a, b) for a in x["r"] + x["w"] for b in o["w"]) or any(meet(a, b) for a in x["w"] for b in o["r"]):
+        return True
+    return o["q"] != x["q"] and any(a[0] == "ps" and meet(a, b) for a in x["r"] for b in o["r"])
+
+
+def order(ops):
+    n = len(ops)
+    dep = []
+    last = {}
+    for i, x in enumerate(ops):
+        d = [(j, ops[j]["cost"] + ops[j]["lat"] + WAKE) for j in range(i) if clash(x, ops[j])]
+        d += x["after"]
+        if x["q"] in "tgy":
+            if x["q"] in last:
+                d.append((last[x["q"]], 0))
+            last[x["q"]] = i
+        dep.append(d)
+    rest = [o["cost"] + o["lat"] for o in ops]
+    for i in range(n - 1, -1, -1):
+        for j, w in dep[i]:
+            rest[j] = max(rest[j], w + rest[i])
+    start, free, out = {}, {q: 0 for q in "vstgy"}, []
+    todo = list(range(n))
+    while todo:
+        ready = {}
+        for i in todo:
+            if all(j in start for j, w in dep[i]):
+                q = ops[i]["q"]
+                ready.setdefault(q, []).append((max([free[q]] + [start[j] + w for j, w in dep[i]]), i))
+        picks = []
+        for q in ready:
+            top = max(ready[q], key=lambda z: (rest[z[1]], -z[1]))
+            fit = [z for z in ready[q] if z[0] + ops[z[1]]["cost"] <= top[0] + TOL and z[0] < top[0]]
+            picks.append(min(fit, key=lambda z: (z[0], -rest[z[1]])) if fit else top)
+        at, i = min(picks)
+        start[i] = at
+        free[ops[i]["q"]] = at + ops[i]["cost"]
+        todo.remove(i)
+        out.append(ops[i])
+    return out
+
+
 def emit(g, T, ops):
     Q = {"v": g.vector, "s": g.scalar, "t": g.tensor, "g": g, "y": g.sync}
     n = len(ops)
     known = {q: set() for q in Q}
     closure, waits, first, before, prev = [], [], {}, {}, {}
     for i in range(n):
-        q, rd, wr = ops[i]["q"], ops[i]["r"], ops[i]["w"]
-        need = set()
+        q = ops[i]["q"]
         k = known[q]
-        for j in range(i):
-            o = ops[j]
-            if o["kind"] == "remote" or j in k:
-                continue
-            hit = any(meet(a, b) for a in rd + wr for b in o["w"]) or any(meet(a, b) for a in wr for b in o["r"])
-            if not hit and o["q"] != q:
-                hit = any(a[0] == "ps" and meet(a, b) for a in rd for b in o["r"])
-            if hit:
-                need.add(j)
+        need = [j for j in range(i) if j not in k and clash(ops[i], ops[j])]
         keep = [j for j in need if not any(j in closure[x] for x in need if x != j)]
         for j in keep:
             k |= closure[j]
             k.add(j)
             first.setdefault(j, i)
-        waits.append(sorted(keep))
+        waits.append(keep)
         closure.append(set(k))
         before[i] = prev.get(q)
         prev[q] = i
@@ -147,68 +183,81 @@ def rank_program(g, core, T, topo):
             hi = SCRATCH[name][1][1]
         ap = T[name][:, lo:hi] if st == 1 else T[name][:, lo:hi:st]
         if name == "ps":
-            return (ap, [("ps", lo // 512 * 512, lo // 512 * 512 + 512, 1)])
-        return (ap, [(name, lo, hi, st)])
+            return (ap, [("ps", lo // 512 * 512, lo // 512 * 512 + 512, 1)], hi - lo)
+        return (ap, [(name, lo, hi, st)], len(range(lo, hi, st)))
+
+    def odd(name, lo, hi):
+        return a(name, 2 * lo + 1, 2 * hi, 2)
+
+    def even(name, lo, hi):
+        return a(name, 2 * lo, 2 * hi, 2)
 
     def bank(b, n=C):
         return a("ps", 512 * b, 512 * b + n)
 
     def ind(win, off):
-        return (win[0].indirect(off[0]), win[1] + off[1])
+        return (win[0].indirect(off[0]), win[1] + off[1], -1)
 
-    def rec(q, fn, rd, wr, kind="op", pre=()):
+    def rec(q, fn, rd, wr, cost, kind="op", pre=(), after=(), lat=0):
         r = []
         for x in rd:
             if isinstance(x, tuple):
                 r += x[1]
+                if x[2] < 0:
+                    cost = 60 + 1.2 * wr[0][2]
         w = []
         for x in wr:
             w += x[1]
-        ops.append({"q": q, "fn": fn, "r": r, "w": w, "kind": kind, "pre": list(pre)})
+        ops.append({"q": q, "fn": fn, "r": r, "w": w, "kind": kind, "pre": list(pre), "after": list(after),
+                    "cost": max(cost, 55), "lat": lat})
+        return len(ops) - 1
 
     def val(x):
         return x[0] if isinstance(x, tuple) else x
 
+    def per(*xs):
+        return 0.42 if all(SCRATCH[x[1][0][0]][2] == "bfloat16" for x in xs) else 0.83
+
     def tt(o, x, y, op):
-        rec("v", lambda e: e.tensor_tensor(o[0], x[0], y[0], op), [x, y], [o])
+        rec("v", lambda e: e.tensor_tensor(o[0], x[0], y[0], op), [x, y], [o], o[2] * (0.83 if x[1][0][0] == "ps" else 1.66))
 
     def ts(o, x, s1, op0, s2=None, op1=None):
         if op1 is None:
-            rec("v", lambda e: e.tensor_scalar(o[0], x[0], val(s1), None, op0), [x, s1], [o])
+            rec("v", lambda e: e.tensor_scalar(o[0], x[0], val(s1), None, op0), [x, s1], [o], o[2] * 0.83)
         else:
-            rec("v", lambda e: e.tensor_scalar(o[0], x[0], val(s1), val(s2), op0, op1), [x, s1, s2], [o])
+            rec("v", lambda e: e.tensor_scalar(o[0], x[0], val(s1), val(s2), op0, op1), [x, s1, s2], [o], o[2] * 0.83)
 
     def cp(o, x):
-        rec("v", lambda e: e.tensor_copy(o[0], x[0]), [x], [o])
+        rec("v", lambda e: e.tensor_copy(o[0], x[0]), [x], [o], o[2] * per(o, x))
 
     def ms(o, c):
-        rec("v", lambda e: e.memset(o[0], c), [], [o])
+        rec("v", lambda e: e.memset(o[0], c), [], [o], o[2] * per(o))
 
-    def scan(o, x):
-        n = len(range(x[1][0][1], x[1][0][2], x[1][0][3]))
-        m = a("cm", 0, n)
-        rec("v", lambda e: e.tensor_tensor_scan(o[0], m[0], x[0], 0.0, A.mult, A.add), [m, x], [o])
+    def scan(o, x, m=None, op0=A.mult, op1=A.add):
+        m = m or a("cm", 0, o[2])
+        rec("v", lambda e: e.tensor_tensor_scan(o[0], m[0], x[0], 0.0, op0, op1), [m, x], [o], o[2] * per(o, x, m))
 
-    def sc(o, x, pre=()):
-        rec("s", lambda e: e.activation(o[0], x[0], F.Copy), [x], [o], pre=pre)
+    def sc(o, x, pre=(), after=()):
+        return rec("s", lambda e: e.activation(o[0], x[0], F.Copy), [x], [o], 60 + o[2] * 0.83, pre=pre, after=after)
 
     def act(o, x, func, bias, scale):
-        rec("s", lambda e: e.activation(o[0], x[0], func, bias=bias, scale=scale), [x], [o])
+        rec("s", lambda e: e.activation(o[0], x[0], func, bias=bias, scale=scale), [x], [o], 60 + o[2] * 0.83)
 
     def quant(q, s, x):
-        rec("v", lambda e: e.quantize_mx(q[0], s[0], x[0]), [x], [q, s])
+        rec("v", lambda e: e.quantize_mx(q[0], s[0], x[0]), [x], [q, s], 12 + 0.22 * x[2])
 
-    def mm(o, wq, wsc, xq, xs, pre=()):
-        rec("t", lambda e: e.matmul_mx(o[0], wq[0], wsc[0], xq[0], xs[0], True, True), [wq, wsc, xq, xs], [o], pre=pre)
+    def mm(o, wq, wsc, xq, xs, pre=(), after=()):
+        rec("t", lambda e: e.matmul_mx(o[0], wq[0], wsc[0], xq[0], xs[0], True, True), [wq, wsc, xq, xs], [o],
+            0.6 * o[2], pre=pre, after=after)
 
-    def dma(q, o, x, rd=(), wr=()):
-        rec(q, lambda e: e.dma_start(o, x), list(rd), list(wr), kind="dma")
+    def dma(q, o, x, rd=(), wr=(), lat=2500):
+        rec(q, lambda e: e.dma_start(o, x), list(rd), list(wr), 100, kind="dma", lat=lat)
 
     def iota(o, pattern, base, cmul, small=False):
         if small:
-            rec("g", lambda e: e.iota(o[0], pattern, base, cmul, allow_small_or_imprecise_dtypes=True), [], [o])
+            rec("g", lambda e: e.iota(o[0], pattern, base, cmul, allow_small_or_imprecise_dtypes=True), [], [o], 130 + 1.7 * o[2])
         else:
-            rec("g", lambda e: e.iota(o[0], pattern, base, cmul), [], [o])
+            rec("g", lambda e: e.iota(o[0], pattern, base, cmul), [], [o], 130 + 1.7 * o[2])
 
     def part(src, dst, which):
         en = topo.engines(src, dst)
@@ -222,7 +271,7 @@ def rank_program(g, core, T, topo):
             sent[0] += len(en)
             tr.append(RemoteDMATransfer(dst_ids=[DstId(rid=rid, pnc=pid)], dma_engine_mask=sum(1 << e for e in en),
                                         remote_sem=T.sem[sem], src=s_, dst=d_))
-        rec("g", lambda e: e.remote_dma_fused(tr, local_sem=T.sem.sent), rd, [], kind="remote")
+        return rec("g", lambda e: e.remote_dma_fused(tr, local_sem=T.sem.sent), rd, [], 300, kind="remote")
 
     from_prv = len(part(prv, core, "all")) + len(part(prv, core, "low"))
     from_nxt = len(part(nxt, core, "all")) + len(part(nxt, core, "high"))
@@ -231,21 +280,27 @@ def rank_program(g, core, T, topo):
     def column(o, x, shift=0.0):
         ts(o, x, shift - 1.5, A.add, 0.25, A.mult)
 
-    s_num, s_hi, s_thr, s_pm, s_tri = a("col", 0, 1), a("col", 1, 2), a("col", 2, 3), a("col", 3, 4), a("col", 5, 6)
+    s_num, s_hi, s_thr, s_pm = a("col", 0, 1), a("col", 1, 2), a("col", 2, 3), a("col", 3, 4)
 
-    def priorities():
-        tt(a("t1", 0, 54), a("hb"), a("tb", 0, 54), A.min)
-        ts(a("lo", 0, 54), a("tb", 0, 54), float(4 * C), A.is_ge, 4096.0, A.mult)
-        tt(a("t3", 0, 54), a("t1", 0, 54), a("lo", 0, 54), A.add)
-        ts(a("pr"), a("t3", 0, 54), -4096.0, A.mult, (4 * C + 1) * 4096.0, A.add)
+    def keys():
+        tt(a("p1"), a("hb"), a("tb", 0, 54), A.min)
+        ts(a("p2"), a("tb", 0, 54), float(4 * C), A.is_ge, 4096.0, A.mult)
+        tt(a("p3"), a("p1"), a("p2"), A.add)
+        ts(a("pr"), a("p3"), -4096.0, A.mult, (4 * C + 1) * 4096.0, A.add)
+        for s_ in range(3):
+            tt(a("kk", 54 * s_, 54 * s_ + 54), a("pr"), a("tb", 18 * s_, 18 * s_ + 54), A.add)
+            ts(a("dfl", s_, 72, 4), a("tb", 18 * s_, 18 * s_ + 18), 2048.0, A.add)
+        tt(a("kk", 162, 216), a("pr"), a("hb"), A.add)
+        ts(a("dfl", 3, 72, 4), a("hb", 0, 18), 2048.0, A.add)
+        column(a("esl"), a("lb", 54, 60))
+        ts(a("uu", 18, 24), a("lb", 54, 60), 4097.0, A.mult)
+        cp(a("kb", 36, 42), a("lb", 54, 60))
 
-    def pick_codes(lo, hi):
+    def pick_u(lo, hi):
         o = a("uoff", lo // 16, hi // 16)
         rec("v", lambda e: e.tensor_copy(T.uq2[:, lo:hi].bitcast(dt.uint32), T.uq[:, 0:128].bitcast(dt.uint32).indirect(o[0])),
-            [a("uq"), o], [a("uq2", lo, hi)])
-
-    def pick_scales(lo, hi):
-        sc(a("us2", lo, hi), ind(a("us"), a("uoff", lo // 16, hi // 16)))
+            [a("uq"), o], [a("uq2", lo, hi)], 60 + 1.2 * (hi - lo))
+        sc(a("us2", lo, hi), ind(a("us"), o))
 
     def signs(t):
         src, h = "xt" if t else "xin", C // 2
@@ -254,11 +309,9 @@ def rank_program(g, core, T, topo):
             quant(q_, s_, a(src, 4 * h * i, 4 * h * i + 4 * h))
             mm(bank(4 + i, h), a("uq2", 128 * t, 128 * t + 128), a("us2", 128 * t, 128 * t + 128), q_, s_)
         act(a("bits", 864, 864 + h), bank(4, h), F.Sign, 0.0, 1.0)
+        ts(a("bits", 864 + h, 1152), bank(5, h), 0.0, A.is_gt)
 
-    def signs_rest():
-        ts(a("bits", 864 + C // 2, 1152), bank(5, C // 2), 0.0, A.is_gt)
-
-    dma("y", T.xin[:], T.x[:], wr=[a("xin")])
+    dma("y", T.xin[:], T.x[:], wr=[a("xin")], lat=3500)
     dma("s", T.twb[:, 0:60], T.tw[:], wr=[a("twb")])
     dma("s", T.ub[:], T.u[:], wr=[a("ub")])
     dma("y", T.wq[:].bitcast(dt.uint8), T.wc[:], wr=[a("wq")])
@@ -267,12 +320,13 @@ def rank_program(g, core, T, topo):
     ms(a("ones"), 1.0)
     iota(a("r16"), [[1, 16]], 128, -1)
     iota(a("base4"), [[4, 384]], 0, 0, True)
-    rec("g", lambda e: e.affine_select(T.ident[:], T.ones[:], [[-1, 128]], A.is_equal, 0.0, 0, 1), [a("ones")], [a("ident")])
+    rec("g", lambda e: e.affine_select(T.ident[:], T.ones[:], [[-1, 128]], A.is_equal, 0.0, 0, 1), [a("ones")], [a("ident")], 400)
     iota(a("uoi"), [[1, 3], [16, 8]], 0, 0)
     iota(a("c16"), [[16, 18]], 0, 0)
     for name, c in (("nf", NOWHERE), ("inf", NOWHERE), ("pf", 0.0)):
         act(a(name, C, 384), a("ones", 0, 96), F.Identity, 0.0, c)
     act(a("bits", 1152, 1248), a("ones", 0, 96), F.Identity, 0.0, 0.0)
+    act(a("f0"), a("ones", 0, 120), F.Identity, 0.0, 0.0)
     iota(a("itab", 0, 768), [[1, 768]], 0, 0, True)
     ms(a("eb"), 0.0)
     ts(a("r16b"), a("r16"), 15, A.bitwise_and)
@@ -288,256 +342,192 @@ def rank_program(g, core, T, topo):
     tt(a("cm", 0, 16), a("c0"), a("c1"), A.max)
     ts(s_num, a("col", 4, 5), 1.0, A.mult, 1.0 / BIG, A.add)
     ts(s_thr, a("col", 4, 5), -BIG / 2, A.mult, BIG / 2, A.add)
-    cp(a("cm", 16, 32), a("cm", 0, 16))
     cp(s_pm, a("coli", 1, 2))
     ts(s_hi, s_num, 1.0 / 4096, A.mult)
-    cp(a("cm", 32, 64), a("cm", 0, 32))
-    ts(s_tri, s_num, 1.0 / 16384, A.mult)
-    cp(a("cm", 64, 128), a("cm", 0, 64))
+    for lo, n in ((16, 16), (32, 32), (64, 64), (128, 128), (256, 32), (288, 288), (576, 576)):
+        cp(a("cm", lo, lo + n), a("cm", 0, n))
     cp(a("eb", 3, 515, 4), a("ident"))
-    cp(a("cm", 128, 256), a("cm", 0, 128))
-    cp(a("cm", 256, 288), a("cm", 0, 32))
     for b in range(4):
         quant(a("eq", 128 * b, 128 * b + 128), a("es", 128 * b, 128 * b + 128), a("eb", 3 - b, 515 - b))
     cp(a("tw16", 0, 60), a("twb", 0, 60))
     cp(a("uoff"), a("uoi"))
     ts(a("vw"), a("c16"), s_pm, A.add)
-    sc(a("tfn", 128, 960), ind(a("inttab"), a("tw16", 8, 60)))
-    cp(a("cm", 288, 576), a("cm", 0, 288))
-    cp(a("tfn", 0, 128), ind(a("inttab"), a("tw16", 0, 8)))
-    cp(a("cm", 576, 1152), a("cm", 0, 576))
+    sc(a("tfn", 192, 960), ind(a("inttab"), a("tw16", 12, 60)))
+    cp(a("tfn", 0, 192), ind(a("inttab"), a("tw16", 0, 12)))
     quant(a("uq"), a("us"), a("ub"))
-    pick_codes(0, 128)
-    pick_scales(0, 128)
+    pick_u(0, 128)
     signs(0)
     for k in range(3):
         scan(a("so", C * k, C * k + C), a("tfn", k, 3 * C, 3))
     scan(a("so", 3 * C, 960), a("tfn", 3 * C, 960))
-    signs_rest()
     ts(a("lb"), a("so", 15, 960, 16), s_num, A.mult)
     ts(a("tb", 0, 54), a("so", 15, 864, 16), s_num, A.mult)
+    ts(a("tb", 54, 90), a("so", 15, 576, 16), s_num, A.mult)
     column(a("e54"), a("lb", 0, 54))
     for k in range(3):
         act(a("hb", 18 * k, 18 * k + 18), a("vw"), F.Identity, float(k), 4.0)
+    keys()
+    for k in range(4):
+        act(a("ntab", k, 1536, 4), a("base4"), F.Identity, 4096.0 * ((k + 1) % 3), 4096.0)
+    act(a("two", 0, 2 * C, 2), a("base4", 0, C), F.Identity, -1e29, 0.0)
+    act(a("two", 1, 2 * C, 2), a("base4", 0, C), F.Identity, 0.0, 0.0)
+    for k, c in enumerate((0.0, 4.0, 2.0)):
+        act(a("hc", 18 * k, 18 * k + 18), a("vw"), F.Identity, c, 0.0)
+    pick_u(128, 256)
+    pick_u(256, 384)
+    quant(a("vq"), a("vs"), a("vb"))
 
     for t in range(R):
         more = t < R - 1
         qx, sx = a("qx%d" % t), a("sx%d" % t)
         lq, ls, lst, fp, fn = "lq%d" % t, "ls%d" % t, "lst%d" % t, "fp%d" % t, "fn%d" % t
         u8 = qx[0].bitcast(dt.uint8)
-        send([(nxt, "all", fp, u8, T[lq][:, C:2 * C].bitcast(dt.uint8))], [qx])
+        big = send([(nxt, "all", fp, u8, T[lq][:, C:2 * C].bitcast(dt.uint8))], [qx])
         send([(nxt, "low", fp, sx[0], T[ls][:, C:2 * C]), (prv, "high", fn, sx[0], T[ls][:, 0:C])], [sx])
         send([(prv, "all", fn, u8, T[lq][:, 0:C].bitcast(dt.uint8))], [qx])
         if t == 0:
             iota(a("itab", 768, 1540), [[1, 772]], 768, 0, True)
 
-        def unpack(b, bk, q_, s_, pre=()):
-            mm(bank(bk), a("eq", 128 * b, 128 * b + 128), a("es", 128 * b, 128 * b + 128), q_, s_, pre)
-
-        def far(h, planes):
-            for b in planes:
-                unpack(b, 4 + b, a(lq, C * h, C * h + C), a(ls, C * h, C * h + C),
-                       [(fp, from_prv) if h else (fn, from_nxt)] if b == 0 else ())
-                sc(a("dn", 576 * b + C * h, 576 * b + C * h + C), bank(4 + b))
+        def unpack(b, bk, q_, s_, pre=(), after=()):
+            mm(bank(bk), a("eq", 128 * b, 128 * b + 128), a("es", 128 * b, 128 * b + 128), q_, s_, pre, after)
 
         pos = a("bits", 864, 1248)
         sc(a("bits", 448, 864), ind(pos, a("e54", 28, 54)))
         cp(a("bits", 0, 448), ind(pos, a("e54", 0, 28)))
-        if t == 0:
-            for k in range(4):
-                act(a("ntab", k, 1536, 4), a("base4"), F.Identity, 4096.0 * ((k + 1) % 3), 4096.0)
         for b in range(4):
             unpack(b, b, qx, sx)
             sc(a("dw", 384 * b, 384 * b + C), bank(b))
+        for h in (1, 0):
+            for b in range(4):
+                unpack(b, 4 + b, a(lq, C * h, C * h + C), a(ls, C * h, C * h + C),
+                       [(fp, from_prv) if h else (fn, from_nxt)] if b == 0 else (), [(big, LAG_A if h else LAG_B)])
+                sc(a("dn", 576 * b + C * h, 576 * b + C * h + C), bank(4 + b))
         scan(a("sb"), a("bits", 0, 1152))
-        if t == 0:
-            priorities()
-            cp(a("tb", 54, 90), a("lb", 0, 36))
         ts(a("pw"), a("sb", 15, 1152, 16), s_thr, A.is_gt)
         for k in range(3):
             tt(a("w", 18 * k, 18 * k + 18), a("pw", 18 * k, 18 * k + 18), a("pw", 54, 72), A.not_equal)
-        if t:
-            tt(a("aq", 18, 24), a("lb", 54, 60), a("t2", 54, 60), A.add)
-        else:
-            cp(a("aq", 18, 24), a("lb", 54, 60))
-        tt(a("wp"), a("w"), a("pr"), A.mult)
-        column(a("esl"), a("lb", 54, 60))
-        ts(a("wp", 0, 18), a("wp", 0, 18), 2048.0, A.max)
-        if t:
-            tt(a("lb", 54, 60), a("lb", 54, 60), a("t2", 54, 60), A.add)
-        else:
-            cp(a("kb", 36, 42), a("lb", 54, 60))
-        for s_ in range(3):
-            tt(a("key", s_, 216, 4), a("wp"), a("tb", 18 * s_, 18 * s_ + 54), A.add)
-        tt(a("key", 3, 216, 4), a("wp"), a("hb"), A.add)
+        for s_ in range(4):
+            tt(a("key", s_, 216, 4), a("w"), a("kk", 54 * s_, 54 * s_ + 54), A.mult)
         tt(a("k1"), a("key", 0, 72), a("key", 72, 144), A.max)
-        tt(a("best"), a("k1"), a("key", 144, 216), A.max)
+        tt(a("k2"), a("key", 144, 216), a("dfl"), A.max)
+        tt(a("best"), a("k1"), a("k2"), A.max)
         ts(a("idx"), a("best", 0, 72, 4), 4095, A.bitwise_and)
-        ts(a("lb", 18, 36), a("best", 1, 72, 4), 2047, A.bitwise_and)
-        ts(a("lb", 0, 18), a("best", 0, 72, 4), 2047, A.bitwise_and)
+        for s_ in range(3):
+            ts(a("lb", 18 * s_, 18 * s_ + 18), a("best", s_, 72, 4), 2047, A.bitwise_and)
         ts(a("offn"), a("idx"), float(NONE), A.min)
         cp(a("offp"), a("lb", 18, 36))
         column(a("e2", 0, 18), a("lb", 0, 18))
         sc(a("nf", 0, C), ind(a("ntab"), a("offn")))
         cp(a("af"), ind(a("itab"), a("offn")))
         sc(a("pf", 0, C), ind(a("itab"), a("offp")))
-        ts(a("lb", 36, 54), a("best", 2, 72, 4), 2047, A.bitwise_and)
         tt(a("inf", 0, C), ind(a("nf"), a("e2", 0, 18)), a("af"), A.add)
-        if t == 0:
-            sc(a("kb", 0, 18), a("vw"))
-            sc(a("kb", 18, 36), a("vw"))
-        tt(a("db", 18, 36), a("lb", 36, 54), a("lb", 18, 36), A.subtract)
         sc(a("zf", C, 384), ind(a("inf"), a("esl")))
         tt(a("zf", 0, C), ind(a("pf"), a("e2", 0, 18)), a("inf", 0, C), A.add)
         sc(a("gf", 0, C), ind(a("inf"), a("e2", 0, 18)))
-        if t == 0:
-            act(a("two", 0, 2 * C, 2), a("base4", 0, C), F.Identity, -1e29, 0.0)
-            act(a("two", 1, 2 * C, 2), a("base4", 0, C), F.Identity, 0.0, 0.0)
-            for k, c in enumerate((0.0, 4.0, 2.0)):
-                act(a("hc", 18 * k, 18 * k + 18), a("vw"), F.Identity, c, 0.0)
-        far(1, range(EARLY))
-        tt(a("aq", 0, 18), a("lb", 36, 54), a("lb", 0, 18), A.add)
-        scan(a("so", 0, 384), a("zf"))
         ts(a("xz"), a("best", 3, 72, 4), 3, A.bitwise_and)
-        ts(a("ib", 36, 60), a("so", 15, 384, 16), s_num, A.mult)
-        ts(a("xb", 54, 60), a("so", C + 15, 384, 16), s_hi, A.mult, -0.49, A.add)
-        ts(a("xb", 18, 36), a("so", 15, C, 16), s_tri, A.mult, -0.49, A.add)
-        ts(a("xb", 36, 54), a("so", 15, C, 16), s_tri, A.mult, -0.49, A.add)
-        ts(a("lo", 36, 60), a("ib", 36, 60), 4095, A.bitwise_and)
-        tt(a("mb", 18, 60), a("xb", 18, 60), a("kb"), A.is_equal)
-        tt(a("db", 36, 60), a("lo", 36, 60), a("aq"), A.subtract)
-        if more:
-            ts(a("hs", 0, 18), a("best", 3, 72, 4), 2047, A.bitwise_and)
-        tt(a("t1", 18, 60), a("mb", 18, 60), a("db", 18, 60), A.mult)
-        if more:
-            ts(a("th", 0, 18), a("xz"), -3.0, A.mult, -3.0, A.min)
-        tt(a("lb", 18, 60), a("lb", 18, 60), a("t1", 18, 60), A.add)
+        ts(a("hs", 0, 18), a("best", 3, 72, 4), 2047, A.bitwise_and)
+        ts(a("th", 0, 18), a("xz"), -3.0, A.mult, -3.0, A.min)
+        tt(a("hs", 18, 36), a("hs", 0, 18), a("th", 0, 18), A.add)
         if more:
             ts(a("th", 18, 36), a("xz"), -3.0, A.mult, -3.0, A.max)
+            tt(a("hs", 36, 54), a("hs", 0, 18), a("th", 18, 36), A.add)
+            tt(a("hb"), a("hs"), a("hc"), A.add)
+        ts(a("kb", 0, 18), a("hs", 18, 36), 4.0, A.add)
+        ts(a("kb", 18, 36), a("hs", 18, 36), 4.0, A.add)
+        ts(a("aq", 18, 36), a("hs", 18, 36), 4.0, A.add, 4096.0, A.mult)
+        tt(a("aq", 0, 18), a("lb", 36, 54), a("lb", 0, 18), A.add)
+        tt(a("uu", 0, 18), a("aq", 0, 18), a("aq", 18, 36), A.add)
+        tt(even("f1", 18, 36), a("lb", 36, 54), a("lb", 18, 36), A.subtract)
+        cp(odd("f1", 0, 60), a("lb"))
+        scan(a("so", 0, 384), a("zf"))
+        ts(a("ib", 36, 60), a("so", 15, 384, 16), s_num, A.mult)
+        ts(a("xb", 36, 60), a("so", 15, 384, 16), s_hi, A.mult, -0.49, A.add)
+        ts(a("xb", 18, 36), a("so", 15, C, 16), s_hi, A.mult, -0.49, A.add)
+        tt(odd("f0", 18, 60), a("xb", 18, 60), a("kb"), A.is_equal)
+        tt(even("f1", 36, 60), a("ib", 36, 60), a("uu"), A.subtract)
+        scan(a("fo", 36, 120), a("f1", 36, 120), a("f0", 36, 120))
         ea, eb_ = a("esend", 8 * t, 8 * t + 3), a("esend", 8 * t + 4, 8 * t + 7)
-        column(ea, a("lb", 54, 57), 4.0 * C)
-        column(eb_, a("lb", 57, 60))
-        send([(nxt, "low", lst, ea[0], T[lst][:, 3:6]), (prv, "high", lst, eb_[0], T[lst][:, 0:3])], [ea, eb_])
+        column(ea, odd("fo", 54, 57), 4.0 * C)
+        column(eb_, odd("fo", 57, 60))
+        small = send([(nxt, "low", lst, ea[0], T[lst][:, 3:6]), (prv, "high", lst, eb_[0], T[lst][:, 0:3])], [ea, eb_])
         if t == 0:
             iota(a("otab", 0, 4 * C), [[3, C], [1, 4]], 0, 0, True)
             iota(a("otab", 4 * C, 1536), [[1, 2 * S], [0, 4]], 3 * C, 0, True)
-        column(a("e2", 18, 54), a("lb", 18, 54))
-        ts(a("t2", 0, 54), a("lb", 0, 54), 4097.0, A.mult)
+        column(a("e2", 18, 54), odd("fo", 18, 54))
+        cp(a("lb", 18, 54), odd("fo", 18, 54))
+        cp(odd("f1", 18, 54), odd("fo", 18, 54))
+        ts(a("u2"), a("lb", 0, 54), 4097.0, A.mult)
         sc(a("gf", 2 * C, 3 * C), ind(a("inf"), a("e2", 36, 54)))
         cp(a("gf", C, 2 * C), ind(a("inf"), a("e2", 18, 36)))
-        far(1, range(EARLY, 4))
-        far(0, range(4))
         scan(a("so", 0, 864), a("gf"))
-        if more:
-            tt(a("hs", 18, 36), a("hs", 0, 18), a("th", 0, 18), A.add)
         ts(a("ib", 0, 54), a("so", 15, 864, 16), s_num, A.mult)
         ts(a("xb", 0, 54), a("so", 15, 864, 16), s_hi, A.mult, -0.49, A.add)
-        tt(a("db", 0, 54), a("ib", 0, 54), a("t2", 0, 54), A.subtract)
-        tt(a("mb", 0, 54), a("xb", 0, 54), a("lb", 0, 54), A.is_equal)
-        if more:
-            tt(a("hs", 36, 54), a("hs", 0, 18), a("th", 18, 36), A.add)
-        tt(a("t1", 0, 54), a("mb", 0, 54), a("db", 0, 54), A.mult)
-        if more:
-            tt(a("hb"), a("hs"), a("hc"), A.add)
-        tt(a("lb", 0, 54), a("lb", 0, 54), a("t1", 0, 54), A.add)
-        column(a("e54"), a("lb", 0, 54))
-
-        def plane(b):
-            return a("dw", 384 * b, 384 * b + 384)
-
-        def border(b):
-            sc(a("dw", 384 * b + C, 384 * b + 384), ind(a("dn", 576 * b, 576 * b + 576), a(lst, 0, 6)),
-               [(lst, lists_in)] if b == 0 else ())
-
-        def both(b):
-            for k in range(2):
-                sc(a("gi", 2 * C * (b - 2) + k, 2 * C * (b - 1), 2), ind(plane(b), a("e54", 18 * k, 18 * k + 18)))
-
-        border(0)
-        border(1)
-        border(2)
-        sc(a("g0", C, 2 * C), ind(plane(1), a("e54", 0, 18)))
-        border(3)
-        both(2)
-        both(3)
-        if t == 0:
-            pick_scales(128, 384)
+        tt(even("f1", 0, 54), a("ib", 0, 54), a("u2"), A.subtract)
+        tt(odd("f0", 0, 54), a("xb", 0, 54), a("lb", 0, 54), A.is_equal)
+        scan(a("fo", 0, 108), a("f1", 0, 108), a("f0", 0, 108))
+        column(a("e54"), odd("fo", 0, 54))
+        cp(a("lb"), odd("fo", 0, 60))
         ts(a("t1"), a("lb"), 3, A.bitwise_and)
         ts(a("t2"), a("t1"), 0.0, A.is_equal, 3.0, A.mult)
         ts(a("t3"), a("t2"), -1.0, A.add)
-        tt(a("t1"), a("lb"), a("t3"), A.add)
-        tt(a("t2"), a("t1"), a("xb"), A.is_equal)
-        tt(a("t1"), a("t2"), a("mb"), A.max)
-        tt(a("t2"), a("t1"), a("t3"), A.mult)
-        if not more:
-            tt(a("tb", 0, 54), a("lb", 0, 54), a("t2", 0, 54), A.add)
-            tt(a("tb", 54, 90), a("lb", 0, 36), a("t2", 0, 36), A.add)
-
-        def p1(b):
-            tt(a("g1", C * b, C * b + C), ind(plane(b), a("e54", 18, 36)), a("g0", C * b, C * b + C), A.max)
-
-        def p2(b):
-            tt(a("mt", b, 4 * C, 4), ind(plane(b), a("e54", 36, 54)), a("g1", C * b, C * b + C), A.max)
-
-        def p3(b):
-            lo, hi = 2 * C * (b - 2), 2 * C * (b - 1)
-            o, x, m = a("go", lo, hi), a("gi", lo, hi), a("two")
-            rec("v", lambda e: e.tensor_tensor_scan(o[0], m[0], x[0], 0.0, A.add, A.max), [m, x], [o])
-
-        def p4(b):
-            tt(a("mt", b, 4 * C, 4), ind(plane(b), a("e54", 36, 54)), a("go", 2 * C * (b - 2) + 1, 2 * C * (b - 1), 2), A.max)
-
-        cp(a("g0", 0, C), ind(plane(0), a("e54", 0, 18)))
-        p1(0)
-        p1(1)
-        p2(0)
-        p2(1)
-        p3(2)
-        p4(2)
-        p3(3)
-        p4(3)
-        quant(a("mq"), a("ms"), a("mt"))
-        for b in range(4):
-            mm(bank(4 + b), a("wq", 128 * b, 128 * b + 128), a("wsc", 128 * b, 128 * b + 128), a("mq"), a("ms"))
-            act(a("rl", C * b, C * b + C), bank(4 + b), F.Relu, 0.0, 0.015625)
+        tt(a("t4"), a("lb"), a("t3"), A.add)
+        tt(a("t5"), a("t4"), a("xb"), A.is_equal)
+        tt(a("t6"), a("t5"), odd("f0", 0, 60), A.max)
+        tt(a("t7"), a("t6"), a("t3"), A.mult)
+        tt(a("tb", 0, 54), a("lb", 0, 54), a("t7", 0, 54), A.add)
+        tt(a("tb", 54, 90), a("lb", 0, 36), a("t7", 0, 36), A.add)
+        tt(a("lb", 54, 60), a("lb", 54, 60), a("t7", 54, 60), A.add)
         if more:
-            tt(a("tb", 0, 54), a("lb", 0, 54), a("t2", 0, 54), A.add)
-            if t == 0:
-                pick_codes(128, 384)
-            else:
-                quant(a("vq"), a("vs"), a("vb"))
-            priorities()
+            keys()
         else:
             for j in range(3):
                 ts(a("wp", 18 * j, 18 * j + 18), a("xz"), float((3 - j) % 3), A.is_equal, 4096.0, A.mult)
-            tt(a("lb", 54, 60), a("lb", 54, 60), a("t2", 54, 60), A.add)
             for s_ in range(3):
                 tt(a("key", s_, 162, 3), a("wp"), a("tb", 18 * s_, 18 * s_ + 54), A.add)
             cp(a("oto", 54, 60), a("lb", 54, 60))
             tt(a("k1", 0, 54), a("key", 0, 54), a("key", 54, 108), A.max)
-            tt(a("best", 0, 54), a("k1", 0, 54), a("key", 108, 162), A.max)
+            tt(a("k2", 0, 54), a("k1", 0, 54), a("key", 108, 162), A.max)
             for s_ in range(3):
-                ts(a("oto", 18 * s_, 18 * s_ + 18), a("best", s_, 54, 3), -4096.0, A.add)
+                ts(a("oto", 18 * s_, 18 * s_ + 18), a("k2", s_, 54, 3), -4096.0, A.add)
+                sc(a("otf", s_, 3 * C, 3), ind(a("otab"), a("oto", 18 * s_, 18 * s_ + 18)))
+            sc(a("otf", 3 * C, 960), ind(a("otab"), a("oto", 54, 60)))
+            dma("s", T.ot[:], T.otf[0:128:16, :], rd=[a("otf")])
+
+        def plane(b):
+            return a("dw", 384 * b, 384 * b + 384)
+
+        gate = [(small, LAG_L)]
         for b in range(4):
+            i = sc(a("dw", 384 * b + C, 384 * b + 384), ind(a("dn", 576 * b, 576 * b + 576), a(lst, 0, 6)),
+                   [(lst, lists_in)] if b == 0 else (), gate)
+            gate = [(i, 0)]
+        cp(a("g0", 0, C), ind(plane(0), a("e54", 0, 18)))
+        sc(a("g0", C, 2 * C), ind(plane(1), a("e54", 0, 18)))
+        for b in (0, 1):
+            tt(a("g1", C * b, C * b + C), ind(plane(b), a("e54", 18, 36)), a("g0", C * b, C * b + C), A.max)
+            tt(a("mt", b, 4 * C, 4), ind(plane(b), a("e54", 36, 54)), a("g1", C * b, C * b + C), A.max)
+        for b in (2, 3):
+            lo, hi = 2 * C * (b - 2), 2 * C * (b - 1)
+            for k in range(2):
+                sc(a("gi", lo + k, hi, 2), ind(plane(b), a("e54", 18 * k, 18 * k + 18)))
+            scan(a("go", lo, hi), a("gi", lo, hi), a("two"), A.add, A.max)
+            tt(a("mt", b, 4 * C, 4), ind(plane(b), a("e54", 36, 54)), a("go", lo + 1, hi, 2), A.max)
+        quant(a("mq"), a("ms"), a("mt"))
+        for b in range(4):
+            mm(bank(4 + b), a("wq", 128 * b, 128 * b + 128), a("wsc", 128 * b, 128 * b + 128), a("mq"), a("ms"))
+            act(a("rl", C * b, C * b + C), bank(4 + b), F.Relu, 0.0, 0.015625)
             tt(a("xt", b, 4 * C, 4), bank(b), a("rl", C * b, C * b + C), A.add)
         if more:
             signs(t + 1)
-            tt(a("tb", 54, 90), a("lb", 0, 36), a("t2", 0, 36), A.add)
-            tt(a("kb", 36, 42), a("lb", 54, 60), a("t2", 54, 60), A.add)
-            signs_rest()
         else:
             quant(a("qx%d" % R), a("sx%d" % R), a("xt"))
 
     qx, sx = a("qx%d" % R), a("sx%d" % R)
-    for k in range(3):
-        sc(a("otf", k, 3 * C, 3), ind(a("otab"), a("oto", 18 * k, 18 * k + 18)))
     mm(bank(4), a("vq"), a("vs"), qx, sx)
     dma("y", T.oc[:], qx[0].bitcast(dt.uint8), rd=[qx])
     for k in range(4):
-        dma("y", T.osc[4 * k:4 * k + 4, :], T["sx%d" % R][32 * k:32 * k + 4, :], rd=[sx])
-    cp(a("otf", 3 * C, 960), ind(a("otab"), a("oto", 54, 60)))
+        dma("y" if k < 2 else "s", T.osc[4 * k:4 * k + 4, :], T["sx%d" % R][32 * k:32 * k + 4, :], rd=[sx])
     cp(a("yb"), bank(4))
     dma("y", T.y[:], T.yb[:], rd=[a("yb")])
-    dma("s", T.ot[:], T.otf[0:128:16, :], rd=[a("otf")])
-    emit(g, T, ops)
+    emit(g, T, order(ops))
     g.wait_ge(T.sem.sent, sent[0])

@@ -2,25 +2,31 @@ from concourse.bass import DstId, RemoteDMATransfer
 from concourse.mybir import dt, AluOpType, ActivationFunctionType
 
 C, S, R = 288, 48, 3
+H = C // 2
 FP8 = "float8_e4m3fn_x4"
-BIG = float(2 ** 32)
-NONE = 1536
+BIG = float(2 ** 50)
+NONE = 1920
 NOWHERE = 2047 * 4096.0
-WAKE, TOL, LAG_A, LAG_B, LAG_L = 200, 60, 6000, 8000, 3000
+SPLIT = 22
+BORDER = "vsvs"
+WAYS = (3, 3, 2, 2)
+WAKE, TOL, LAG_A, LAG_B, LAG_L, LAG_1 = 200, 60, 4500, 6500, 2500, 1500
 
 SCRATCH = {"ps": ("psum", [128, 4096], "float32")}
 for _d, _bufs in (
-    ("bfloat16", {"xin": 4 * C, "xt": 4 * C, "mt": 4 * C, "ub": 512, "vb": 512, "eb": 520, "ones": 128, "ident": 128,
-                  "cm": 1152, "sb": 1152, "bits": 1248, "dw": 4 * 384, "dn": 4 * 576, "g0": 2 * C, "g1": 2 * C,
-                  "gi": 4 * C, "go": 4 * C, "two": 2 * C}),
-    ("float32", {"c0": 16, "c1": 16, "col": 8, "vw": 18, "base4": 384, "inttab": 960, "itab": 1540, "ntab": 1540,
-                 "otab": 1536, "tfn": 960, "otf": 960, "so": 960, "pw": 72, "w": 54, "wp": 54, "pr": 54, "hb": 54,
-                 "hc": 54, "kb": 42, "af": C, "nf": 384, "pf": 384, "inf": 384, "zf": 384, "gf": 864, "rl": 4 * C,
-                 "yb": C, "kk": 216, "dfl": 72, "f0": 120, "f1": 120, "fo": 120, "uu": 24, "u2": 54}),
-    ("int32", {"twb": 64, "r16": 16, "r16b": 16, "coli": 8, "c16": 18, "uoi": 24, "key": 216, "k1": 72, "k2": 72,
-               "best": 72, "tb": 90, "hs": 54, "th": 36, "lb": 60, "xb": 60, "ib": 60, "p1": 54, "p2": 54, "p3": 54,
-               "t1": 60, "t2": 60, "t3": 60, "t4": 60, "t5": 60, "t6": 60, "t7": 60, "idx": 18, "aq": 36, "xz": 18}),
-    ("uint16", {"tw16": 64, "uoff": 24, "offn": 18, "offp": 18, "e2": 54, "e54": 54, "esl": 6, "oto": 60, "esend": 24}),
+    ("bfloat16", {"xin": 4 * C, "xt": 4 * C, "mt": 4 * C, "ub": 512, "vb": 512, "eb": 520, "ones": 384, "five": 384,
+                  "ident": 128, "cm": 576, "sb": 864, "sbo": C, "sg": 384, "bits": 864, "dw": 4 * 384, "du": 4 * C,
+                  "dn": 4 * 576, "g0": 4 * C, "g1": 4 * C, "gi": 8 * C, "go": 8 * C, "two": 2 * C}),
+    ("float32", {"c0": 16, "c1": 16, "col": 12, "vw": 18, "base": 384, "inttab": 960, "turn": 1928, "otab": 1920,
+                 "tfn": 960, "otf": 960, "so": 960, "si": C, "sp": C, "own": 18, "w": 54, "pr": 54, "lab": 54, "v5": 54,
+                 "kap": 54, "af": C, "nf": 384, "pf": 384, "inf": 384, "bo": C, "gf": 960, "yb": C, "kk": 162,
+                 "dfl": 54, "f0": 120, "f1": 120, "fo": 120, "h0": 72, "h1": 72, "ho": 72, "yy": 60, "tb": 60,
+                 "t4": 54, "tk": 90, "low": 54, "thr": 18, "zf": 18, "e1": 60, "e2f": 60, "cor": 60, "val": 60,
+                 "ks": 18}),
+    ("int32", {"twb": 64, "r16": 16, "r16b": 16, "coli": 8, "c16": 18, "uoi": 24, "key": 162, "k1": 54, "k2": 54,
+               "best": 54, "lb": 54, "idx": 18, "nd": 60, "ki": 36}),
+    ("uint16", {"tw16": 64, "uoff": 24, "offn": 18, "offa": 18, "offp": 18, "e2": 54, "e54": 54, "esl": 6, "oto": 60,
+                "esend": 24}),
     (FP8, {"wq": 512, "uq": 128, "uq2": 384, "vq": 128, "eq": 512, "mq": C}),
     ("uint8", {"wsc": 512, "us": 128, "us2": 384, "vs": 128, "es": 512, "ms": C}),
 ):
@@ -57,12 +63,25 @@ def clash(x, o):
     return o["q"] != x["q"] and any(a[0] == "ps" and meet(a, b) for a in x["r"] for b in o["r"])
 
 
+def clashes(ops):
+    seen, out = {}, []
+    for i, x in enumerate(ops):
+        names = {z[0] for z in x["r"] + x["w"]}
+        near = set()
+        for name in names:
+            near.update(seen.setdefault(name, []))
+            seen[name].append(i)
+        out.append(sorted(j for j in near if clash(x, ops[j])))
+    return out
+
+
 def order(ops):
     n = len(ops)
     dep = []
     last = {}
+    must = clashes(ops)
     for i, x in enumerate(ops):
-        d = [(j, ops[j]["cost"] + ops[j]["lat"] + WAKE) for j in range(i) if clash(x, ops[j])]
+        d = [(j, ops[j]["cost"] + ops[j]["lat"] + WAKE) for j in must[i]]
         d += x["after"]
         if x["q"] in "tgy":
             if x["q"] in last:
@@ -74,13 +93,17 @@ def order(ops):
         for j, w in dep[i]:
             rest[j] = max(rest[j], w + rest[i])
     start, free, out = {}, {q: 0 for q in "vstgy"}, []
-    todo = list(range(n))
+    users, left, soon = [[] for _ in ops], [0] * n, [0] * n
+    for i in range(n):
+        for j, w in dep[i]:
+            users[j].append((i, w))
+            left[i] += 1
+    todo = [i for i in range(n) if left[i] == 0]
     while todo:
         ready = {}
         for i in todo:
-            if all(j in start for j, w in dep[i]):
-                q = ops[i]["q"]
-                ready.setdefault(q, []).append((max([free[q]] + [start[j] + w for j, w in dep[i]]), i))
+            q = ops[i]["q"]
+            ready.setdefault(q, []).append((max(free[q], soon[i]), i))
         picks = []
         for q in ready:
             top = max(ready[q], key=lambda z: (rest[z[1]], -z[1]))
@@ -90,6 +113,11 @@ def order(ops):
         start[i] = at
         free[ops[i]["q"]] = at + ops[i]["cost"]
         todo.remove(i)
+        for j, w in users[i]:
+            soon[j] = max(soon[j], at + w)
+            left[j] -= 1
+            if left[j] == 0:
+                todo.append(j)
         out.append(ops[i])
     return out
 
@@ -99,10 +127,11 @@ def emit(g, T, ops):
     n = len(ops)
     known = {q: set() for q in Q}
     closure, waits, first, before, prev = [], [], {}, {}, {}
+    must = clashes(ops)
     for i in range(n):
         q = ops[i]["q"]
         k = known[q]
-        need = [j for j in range(i) if j not in k and clash(ops[i], ops[j])]
+        need = [j for j in must[i] if j not in k]
         keep = [j for j in need if not any(j in closure[x] for x in need if x != j)]
         for j in keep:
             k |= closure[j]
@@ -192,6 +221,9 @@ def rank_program(g, core, T, topo):
     def even(name, lo, hi):
         return a(name, 2 * lo, 2 * hi, 2)
 
+    def ends(name, lo, hi):
+        return a(name, 16 * lo + 15, 16 * hi, 16)
+
     def bank(b, n=C):
         return a("ps", 512 * b, 512 * b + n)
 
@@ -204,7 +236,7 @@ def rank_program(g, core, T, topo):
             if isinstance(x, tuple):
                 r += x[1]
                 if x[2] < 0:
-                    cost = 60 + 1.2 * wr[0][2]
+                    cost = 60 + 1.3 * wr[0][2]
         w = []
         for x in wr:
             w += x[1]
@@ -227,30 +259,30 @@ def rank_program(g, core, T, topo):
         else:
             rec("v", lambda e: e.tensor_scalar(o[0], x[0], val(s1), val(s2), op0, op1), [x, s1, s2], [o], o[2] * 0.83)
 
-    def cp(o, x):
-        rec("v", lambda e: e.tensor_copy(o[0], x[0]), [x], [o], o[2] * per(o, x))
+    def cp(o, x, pre=(), after=()):
+        return rec("v", lambda e: e.tensor_copy(o[0], x[0]), [x], [o], o[2] * per(o, x), pre=pre, after=after)
 
     def ms(o, c):
         rec("v", lambda e: e.memset(o[0], c), [], [o], o[2] * per(o))
 
-    def scan(o, x, m=None, op0=A.mult, op1=A.add):
+    def scan(o, x, m=None, op0=A.mult, op1=A.add, first=0.0):
         m = m or a("cm", 0, o[2])
-        rec("v", lambda e: e.tensor_tensor_scan(o[0], m[0], x[0], 0.0, op0, op1), [m, x], [o], o[2] * per(o, x, m))
+        rec("v", lambda e: e.tensor_tensor_scan(o[0], m[0], x[0], first, op0, op1), [m, x], [o], o[2] * per(o, x, m))
 
     def sc(o, x, pre=(), after=()):
         return rec("s", lambda e: e.activation(o[0], x[0], F.Copy), [x], [o], 60 + o[2] * 0.83, pre=pre, after=after)
 
-    def act(o, x, func, bias, scale):
-        rec("s", lambda e: e.activation(o[0], x[0], func, bias=bias, scale=scale), [x], [o], 60 + o[2] * 0.83)
+    def act(o, x, bias, scale, func=F.Identity):
+        rec("s", lambda e: e.activation(o[0], x[0], func, bias=bias, scale=val(scale)), [x, scale], [o], 60 + o[2] * 0.83)
 
     def quant(q, s, x):
         rec("v", lambda e: e.quantize_mx(q[0], s[0], x[0]), [x], [q, s], 12 + 0.22 * x[2])
 
-    def mm(o, wq, wsc, xq, xs, pre=(), after=()):
-        rec("t", lambda e: e.matmul_mx(o[0], wq[0], wsc[0], xq[0], xs[0], True, True), [wq, wsc, xq, xs], [o],
+    def mm(o, wq, wsc, xq, xs, pre=(), after=(), start=True, stop=True):
+        rec("t", lambda e: e.matmul_mx(o[0], wq[0], wsc[0], xq[0], xs[0], start, stop), [wq, wsc, xq, xs], [o],
             0.6 * o[2], pre=pre, after=after)
 
-    def dma(q, o, x, rd=(), wr=(), lat=2500):
+    def dma(q, o, x, rd=(), wr=(), lat=2000):
         rec(q, lambda e: e.dma_start(o, x), list(rd), list(wr), 100, kind="dma", lat=lat)
 
     def iota(o, pattern, base, cmul, small=False):
@@ -277,102 +309,116 @@ def rank_program(g, core, T, topo):
     from_nxt = len(part(nxt, core, "all")) + len(part(nxt, core, "high"))
     lists_in = len(part(prv, core, "low")) + len(part(nxt, core, "high"))
 
-    def column(o, x, shift=0.0):
-        ts(o, x, shift - 1.5, A.add, 0.25, A.mult)
+    c_big, c_inv, c_own, c_col, c_y, c_round, c_step, c_thr, c_mid, c_pm, c_last, c_rest = [a("col", i, i + 1) for i in range(12)]
 
-    s_num, s_hi, s_thr, s_pm = a("col", 0, 1), a("col", 1, 2), a("col", 2, 3), a("col", 3, 4)
+    def column(o, x, shift=0.0):
+        ts(o, x, c_col, A.mult, shift - 0.2, A.add)
+
+    def near(o, x):
+        ts(o, x, c_round, A.add, c_round, A.is_equal)
 
     def keys():
-        tt(a("p1"), a("hb"), a("tb", 0, 54), A.min)
-        ts(a("p2"), a("tb", 0, 54), float(4 * C), A.is_ge, 4096.0, A.mult)
-        tt(a("p3"), a("p1"), a("p2"), A.add)
-        ts(a("pr"), a("p3"), -4096.0, A.mult, (4 * C + 1) * 4096.0, A.add)
-        for s_ in range(3):
-            tt(a("kk", 54 * s_, 54 * s_ + 54), a("pr"), a("tb", 18 * s_, 18 * s_ + 54), A.add)
-            ts(a("dfl", s_, 72, 4), a("tb", 18 * s_, 18 * s_ + 18), 2048.0, A.add)
-        tt(a("kk", 162, 216), a("pr"), a("hb"), A.add)
-        ts(a("dfl", 3, 72, 4), a("hb", 0, 18), 2048.0, A.add)
-        column(a("esl"), a("lb", 54, 60))
-        ts(a("uu", 18, 24), a("lb", 54, 60), 4097.0, A.mult)
-        cp(a("kb", 36, 42), a("lb", 54, 60))
+        tt(a("low"), a("lab"), a("tb", 0, 54), A.min)
+        ts(a("pr"), a("low"), -8192.0, A.mult, (5 * C + 1) * 8192.0, A.add)
+        act(a("t4"), a("tb", 0, 54), 0.0, 4.0)
+        tt(a("tk", 0, 54), a("t4"), a("kap"), A.add)
+        sc(a("tk", 54, 90), a("tk", 0, 36))
+        tt(a("kk", 0, 54), a("pr"), a("tb", 0, 54), A.add)
+        act(a("dfl", 0, 54, 3), a("tb", 0, 18), 2048.0, 1.0)
+        for s_ in (1, 2):
+            tt(a("kk", 54 * s_, 54 * s_ + 54), a("pr"), a("tk", 18 * s_, 18 * s_ + 54), A.add)
+            sc(a("dfl", s_, 54, 3), a("tk", 18 * s_, 18 * s_ + 18))
+        ts(a("esl"), a("tb", 54, 60), 0.2, A.mult, -0.2, A.add)
+        act(odd("f1", 54, 60), a("tb", 54, 60), 0.0, c_big)
+        act(a("yy", 54, 60), a("tb", 54, 60), 0.0, c_y)
 
     def pick_u(lo, hi):
         o = a("uoff", lo // 16, hi // 16)
         rec("v", lambda e: e.tensor_copy(T.uq2[:, lo:hi].bitcast(dt.uint32), T.uq[:, 0:128].bitcast(dt.uint32).indirect(o[0])),
-            [a("uq"), o], [a("uq2", lo, hi)], 60 + 1.2 * (hi - lo))
+            [a("uq"), o], [a("uq2", lo, hi)], 60 + 1.3 * (hi - lo))
         sc(a("us2", lo, hi), ind(a("us"), o))
 
-    def signs(t):
-        src, h = "xt" if t else "xin", C // 2
-        for i in range(2):
-            q_, s_ = a("qx%d" % t, h * i, h * i + h), a("sx%d" % t, h * i, h * i + h)
-            quant(q_, s_, a(src, 4 * h * i, 4 * h * i + 4 * h))
-            mm(bank(4 + i, h), a("uq2", 128 * t, 128 * t + 128), a("us2", 128 * t, 128 * t + 128), q_, s_)
-        act(a("bits", 864, 864 + h), bank(4, h), F.Sign, 0.0, 1.0)
-        ts(a("bits", 864 + h, 1152), bank(5, h), 0.0, A.is_gt)
+    def half(name, h):
+        return a(name, H * h, H * h + H)
 
-    dma("y", T.xin[:], T.x[:], wr=[a("xin")], lat=3500)
-    dma("s", T.twb[:, 0:60], T.tw[:], wr=[a("twb")])
-    dma("s", T.ub[:], T.u[:], wr=[a("ub")])
-    dma("y", T.wq[:].bitcast(dt.uint8), T.wc[:], wr=[a("wq")])
-    dma("y", T.wsc[:], T.ws[:], wr=[a("wsc")])
-    dma("y", T.vb[:], T.v[:], wr=[a("vb")])
+    def tile_e(b):
+        return a("eq", 128 * b, 128 * b + 128), a("es", 128 * b, 128 * b + 128)
+
+    def state(t, h):
+        q_, s_ = half("qx%d" % t, h), half("sx%d" % t, h)
+        quant(q_, s_, a("xt" if t else "xin", 4 * H * h, 4 * H * h + 4 * H))
+        if t < R:
+            mm(bank(h, H), a("uq2", 128 * t, 128 * t + 128), a("us2", 128 * t, 128 * t + 128), q_, s_)
+            ts(half("sg", h), bank(h, H), 0.0, A.is_gt, 0.5, A.subtract)
+        else:
+            mm(bank(h, H), a("vq"), a("vs"), q_, s_)
+
+    dma("y", T.twb[:, 0:60], T.tw[:], wr=[a("twb")], lat=1500)
+    dma("s", T.ub[:], T.u[:], wr=[a("ub")], lat=2200)
+    dma("y", T.xin[:], T.x[:], wr=[a("xin")], lat=2800)
+    dma("y", T.wq[:].bitcast(dt.uint8), T.wc[:], rd=[a("xin")], wr=[a("wq")], lat=4000)
+    dma("y", T.wsc[:], T.ws[:], wr=[a("wsc")], lat=4000)
+    dma("y", T.vb[:], T.v[:], wr=[a("vb")], lat=4500)
     ms(a("ones"), 1.0)
+    ms(a("five"), 5.0)
     iota(a("r16"), [[1, 16]], 128, -1)
-    iota(a("base4"), [[4, 384]], 0, 0, True)
-    rec("g", lambda e: e.affine_select(T.ident[:], T.ones[:], [[-1, 128]], A.is_equal, 0.0, 0, 1), [a("ones")], [a("ident")], 400)
     iota(a("uoi"), [[1, 3], [16, 8]], 0, 0)
     iota(a("c16"), [[16, 18]], 0, 0)
-    for name, c in (("nf", NOWHERE), ("inf", NOWHERE), ("pf", 0.0)):
-        act(a(name, C, 384), a("ones", 0, 96), F.Identity, 0.0, c)
-    act(a("bits", 1152, 1248), a("ones", 0, 96), F.Identity, 0.0, 0.0)
-    act(a("f0"), a("ones", 0, 120), F.Identity, 0.0, 0.0)
-    iota(a("itab", 0, 768), [[1, 768]], 0, 0, True)
+    rec("g", lambda e: e.affine_select(T.ident[:], T.ones[:, 0:128], [[-1, 128]], A.is_equal, 0.0, 0, 1),
+        [a("ones")], [a("ident")], 400)
+    scan(a("base"), a("five"), a("ones"), first=-5.0)
+    for k in range(3):
+        act(a("inttab", k, 3 * C, 3), a("base", 0, C), float(k), 1.0)
+    sc(a("inttab", 3 * C, 960), a("base", C, 384))
     ms(a("eb"), 0.0)
     ts(a("r16b"), a("r16"), 15, A.bitwise_and)
     ts(a("coli", 0, 1), a("r16", 0, 1), -1.0, A.mult, 128.0, A.add)
-    for k in range(3):
-        act(a("inttab", k, 3 * C, 3), a("base4", 0, C), F.Identity, float(k), 1.0)
-    sc(a("inttab", 3 * C, 960), a("base4", C, 384))
-    ms(a("ntab", 1536, 1540), NOWHERE)
     ts(a("c0"), a("r16b"), 0.0, A.not_equal)
     ts(a("c1"), a("r16b"), 1.0, A.is_equal, BIG, A.mult)
-    ts(a("col", 4, 5), a("r16b", 0, 1), 1.0, A.is_equal)
+    ts(c_last, a("r16b", 0, 1), 1.0, A.is_equal)
+    ts(c_rest, a("r16b", 0, 1), 1.0, A.not_equal)
     ts(a("coli", 1, 2), a("coli", 0, 1), 15, A.bitwise_and)
     tt(a("cm", 0, 16), a("c0"), a("c1"), A.max)
-    ts(s_num, a("col", 4, 5), 1.0, A.mult, 1.0 / BIG, A.add)
-    ts(s_thr, a("col", 4, 5), -BIG / 2, A.mult, BIG / 2, A.add)
-    cp(s_pm, a("coli", 1, 2))
-    ts(s_hi, s_num, 1.0 / 4096, A.mult)
-    for lo, n in ((16, 16), (32, 32), (64, 64), (128, 128), (256, 32), (288, 288), (576, 576)):
+    ts(c_inv, c_last, 1.0, A.mult, 1.0 / BIG, A.add)
+    ts(c_big, c_rest, BIG, A.mult, 1.0, A.add)
+    cp(c_pm, a("coli", 1, 2))
+    ts(c_own, c_inv, c_inv, A.mult, -4.0, A.mult)
+    for o, x, c in ((c_col, c_inv, 0.2), (c_step, c_inv, 1.0 / 4096), (c_y, c_big, 4097.0), (c_round, c_big, 1.5 * 2 ** 35),
+                    (c_thr, c_big, 4096.0), (c_mid, c_big, 1024.0)):
+        ts(o, x, c, A.mult)
+    for lo, n in ((16, 16), (32, 32), (64, 64), (128, 128), (256, 32), (288, 288)):
         cp(a("cm", lo, lo + n), a("cm", 0, n))
+    for name, c in (("nf", NOWHERE), ("inf", NOWHERE), ("pf", 0.0), ("sg", 0.0)):
+        ms(a(name, C, 384), c)
+    ms(a("f0"), 0.0)
+    ms(a("h0"), 0.0)
+    ms(a("turn", NONE, NONE + 8), 2047.0)
     cp(a("eb", 3, 515, 4), a("ident"))
     for b in range(4):
-        quant(a("eq", 128 * b, 128 * b + 128), a("es", 128 * b, 128 * b + 128), a("eb", 3 - b, 515 - b))
+        quant(tile_e(b)[0], tile_e(b)[1], a("eb", 3 - b, 515 - b))
     cp(a("tw16", 0, 60), a("twb", 0, 60))
     cp(a("uoff"), a("uoi"))
-    ts(a("vw"), a("c16"), s_pm, A.add)
+    ts(a("vw"), a("c16"), c_pm, A.add)
     sc(a("tfn", 192, 960), ind(a("inttab"), a("tw16", 12, 60)))
     cp(a("tfn", 0, 192), ind(a("inttab"), a("tw16", 0, 12)))
     quant(a("uq"), a("us"), a("ub"))
     pick_u(0, 128)
-    signs(0)
+    state(0, 0)
+    state(0, 1)
     for k in range(3):
         scan(a("so", C * k, C * k + C), a("tfn", k, 3 * C, 3))
     scan(a("so", 3 * C, 960), a("tfn", 3 * C, 960))
-    ts(a("lb"), a("so", 15, 960, 16), s_num, A.mult)
-    ts(a("tb", 0, 54), a("so", 15, 864, 16), s_num, A.mult)
-    ts(a("tb", 54, 90), a("so", 15, 576, 16), s_num, A.mult)
-    column(a("e54"), a("lb", 0, 54))
+    ts(a("tb"), ends("so", 0, 60), c_inv, A.mult)
+    column(a("e54"), ends("so", 0, 54))
     for k in range(3):
-        act(a("hb", 18 * k, 18 * k + 18), a("vw"), F.Identity, float(k), 4.0)
+        act(a("lab", 18 * k, 18 * k + 18), a("vw"), float(k), 5.0)
+        act(a("v5", 18 * k, 18 * k + 18), a("vw"), 0.0, 5.0)
+        ms(a("kap", 18 * k, 18 * k + 18), float(k))
     keys()
-    for k in range(4):
-        act(a("ntab", k, 1536, 4), a("base4"), F.Identity, 4096.0 * ((k + 1) % 3), 4096.0)
-    act(a("two", 0, 2 * C, 2), a("base4", 0, C), F.Identity, -1e29, 0.0)
-    act(a("two", 1, 2 * C, 2), a("base4", 0, C), F.Identity, 0.0, 0.0)
-    for k, c in enumerate((0.0, 4.0, 2.0)):
-        act(a("hc", 18 * k, 18 * k + 18), a("vw"), F.Identity, c, 0.0)
+    for k, c in enumerate((2.0, 0.0, 1.0, 2.0, 0.0)):
+        act(a("turn", k, NONE, 5), a("base"), c, 1.0)
+    act(a("two", 0, 2 * C, 2), a("base", 0, C), -1e29, 0.0)
+    act(a("two", 1, 2 * C, 2), a("base", 0, C), 0.0, 0.0)
     pick_u(128, 256)
     pick_u(256, 384)
     quant(a("vq"), a("vs"), a("vb"))
@@ -385,108 +431,108 @@ def rank_program(g, core, T, topo):
         big = send([(nxt, "all", fp, u8, T[lq][:, C:2 * C].bitcast(dt.uint8))], [qx])
         send([(nxt, "low", fp, sx[0], T[ls][:, C:2 * C]), (prv, "high", fn, sx[0], T[ls][:, 0:C])], [sx])
         send([(prv, "all", fn, u8, T[lq][:, 0:C].bitcast(dt.uint8))], [qx])
-        if t == 0:
-            iota(a("itab", 768, 1540), [[1, 772]], 768, 0, True)
 
-        def unpack(b, bk, q_, s_, pre=(), after=()):
-            mm(bank(bk), a("eq", 128 * b, 128 * b + 128), a("es", 128 * b, 128 * b + 128), q_, s_, pre, after)
-
-        pos = a("bits", 864, 1248)
-        sc(a("bits", 448, 864), ind(pos, a("e54", 28, 54)))
-        cp(a("bits", 0, 448), ind(pos, a("e54", 0, 28)))
+        sc(a("bits", 16 * SPLIT, 864), ind(a("sg"), a("e54", SPLIT, 54)))
+        cp(a("bits", 0, 16 * SPLIT), ind(a("sg"), a("e54", 0, SPLIT)))
+        scan(a("sbo"), a("sg", 0, C))
+        ts(a("own"), ends("sbo", 0, 18), c_own, A.mult)
+        scan(a("sb", 0, 16 * SPLIT), a("bits", 0, 16 * SPLIT))
+        scan(a("sb", 16 * SPLIT, 864), a("bits", 16 * SPLIT, 864))
         for b in range(4):
-            unpack(b, b, qx, sx)
-            sc(a("dw", 384 * b, 384 * b + C), bank(b))
+            mm(bank(4 + b), tile_e(b)[0], tile_e(b)[1], qx, sx)
+            act(a("dw", 384 * b, 384 * b + C), bank(4 + b), 0.0, 0.015625)
+            sc(a("du", C * b, C * b + C), bank(4 + b))
         for h in (1, 0):
             for b in range(4):
-                unpack(b, 4 + b, a(lq, C * h, C * h + C), a(ls, C * h, C * h + C),
-                       [(fp, from_prv) if h else (fn, from_nxt)] if b == 0 else (), [(big, LAG_A if h else LAG_B)])
-                sc(a("dn", 576 * b + C * h, 576 * b + C * h + C), bank(4 + b))
-        scan(a("sb"), a("bits", 0, 1152))
-        ts(a("pw"), a("sb", 15, 1152, 16), s_thr, A.is_gt)
+                bk = bank(b + 4 * (1 - h))
+                mm(bk, tile_e(b)[0], tile_e(b)[1], a(lq, C * h, C * h + C), a(ls, C * h, C * h + C),
+                   [(fp, from_prv) if h else (fn, from_nxt)] if b == 0 else (),
+                   [(big, (LAG_A if h else LAG_B) + (LAG_1 if t == 0 else 0))])
+                act(a("dn", 576 * b + C * h, 576 * b + C * h + C), bk, 0.0, 0.015625)
+        for h in range(2):
+            for b in range(4):
+                mm(bank(4 * h + b, H), tile_e(b)[0], tile_e(b)[1], half("qx%d" % t, h), half("sx%d" % t, h), stop=False)
         for k in range(3):
-            tt(a("w", 18 * k, 18 * k + 18), a("pw", 18 * k, 18 * k + 18), a("pw", 54, 72), A.not_equal)
-        for s_ in range(4):
-            tt(a("key", s_, 216, 4), a("w"), a("kk", 54 * s_, 54 * s_ + 54), A.mult)
-        tt(a("k1"), a("key", 0, 72), a("key", 72, 144), A.max)
-        tt(a("k2"), a("key", 144, 216), a("dfl"), A.max)
-        tt(a("best"), a("k1"), a("k2"), A.max)
-        ts(a("idx"), a("best", 0, 72, 4), 4095, A.bitwise_and)
+            tt(a("w", 18 * k, 18 * k + 18), ends("sb", 18 * k, 18 * k + 18), a("own"), A.mult)
         for s_ in range(3):
-            ts(a("lb", 18 * s_, 18 * s_ + 18), a("best", s_, 72, 4), 2047, A.bitwise_and)
-        ts(a("offn"), a("idx"), float(NONE), A.min)
-        cp(a("offp"), a("lb", 18, 36))
-        column(a("e2", 0, 18), a("lb", 0, 18))
-        sc(a("nf", 0, C), ind(a("ntab"), a("offn")))
-        cp(a("af"), ind(a("itab"), a("offn")))
-        sc(a("pf", 0, C), ind(a("itab"), a("offp")))
+            tt(a("key", s_, 162, 3), a("w"), a("kk", 54 * s_, 54 * s_ + 54), A.mult)
+        tt(a("k1"), a("key", 0, 54), a("key", 54, 108), A.max)
+        tt(a("k2"), a("key", 108, 162), a("dfl"), A.max)
+        tt(a("best"), a("k1"), a("k2"), A.max)
+        ts(a("idx"), a("best", 0, 54, 3), 4095, A.bitwise_and)
+        ts(a("lb", 0, 18), a("best", 0, 54, 3), 2047, A.bitwise_and)
+        for s_ in (1, 2):
+            ts(a("lb", 18 * s_, 18 * s_ + 18), a("best", s_, 54, 3), 2, A.logical_shift_right, 2047, A.bitwise_and)
+            ts(a("ki", 18 * s_ - 18, 18 * s_), a("best", s_, 54, 3), 3, A.bitwise_and)
+        ts(a("offn"), a("idx"), float(NONE), A.min, 2.0, A.add)
+        cp(a("offa"), a("lb", 0, 18))
+        ts(a("offp"), a("lb", 18, 36), 1.0, A.add)
+        ts(a("e2", 0, 18), a("lb", 0, 18), 0.2, A.mult, -0.2, A.add)
+        act(a("nf", 0, C), ind(a("turn"), a("offn")), 0.0, 4096.0)
+        cp(a("af"), ind(a("turn"), a("offa")))
+        sc(a("pf", 0, C), ind(a("turn"), a("offp")))
         tt(a("inf", 0, C), ind(a("nf"), a("e2", 0, 18)), a("af"), A.add)
-        sc(a("zf", C, 384), ind(a("inf"), a("esl")))
-        tt(a("zf", 0, C), ind(a("pf"), a("e2", 0, 18)), a("inf", 0, C), A.add)
+        cp(a("gf", 864, 960), ind(a("inf"), a("esl")))
+        sc(a("bo"), ind(a("pf"), a("e2", 0, 18)))
         sc(a("gf", 0, C), ind(a("inf"), a("e2", 0, 18)))
-        ts(a("xz"), a("best", 3, 72, 4), 3, A.bitwise_and)
-        ts(a("hs", 0, 18), a("best", 3, 72, 4), 2047, A.bitwise_and)
-        ts(a("th", 0, 18), a("xz"), -3.0, A.mult, -3.0, A.min)
-        tt(a("hs", 18, 36), a("hs", 0, 18), a("th", 0, 18), A.add)
+        cp(a("kap", 18, 54), a("ki"))
+        tt(a("ks"), a("ki", 0, 18), a("ki", 18, 36), A.add)
+        ts(a("kap", 0, 18), a("ks"), -1.0, A.mult, 3.0, A.add)
+        tt(a("lab", 18, 36), a("ki", 0, 18), a("v5", 0, 18), A.add)
         if more:
-            ts(a("th", 18, 36), a("xz"), -3.0, A.mult, -3.0, A.max)
-            tt(a("hs", 36, 54), a("hs", 0, 18), a("th", 18, 36), A.add)
-            tt(a("hb"), a("hs"), a("hc"), A.add)
-        ts(a("kb", 0, 18), a("hs", 18, 36), 4.0, A.add)
-        ts(a("kb", 18, 36), a("hs", 18, 36), 4.0, A.add)
-        ts(a("aq", 18, 36), a("hs", 18, 36), 4.0, A.add, 4096.0, A.mult)
-        tt(a("aq", 0, 18), a("lb", 36, 54), a("lb", 0, 18), A.add)
-        tt(a("uu", 0, 18), a("aq", 0, 18), a("aq", 18, 36), A.add)
-        tt(even("f1", 18, 36), a("lb", 36, 54), a("lb", 18, 36), A.subtract)
-        cp(odd("f1", 0, 60), a("lb"))
-        scan(a("so", 0, 384), a("zf"))
-        ts(a("ib", 36, 60), a("so", 15, 384, 16), s_num, A.mult)
-        ts(a("xb", 36, 60), a("so", 15, 384, 16), s_hi, A.mult, -0.49, A.add)
-        ts(a("xb", 18, 36), a("so", 15, C, 16), s_hi, A.mult, -0.49, A.add)
-        tt(odd("f0", 18, 60), a("xb", 18, 60), a("kb"), A.is_equal)
-        tt(even("f1", 36, 60), a("ib", 36, 60), a("uu"), A.subtract)
-        scan(a("fo", 36, 120), a("f1", 36, 120), a("f0", 36, 120))
+            tt(a("lab", 0, 18), a("kap", 0, 18), a("v5", 0, 18), A.add)
+            tt(a("lab", 36, 54), a("ki", 18, 36), a("v5", 0, 18), A.add)
+        ts(a("thr"), a("lab", 18, 36), c_thr, A.mult, c_mid, A.add)
+        ts(odd("f1", 0, 18), a("lb", 0, 18), c_big, A.mult)
+        ts(a("yy", 0, 18), a("lb", 0, 18), c_y, A.mult)
+        ts(odd("h1", 0, 36), a("lb", 18, 54), c_big, A.mult)
+        tt(even("h1", 0, 18), odd("h1", 18, 36), odd("h1", 0, 18), A.subtract)
+
+        def moved(lo, hi):
+            tt(even("f1", lo, hi), ends("so", lo, hi), a("yy", lo, hi), A.subtract)
+            near(odd("f0", lo, hi), even("f1", lo, hi))
+            scan(a("fo", 2 * lo, 2 * hi), a("f1", 2 * lo, 2 * hi), a("f0", 2 * lo, 2 * hi))
+
+        scan(a("so", 864, 960), a("gf", 864, 960))
+        moved(54, 60)
         ea, eb_ = a("esend", 8 * t, 8 * t + 3), a("esend", 8 * t + 4, 8 * t + 7)
-        column(ea, odd("fo", 54, 57), 4.0 * C)
+        column(ea, odd("fo", 54, 57), float(C))
         column(eb_, odd("fo", 57, 60))
         small = send([(nxt, "low", lst, ea[0], T[lst][:, 3:6]), (prv, "high", lst, eb_[0], T[lst][:, 0:3])], [ea, eb_])
         if t == 0:
-            iota(a("otab", 0, 4 * C), [[3, C], [1, 4]], 0, 0, True)
-            iota(a("otab", 4 * C, 1536), [[1, 2 * S], [0, 4]], 3 * C, 0, True)
-        column(a("e2", 18, 54), odd("fo", 18, 54))
-        cp(a("lb", 18, 54), odd("fo", 18, 54))
-        cp(odd("f1", 18, 54), odd("fo", 18, 54))
-        ts(a("u2"), a("lb", 0, 54), 4097.0, A.mult)
+            iota(a("otab", 0, 5 * C), [[3, C], [1, 5]], 0, 0, True)
+            iota(a("otab", 5 * C, NONE), [[1, 2 * S], [0, 5]], 3 * C, 0, True)
+        scan(a("si"), a("inf", 0, C))
+        scan(a("sp"), a("bo"))
+        tt(a("zf"), ends("si", 0, 18), a("thr"), A.subtract)
+        tt(even("h1", 18, 36), ends("sp", 0, 18), odd("h1", 18, 36), A.subtract)
+        near(odd("h0", 0, 18), a("zf"))
+        near(odd("h0", 18, 36), a("zf"))
+        scan(a("ho"), a("h1"), a("h0"))
+        column(a("e2", 18, 54), odd("ho", 0, 36))
+        ts(a("yy", 18, 54), odd("ho", 0, 36), 4097.0, A.mult)
+        cp(odd("f1", 18, 54), odd("ho", 0, 36))
         sc(a("gf", 2 * C, 3 * C), ind(a("inf"), a("e2", 36, 54)))
         cp(a("gf", C, 2 * C), ind(a("inf"), a("e2", 18, 36)))
-        scan(a("so", 0, 864), a("gf"))
-        ts(a("ib", 0, 54), a("so", 15, 864, 16), s_num, A.mult)
-        ts(a("xb", 0, 54), a("so", 15, 864, 16), s_hi, A.mult, -0.49, A.add)
-        tt(even("f1", 0, 54), a("ib", 0, 54), a("u2"), A.subtract)
-        tt(odd("f0", 0, 54), a("xb", 0, 54), a("lb", 0, 54), A.is_equal)
-        scan(a("fo", 0, 108), a("f1", 0, 108), a("f0", 0, 108))
+        for k in range(3):
+            scan(a("so", C * k, C * k + C), a("gf", C * k, C * k + C))
+        moved(0, 54)
         column(a("e54"), odd("fo", 0, 54))
-        cp(a("lb"), odd("fo", 0, 60))
-        ts(a("t1"), a("lb"), 3, A.bitwise_and)
-        ts(a("t2"), a("t1"), 0.0, A.is_equal, 3.0, A.mult)
-        ts(a("t3"), a("t2"), -1.0, A.add)
-        tt(a("t4"), a("lb"), a("t3"), A.add)
-        tt(a("t5"), a("t4"), a("xb"), A.is_equal)
-        tt(a("t6"), a("t5"), odd("f0", 0, 60), A.max)
-        tt(a("t7"), a("t6"), a("t3"), A.mult)
-        tt(a("tb", 0, 54), a("lb", 0, 54), a("t7", 0, 54), A.add)
-        tt(a("tb", 54, 90), a("lb", 0, 36), a("t7", 0, 36), A.add)
-        tt(a("lb", 54, 60), a("lb", 54, 60), a("t7", 54, 60), A.add)
+        ts(a("nd"), even("f1", 0, 60), c_step, A.mult)
+        ts(a("e1"), a("nd"), -1.0, A.is_equal, -1.0, A.mult)
+        ts(a("e2f"), a("nd"), 2.0, A.is_equal, 2.0, A.mult)
+        act(a("val"), odd("fo", 0, 60), 0.0, c_inv)
+        tt(a("cor"), a("e1"), a("e2f"), A.add)
+        tt(a("tb"), a("val"), a("cor"), A.add)
         if more:
             keys()
         else:
-            for j in range(3):
-                ts(a("wp", 18 * j, 18 * j + 18), a("xz"), float((3 - j) % 3), A.is_equal, 4096.0, A.mult)
             for s_ in range(3):
-                tt(a("key", s_, 162, 3), a("wp"), a("tb", 18 * s_, 18 * s_ + 54), A.add)
-            cp(a("oto", 54, 60), a("lb", 54, 60))
-            tt(a("k1", 0, 54), a("key", 0, 54), a("key", 54, 108), A.max)
-            tt(a("k2", 0, 54), a("k1", 0, 54), a("key", 108, 162), A.max)
+                ts(a("kk", 54 * s_, 54 * s_ + 54), a("kap"), float(s_), A.is_equal, 4096.0, A.mult)
+                tt(a("key", s_, 162, 3), a("kk", 54 * s_, 54 * s_ + 54), a("tb", 0, 54), A.add)
+            cp(a("oto", 54, 60), a("tb", 54, 60))
+            tt(a("k1"), a("key", 0, 54), a("key", 54, 108), A.max)
+            tt(a("k2"), a("k1"), a("key", 108, 162), A.max)
             for s_ in range(3):
                 ts(a("oto", 18 * s_, 18 * s_ + 18), a("k2", s_, 54, 3), -4096.0, A.add)
                 sc(a("otf", s_, 3 * C, 3), ind(a("otab"), a("oto", 18 * s_, 18 * s_ + 18)))
@@ -496,38 +542,45 @@ def rank_program(g, core, T, topo):
         def plane(b):
             return a("dw", 384 * b, 384 * b + 384)
 
-        gate = [(small, LAG_L)]
+        def third(k):
+            return a("e54", 18 * k, 18 * k + 18)
+
+        gate = {q: [(small, LAG_L)] for q in "vs"}
         for b in range(4):
-            i = sc(a("dw", 384 * b + C, 384 * b + 384), ind(a("dn", 576 * b, 576 * b + 576), a(lst, 0, 6)),
-                   [(lst, lists_in)] if b == 0 else (), gate)
-            gate = [(i, 0)]
-        cp(a("g0", 0, C), ind(plane(0), a("e54", 0, 18)))
-        sc(a("g0", C, 2 * C), ind(plane(1), a("e54", 0, 18)))
-        for b in (0, 1):
-            tt(a("g1", C * b, C * b + C), ind(plane(b), a("e54", 18, 36)), a("g0", C * b, C * b + C), A.max)
-            tt(a("mt", b, 4 * C, 4), ind(plane(b), a("e54", 36, 54)), a("g1", C * b, C * b + C), A.max)
-        for b in (2, 3):
-            lo, hi = 2 * C * (b - 2), 2 * C * (b - 1)
-            for k in range(2):
-                sc(a("gi", lo + k, hi, 2), ind(plane(b), a("e54", 18 * k, 18 * k + 18)))
-            scan(a("go", lo, hi), a("gi", lo, hi), a("two"), A.add, A.max)
-            tt(a("mt", b, 4 * C, 4), ind(plane(b), a("e54", 36, 54)), a("go", lo + 1, hi, 2), A.max)
-        quant(a("mq"), a("ms"), a("mt"))
+            q = BORDER[b]
+            i = (cp if q == "v" else sc)(a("dw", 384 * b + C, 384 * b + 384), ind(a("dn", 576 * b, 576 * b + 576), a(lst, 0, 6)),
+                                         [(lst, lists_in)] if BORDER.index(q) == b else (), gate[q])
+            gate[q] = [(i, 0)]
         for b in range(4):
-            mm(bank(4 + b), a("wq", 128 * b, 128 * b + 128), a("wsc", 128 * b, 128 * b + 128), a("mq"), a("ms"))
-            act(a("rl", C * b, C * b + C), bank(4 + b), F.Relu, 0.0, 0.015625)
-            tt(a("xt", b, 4 * C, 4), bank(b), a("rl", C * b, C * b + C), A.add)
-        if more:
-            signs(t + 1)
-        else:
-            quant(a("qx%d" % R), a("sx%d" % R), a("xt"))
+            g0, g1 = a("g0", C * b, C * b + C), a("g1", C * b, C * b + C)
+            if WAYS[b] < 3:
+                (cp if WAYS[b] == 1 else sc)(g0, ind(plane(b), third(0)))
+                tt(g1, ind(plane(b), third(1)), g0, A.max)
+            else:
+                lo, hi = 2 * C * b, 2 * C * b + 2 * C
+                for k in range(2):
+                    sc(a("gi", lo + k, hi, 2), ind(plane(b), third(k)))
+                scan(a("go", lo, hi), a("gi", lo, hi), a("two"), A.add, A.max)
+                g1 = a("go", lo + 1, hi, 2)
+            tt(a("mt", b, 4 * C, 4), ind(plane(b), third(2)), g1, A.max)
+        for h in range(2):
+            quant(half("mq", h), half("ms", h), a("mt", 4 * H * h, 4 * H * h + 4 * H))
+            for b in range(4):
+                mm(bank(4 * h + b, H), a("wq", 128 * b, 128 * b + 128), a("wsc", 128 * b, 128 * b + 128),
+                   half("mq", h), half("ms", h), start=False)
+        for h in range(2):
+            for b in range(4):
+                tt(a("xt", 4 * H * h + b, 4 * H * h + 4 * H, 4), bank(4 * h + b, H),
+                   a("du", C * b + H * h, C * b + H * h + H), A.max)
+        state(t + 1, 0)
+        state(t + 1, 1)
 
     qx, sx = a("qx%d" % R), a("sx%d" % R)
-    mm(bank(4), a("vq"), a("vs"), qx, sx)
+    sc(half("yb", 0), bank(0, H))
+    cp(half("yb", 1), bank(1, H))
     dma("y", T.oc[:], qx[0].bitcast(dt.uint8), rd=[qx])
+    dma("s", T.y[:], T.yb[:], rd=[a("yb")])
     for k in range(4):
-        dma("y" if k < 2 else "s", T.osc[4 * k:4 * k + 4, :], T["sx%d" % R][32 * k:32 * k + 4, :], rd=[sx])
-    cp(a("yb"), bank(4))
-    dma("y", T.y[:], T.yb[:], rd=[a("yb")])
+        dma("y", T.osc[4 * k:4 * k + 4, :], T["sx%d" % R][32 * k:32 * k + 4, :], rd=[sx])
     emit(g, T, order(ops))
     g.wait_ge(T.sem.sent, sent[0])

@@ -1,32 +1,37 @@
+import math
+import numpy as np
 from concourse.bass import DstId, RemoteDMATransfer
 from concourse.mybir import dt, AluOpType, ActivationFunctionType
 
 C, S, R = 288, 48, 3
-H = C // 2
+CUT = (0, 160, C)
+PARTS = ((0, 160), (160, C))
+WAYS = ((3, 3, 2, 2), (3, 3, 3, 3))
 FP8 = "float8_e4m3fn_x4"
 BIG = float(2 ** 50)
 NONE = 1920
 NOWHERE = 2047 * 4096.0
-SPLIT = 22
-BORDER = "vsvs"
-WAYS = (3, 3, 2, 2)
-WAKE, TOL, LAG_A, LAG_B, LAG_L, LAG_1 = 200, 60, 4500, 6500, 2500, 1500
+SPLIT = 20
+TFN = ((0, 20), (20, 40), (40, 60))
+TURNS = 3
+WAKE, LAG_A, LAG_B, LAG_L, LAG_1 = 200, 4500, 6500, 1600, 1500
+PASSES, HEAT, SOFT, JUMP, LEAN, EARLY, SEED, PLAN = 60000, 20.0, 0.3, 0.6, 400.0, 9000, 1, {}
 
 SCRATCH = {"ps": ("psum", [128, 4096], "float32")}
 for _d, _bufs in (
-    ("bfloat16", {"xin": 4 * C, "xt": 4 * C, "mt": 4 * C, "ub": 512, "vb": 512, "eb": 520, "ones": 384, "five": 384,
-                  "ident": 128, "cm": 576, "sb": 864, "sbo": C, "sg": 384, "bits": 864, "dw": 4 * 384, "du": 4 * C,
+    ("bfloat16", {"xin": 4 * C, "xt": 4 * C, "mt": 4 * C, "ub": 512, "vb": 512, "eb": 520, "ones": 128,
+                  "cm": 576, "sb": 864, "sbo": C, "sg": 384, "bits": 864, "dw": 4 * 384, "du": 4 * C,
                   "dn": 4 * 576, "g0": 4 * C, "g1": 4 * C, "gi": 8 * C, "go": 8 * C, "two": 2 * C}),
-    ("float32", {"c0": 16, "c1": 16, "col": 12, "vw": 18, "base": 384, "inttab": 960, "turn": 1928, "otab": 1920,
-                 "tfn": 960, "otf": 960, "so": 960, "si": C, "sp": C, "own": 18, "w": 54, "pr": 54, "lab": 54, "v5": 54,
-                 "kap": 54, "af": C, "nf": 384, "pf": 384, "inf": 384, "bo": C, "gf": 960, "yb": C, "kk": 162,
-                 "dfl": 54, "f0": 120, "f1": 120, "fo": 120, "h0": 72, "h1": 72, "ho": 72, "yy": 60, "tb": 60,
-                 "t4": 54, "tk": 90, "low": 54, "thr": 18, "zf": 18, "e1": 60, "e2f": 60, "cor": 60, "val": 60,
-                 "ks": 18}),
+    ("float32", {"c0": 16, "c1": 16, "col": 16, "vw": 18, "base": 384, "inttab": 960, "turn": 1928, "otab": 1920,
+                 "tfn": 960, "otf": 960, "so": 960, "sp": C, "own": 18, "w": 54, "pr": 54, "lab": 54, "v5": 54,
+                 "af": C, "nf": 384, "pf": 384, "inf": 384, "bo": C, "gf": 960, "yb": C, "kk": 162, "ko": 54,
+                 "kq": 72, "four": 72, "dfl": 36, "f0": 216, "f1": 216, "fo": 216, "h0": 36, "h1": 36, "ho": 36,
+                 "s0": 30, "s1": 30, "sn": 30, "yy": 54, "ys": 96, "tb": 60, "t4": 54, "tk": 90, "low": 54, "fa": 36,
+                 "ks": 18, "dd": 36}),
     ("int32", {"twb": 64, "r16": 16, "r16b": 16, "coli": 8, "c16": 18, "uoi": 24, "key": 162, "k1": 54, "k2": 54,
-               "best": 54, "lb": 54, "idx": 18, "nd": 60, "ki": 36}),
-    ("uint16", {"tw16": 64, "uoff": 24, "offn": 18, "offa": 18, "offp": 18, "e2": 54, "e54": 54, "esl": 6, "oto": 60,
-                "esend": 24}),
+               "best": 36, "bq": 72, "lb": 54, "idx": 18, "kap": 54}),
+    ("uint16", {"tw16": 64, "uoff": 24, "offn": 18, "offa": 18, "offp": 18, "e2": 54, "e54": 54, "eg": 54, "esl": 6,
+                "osl": 6, "oto": 60, "esend": 24}),
     (FP8, {"wq": 512, "uq": 128, "uq2": 384, "vq": 128, "eq": 512, "mq": C}),
     ("uint8", {"wsc": 512, "us": 128, "us2": 384, "vs": 128, "es": 512, "ms": C}),
 ):
@@ -77,49 +82,147 @@ def clashes(ops):
 
 def order(ops):
     n = len(ops)
-    dep = []
-    last = {}
+    dep, back, last = [], [[] for _ in ops], {}
     must = clashes(ops)
     for i, x in enumerate(ops):
-        d = [(j, ops[j]["cost"] + ops[j]["lat"] + WAKE) for j in must[i]]
-        d += x["after"]
+        d = {j: ops[j]["lat"] + WAKE for j in must[i]}
+        for j, w in x["after"]:
+            d[j] = max(d.get(j, 0), w)
         if x["q"] in "tgy":
             if x["q"] in last:
-                d.append((last[x["q"]], 0))
+                d.setdefault(last[x["q"]], 0)
             last[x["q"]] = i
-        dep.append(d)
-    rest = [o["cost"] + o["lat"] for o in ops]
+        reach = set()
+        for j in d:
+            reach.update(k for k, w in dep[j] if d.get(k, 0) <= WAKE)
+        dep.append([(j, d[j]) for j in d if j not in reach])
+        for j, w in dep[i]:
+            back[j].append((i, w))
+    lat = [o["lat"] for o in ops]
+    ways = [sorted((q, o["ways"][q][1]) for q in o["ways"]) for o in ops]
+    cost = [dict(w) for w in ways]
+    lean = [o.get("lean", LEAN) for o in ops]
+
+    def place(key, edges, users, soonest, ways):
+        end, queue, busy = [0] * n, [None] * n, {q: [] for q in "vstgy"}
+        left = [len(e) for e in edges]
+        ready = [i for i in range(n) if left[i] == 0]
+        while ready:
+            i = min(ready, key=lambda z: key[z])
+            ready.remove(i)
+            soon = max([soonest[i]] + [end[j] + w for j, w in edges[i]])
+            pick = None
+            for q, c in ways[i]:
+                line, at = busy[q], soon
+                k = len(line)
+                while k and line[k - 1][1] > at:
+                    k -= 1
+                while k < len(line) and line[k][0] < at + c:
+                    at = max(at, line[k][1])
+                    k += 1
+                if pick is None or at + c + lean[i] < pick[0]:
+                    pick = (at + c, at, q, k)
+            busy[pick[2]].insert(pick[3], (pick[1], pick[0]))
+            end[i], queue[i] = pick[0], (pick[2], pick[0] - pick[1])
+            for j, w in users[i]:
+                left[j] -= 1
+                if left[j] == 0:
+                    ready.append(j)
+        return end, queue
+
+    def run(lines):
+        end, why, left, after, soon, took = [0] * n, [None] * n, [len(e) for e in dep], [None] * n, [0] * n, [0] * n
+        for q in lines:
+            line = lines[q]
+            for k in range(len(line)):
+                took[line[k]] = cost[line[k]][q]
+                if k:
+                    after[line[k - 1]] = line[k]
+                    left[line[k]] += 1
+        ready, done = [i for i in range(n) if left[i] == 0], 0
+        while ready:
+            i = ready.pop()
+            done += 1
+            e = end[i] = soon[i] + took[i]
+            for j, w in back[i]:
+                if e + w > soon[j]:
+                    soon[j], why[j] = e + w, i
+                left[j] -= 1
+                if not left[j]:
+                    ready.append(j)
+            j = after[i]
+            if j is not None:
+                if e > soon[j]:
+                    soon[j], why[j] = e, -1 - i
+                left[j] -= 1
+                if not left[j]:
+                    ready.append(j)
+        return (end, why, soon) if done == n else None
+
+    key, best = [0] * n, None
     for i in range(n - 1, -1, -1):
-        for j, w in dep[i]:
-            rest[j] = max(rest[j], w + rest[i])
-    start, free, out = {}, {q: 0 for q in "vstgy"}, []
-    users, left, soon = [[] for _ in ops], [0] * n, [0] * n
-    for i in range(n):
-        for j, w in dep[i]:
-            users[j].append((i, w))
-            left[i] += 1
-    todo = [i for i in range(n) if left[i] == 0]
-    while todo:
-        ready = {}
-        for i in todo:
-            q = ops[i]["q"]
-            ready.setdefault(q, []).append((max(free[q], soon[i]), i))
-        picks = []
-        for q in ready:
-            top = max(ready[q], key=lambda z: (rest[z[1]], -z[1]))
-            fit = [z for z in ready[q] if z[0] + ops[z[1]]["cost"] <= top[0] + TOL and z[0] < top[0]]
-            picks.append(min(fit, key=lambda z: (z[0], -rest[z[1]])) if fit else top)
-        at, i = min(picks)
-        start[i] = at
-        free[ops[i]["q"]] = at + ops[i]["cost"]
-        todo.remove(i)
-        for j, w in users[i]:
-            soon[j] = max(soon[j], at + w)
-            left[j] -= 1
-            if left[j] == 0:
-                todo.append(j)
-        out.append(ops[i])
-    return out
+        key[i] = min([-lat[i]] + [key[j] - w for j, w in back[i]]) - ways[i][0][1]
+    for turn in range(4):
+        end, queue = place(key, dep, back, [0] * n, ways)
+        late = place([-e for e in end], back, dep, lat, [[x] for x in queue])[0]
+        key = [-late[i] - ops[i].get("early", 0) for i in range(n)]
+        if turn == 1 or (turn > 1 and max(end) < best[0]):
+            best = (max(end), end, queue)
+    lines = {q: [i for i in sorted(range(n), key=lambda z: best[1][z]) if best[2][i][0] == q] for q in "vstgy"}
+    tails = [i for i in range(n) if not back[i]]
+    rng, now, top, trial = np.random.RandomState(SEED), None, None, lines
+    for turn in range(PASSES):
+        got = run(trial)
+        if got:
+            end, why, soon = got
+            i = max(tails, key=lambda z: end[z] + lat[z])
+            total = end[i] + lat[i]
+            worth = total + SOFT * sum(end) / n
+            if now is None or worth <= now[0] - HEAT * (1 - turn / PASSES) * math.log(1 - rng.random_sample()):
+                held = []
+                while i is not None:
+                    j = why[i]
+                    if j is not None and j < 0:
+                        j = -1 - j
+                        if ops[i]["q"][0] not in "tgy":
+                            held.append((i, j))
+                    i = j
+                now = (worth, trial, held, soon, end)
+                if top is None or total < top[0]:
+                    top = (total, trial, end, soon)
+        trial = dict(now[1])
+        how = rng.randint(8)
+        if how < 6 and now[2]:
+            i, j = now[2][rng.randint(len(now[2]))]
+            x = (i, j)[how % 2]
+        else:
+            x = rng.randint(n)
+            if ops[x]["q"][0] in "tgy":
+                continue
+        q = "v" if x in now[1]["v"] else "s"
+        line = list(trial[q])
+        k = line.index(x)
+        del line[k]
+        trial[q] = line
+        if ops[x]["kind"] == "op" and rng.random_sample() < JUMP:
+            q = "sv"[rng.randint(2)] if len(cost[x]) > 1 else q
+            lo = max([0] + [now[4][z] + w for z, w in dep[x]])
+            hi = min([now[0]] + [now[3][z] - w for z, w in back[x]]) - cost[x][q]
+            line, at = list(trial[q]), lo + (hi - lo) * rng.random_sample() ** 2 + rng.normal(0.0, 100.0)
+            k = 0
+            while k < len(line) and now[3][line[k]] < at:
+                k += 1
+            trial[q] = line
+        else:
+            far = 1 + int(rng.exponential(2.0))
+            k = min(max(k - far if (how < 6 and x == i) or how == 6 else k + far, 0), len(line))
+        line.insert(k, x)
+    PLAN["total"] = top[0]
+    queue = [None] * n
+    for q in top[1]:
+        for i in top[1][q]:
+            queue[i] = q
+    return sorted(range(n), key=lambda i: (top[3][i], top[2][i])), queue
 
 
 def emit(g, T, ops):
@@ -153,7 +256,7 @@ def emit(g, T, ops):
     closure = []
     last = {q: [None] * POOL[q] for q in POOL}
     count = {q: [0] * POOL[q] for q in POOL}
-    tag, ndma, stores = {}, [0], []
+    tag, ndma, stores, arrived = {}, [0], [], set()
 
     def learn(k, j):
         for x in group[j]:
@@ -187,7 +290,9 @@ def emit(g, T, ops):
             for x in group[i]:
                 tag[x] = ("%s%d" % (q, s), count[q][s])
         for name, val in o["pre"]:
-            Q[q].wait_ge(T.sem[name], val)
+            if (q, name) not in arrived:
+                arrived.add((q, name))
+                Q[q].wait_ge(T.sem[name], val)
         for j in ws:
             Q[q].wait_ge(T.sem[tag[j][0]], tag[j][1])
         closure.append(set(k))
@@ -215,17 +320,20 @@ def rank_program(g, core, T, topo):
             return (ap, [("ps", lo // 512 * 512, lo // 512 * 512 + 512, 1)], hi - lo)
         return (ap, [(name, lo, hi, st)], len(range(lo, hi, st)))
 
-    def odd(name, lo, hi):
-        return a(name, 2 * lo + 1, 2 * hi, 2)
-
-    def even(name, lo, hi):
-        return a(name, 2 * lo, 2 * hi, 2)
-
     def ends(name, lo, hi):
         return a(name, 16 * lo + 15, 16 * hi, 16)
 
+    def step(buf, k, lo, hi, n=4):
+        return a(buf, n * lo + k, n * hi, n)
+
     def bank(b, n=C):
         return a("ps", 512 * b, 512 * b + n)
+
+    def half(name, h, at=0, n=1):
+        return a(name, at + n * CUT[h], at + n * CUT[h + 1])
+
+    def hbank(b, h):
+        return bank(b, CUT[h + 1] - CUT[h])
 
     def ind(win, off):
         return (win[0].indirect(off[0]), win[1] + off[1], -1)
@@ -240,8 +348,8 @@ def rank_program(g, core, T, topo):
         w = []
         for x in wr:
             w += x[1]
-        ops.append({"q": q, "fn": fn, "r": r, "w": w, "kind": kind, "pre": list(pre), "after": list(after),
-                    "cost": max(cost, 55), "lat": lat})
+        ops.append({"q": q, "ways": {q: (fn, max(cost, 55))}, "r": r, "w": w, "kind": kind, "pre": list(pre),
+                    "after": list(after), "lat": lat})
         return len(ops) - 1
 
     def val(x):
@@ -250,37 +358,42 @@ def rank_program(g, core, T, topo):
     def per(*xs):
         return 0.42 if all(SCRATCH[x[1][0][0]][2] == "bfloat16" for x in xs) else 0.83
 
+    def act(o, x, bias=0.0, scale=1.0, pre=(), after=(), only=None):
+        i = rec("s", lambda e: e.activation(o[0], x[0], F.Identity, bias=val(bias), scale=val(scale)), [x, bias, scale],
+                [o], 60 + o[2] * 0.83, pre=pre, after=after)
+        if only != "s":
+            plain = bias == 0.0 and scale == 1.0
+            fn = ((lambda e: e.tensor_copy(o[0], x[0])) if plain
+                  else (lambda e: e.tensor_scalar(o[0], x[0], val(scale), val(bias), A.mult, A.add)))
+            ops[i]["ways"]["v"] = (fn, 50 + 1.3 * o[2] if x[2] < 0 else max(55, o[2] * per(o, x)))
+            ops[i]["q"] = "e%d" % i
+        return i
+
     def tt(o, x, y, op):
         rec("v", lambda e: e.tensor_tensor(o[0], x[0], y[0], op), [x, y], [o], o[2] * (0.83 if x[1][0][0] == "ps" else 1.66))
 
     def ts(o, x, s1, op0, s2=None, op1=None):
         if op1 is None:
-            rec("v", lambda e: e.tensor_scalar(o[0], x[0], val(s1), None, op0), [x, s1], [o], o[2] * 0.83)
+            rec("v", lambda e: e.tensor_scalar(o[0], x[0], val(s1), None, op0), [x, s1], [o], o[2] * per(o, x))
         else:
-            rec("v", lambda e: e.tensor_scalar(o[0], x[0], val(s1), val(s2), op0, op1), [x, s1, s2], [o], o[2] * 0.83)
+            rec("v", lambda e: e.tensor_scalar(o[0], x[0], val(s1), val(s2), op0, op1), [x, s1, s2], [o], o[2] * per(o, x))
 
-    def cp(o, x, pre=(), after=()):
-        return rec("v", lambda e: e.tensor_copy(o[0], x[0]), [x], [o], o[2] * per(o, x), pre=pre, after=after)
+    def cp(o, x):
+        rec("v", lambda e: e.tensor_copy(o[0], x[0]), [x], [o], o[2] * per(o, x))
 
     def ms(o, c):
         rec("v", lambda e: e.memset(o[0], c), [], [o], o[2] * per(o))
 
-    def scan(o, x, m=None, op0=A.mult, op1=A.add, first=0.0):
+    def scan(o, x, m=None, op0=A.mult, op1=A.add):
         m = m or a("cm", 0, o[2])
-        rec("v", lambda e: e.tensor_tensor_scan(o[0], m[0], x[0], first, op0, op1), [m, x], [o], o[2] * per(o, x, m))
-
-    def sc(o, x, pre=(), after=()):
-        return rec("s", lambda e: e.activation(o[0], x[0], F.Copy), [x], [o], 60 + o[2] * 0.83, pre=pre, after=after)
-
-    def act(o, x, bias, scale, func=F.Identity):
-        rec("s", lambda e: e.activation(o[0], x[0], func, bias=bias, scale=val(scale)), [x, scale], [o], 60 + o[2] * 0.83)
+        rec("v", lambda e: e.tensor_tensor_scan(o[0], m[0], x[0], 0.0, op0, op1), [m, x], [o], o[2] * per(o, x, m))
 
     def quant(q, s, x):
         rec("v", lambda e: e.quantize_mx(q[0], s[0], x[0]), [x], [q, s], 12 + 0.22 * x[2])
 
     def mm(o, wq, wsc, xq, xs, pre=(), after=(), start=True, stop=True):
         rec("t", lambda e: e.matmul_mx(o[0], wq[0], wsc[0], xq[0], xs[0], start, stop), [wq, wsc, xq, xs], [o],
-            0.6 * o[2], pre=pre, after=after)
+            10 + 0.6 * o[2], pre=pre, after=after)
 
     def dma(q, o, x, rd=(), wr=(), lat=2000):
         rec(q, lambda e: e.dma_start(o, x), list(rd), list(wr), 100, kind="dma", lat=lat)
@@ -309,49 +422,56 @@ def rank_program(g, core, T, topo):
     from_nxt = len(part(nxt, core, "all")) + len(part(nxt, core, "high"))
     lists_in = len(part(prv, core, "low")) + len(part(nxt, core, "high"))
 
-    c_big, c_inv, c_own, c_col, c_y, c_round, c_step, c_thr, c_mid, c_pm, c_last, c_rest = [a("col", i, i + 1) for i in range(12)]
+    c_big, c_less, c_inv, c_half, c_own, c_col, c_y, c_pm, c_last, c_rest = [a("col", i, i + 1) for i in range(10)]
+    c_near = {k: a("col", 13 + k, 14 + k) for k in range(-2, 3)}
 
-    def column(o, x, shift=0.0):
-        ts(o, x, c_col, A.mult, shift - 0.2, A.add)
+    def column(o, x):
+        ts(o, x, 0.2, A.mult, -0.2, A.add)
 
-    def near(o, x):
-        ts(o, x, c_round, A.add, c_round, A.is_equal)
+    def near(o, z, k, op=A.is_equal):
+        ts(o, z, c_near[k], A.add, c_near[0], op)
+
+    def moved(m, x, lo, hi, z, n=4):
+        near(step(m, 1, lo, hi, n), z, 0)
+        near(step(x, 2, lo, hi, n), z, 2)
+        near(step(x, 3, lo, hi, n), z, -1, A.not_equal)
 
     def keys():
         tt(a("low"), a("lab"), a("tb", 0, 54), A.min)
-        ts(a("pr"), a("low"), -8192.0, A.mult, (5 * C + 1) * 8192.0, A.add)
+        act(a("pr"), a("low"), (5 * C + 1) * 8192.0, -8192.0)
         act(a("t4"), a("tb", 0, 54), 0.0, 4.0)
         tt(a("tk", 0, 54), a("t4"), a("kap"), A.add)
-        sc(a("tk", 54, 90), a("tk", 0, 36))
+        act(a("tk", 54, 90), a("tk", 0, 36))
         tt(a("kk", 0, 54), a("pr"), a("tb", 0, 54), A.add)
-        act(a("dfl", 0, 54, 3), a("tb", 0, 18), 2048.0, 1.0)
+        act(step("kq", 0, 0, 18), a("tb", 0, 18), 2048.0, 1.0)
         for s_ in (1, 2):
             tt(a("kk", 54 * s_, 54 * s_ + 54), a("pr"), a("tk", 18 * s_, 18 * s_ + 54), A.add)
-            sc(a("dfl", s_, 54, 3), a("tk", 18 * s_, 18 * s_ + 18))
-        ts(a("esl"), a("tb", 54, 60), 0.2, A.mult, -0.2, A.add)
-        act(odd("f1", 54, 60), a("tb", 54, 60), 0.0, c_big)
-        act(a("yy", 54, 60), a("tb", 54, 60), 0.0, c_y)
+            act(a("dfl", s_ - 1, 36, 2), a("tk", 18 * s_, 18 * s_ + 18))
+
+    def slots(x):
+        column(a("esl"), x)
+        ts(a("osl"), x, 1.0, A.add)
+        act(a("ys"), ind(a("turn"), a("osl")), 0.0, 4097.0)
+        act(step("s1", 1, 0, 6, 5), x, c_less, c_big)
 
     def pick_u(lo, hi):
         o = a("uoff", lo // 16, hi // 16)
         rec("v", lambda e: e.tensor_copy(T.uq2[:, lo:hi].bitcast(dt.uint32), T.uq[:, 0:128].bitcast(dt.uint32).indirect(o[0])),
             [a("uq"), o], [a("uq2", lo, hi)], 60 + 1.3 * (hi - lo))
-        sc(a("us2", lo, hi), ind(a("us"), o))
-
-    def half(name, h):
-        return a(name, H * h, H * h + H)
+        x = ind(a("us"), o)
+        rec("s", lambda e: e.activation(T.us2[:, lo:hi], x[0], F.Copy), [x], [a("us2", lo, hi)], 0)
 
     def tile_e(b):
         return a("eq", 128 * b, 128 * b + 128), a("es", 128 * b, 128 * b + 128)
 
     def state(t, h):
         q_, s_ = half("qx%d" % t, h), half("sx%d" % t, h)
-        quant(q_, s_, a("xt" if t else "xin", 4 * H * h, 4 * H * h + 4 * H))
+        quant(q_, s_, half("xt" if t else "xin", h, 0, 4))
         if t < R:
-            mm(bank(h, H), a("uq2", 128 * t, 128 * t + 128), a("us2", 128 * t, 128 * t + 128), q_, s_)
-            ts(half("sg", h), bank(h, H), 0.0, A.is_gt, 0.5, A.subtract)
+            mm(hbank(h, h), a("uq2", 128 * t, 128 * t + 128), a("us2", 128 * t, 128 * t + 128), q_, s_)
+            ts(half("sg", h), hbank(h, h), 0.0, A.is_gt, 0.5, A.subtract)
         else:
-            mm(bank(h, H), a("vq"), a("vs"), q_, s_)
+            mm(hbank(h, h), a("vq"), a("vs"), q_, s_)
 
     dma("y", T.twb[:, 0:60], T.tw[:], wr=[a("twb")], lat=1500)
     dma("s", T.ub[:], T.u[:], wr=[a("ub")], lat=2200)
@@ -359,18 +479,28 @@ def rank_program(g, core, T, topo):
     dma("y", T.wq[:].bitcast(dt.uint8), T.wc[:], rd=[a("xin")], wr=[a("wq")], lat=4000)
     dma("y", T.wsc[:], T.ws[:], wr=[a("wsc")], lat=4000)
     dma("y", T.vb[:], T.v[:], wr=[a("vb")], lat=4500)
+    first = len(ops)
     ms(a("ones"), 1.0)
-    ms(a("five"), 5.0)
+    ms(a("eb"), 0.0)
     iota(a("r16"), [[1, 16]], 128, -1)
+    iota(a("base"), [[5, 384]], 0, 0, True)
+    rec("g", lambda e: e.affine_select(T.eb[:, 3:515:4], T.ones[:], [[-1, 128]], A.is_equal, 0.0, 0, 1),
+        [a("ones")], [a("eb", 3, 515, 4)], 400)
+    for b in range(4):
+        quant(tile_e(b)[0], tile_e(b)[1], a("eb", 3 - b, 515 - b))
+    for o in ops[first:]:
+        o["early"] = EARLY
     iota(a("uoi"), [[1, 3], [16, 8]], 0, 0)
     iota(a("c16"), [[16, 18]], 0, 0)
-    rec("g", lambda e: e.affine_select(T.ident[:], T.ones[:, 0:128], [[-1, 128]], A.is_equal, 0.0, 0, 1),
-        [a("ones")], [a("ident")], 400)
-    scan(a("base"), a("five"), a("ones"), first=-5.0)
+    iota(a("kap"), [[1, 3], [0, 18]], 0, 0)
+    for k, c in enumerate((2, 0, 1, 2, 0)):
+        if k < TURNS:
+            iota(a("turn", k, NONE, 5), [[5, 384]], c, 0, True)
+        else:
+            act(a("turn", k, NONE, 5), a("base"), float(c), 1.0)
     for k in range(3):
         act(a("inttab", k, 3 * C, 3), a("base", 0, C), float(k), 1.0)
-    sc(a("inttab", 3 * C, 960), a("base", C, 384))
-    ms(a("eb"), 0.0)
+    act(a("inttab", 3 * C, 960), a("base", C, 384))
     ts(a("r16b"), a("r16"), 15, A.bitwise_and)
     ts(a("coli", 0, 1), a("r16", 0, 1), -1.0, A.mult, 128.0, A.add)
     ts(a("c0"), a("r16b"), 0.0, A.not_equal)
@@ -379,28 +509,34 @@ def rank_program(g, core, T, topo):
     ts(c_rest, a("r16b", 0, 1), 1.0, A.not_equal)
     ts(a("coli", 1, 2), a("coli", 0, 1), 15, A.bitwise_and)
     tt(a("cm", 0, 16), a("c0"), a("c1"), A.max)
-    ts(c_inv, c_last, 1.0, A.mult, 1.0 / BIG, A.add)
-    ts(c_big, c_rest, BIG, A.mult, 1.0, A.add)
+    act(c_inv, c_last, 1.0 / BIG, 1.0)
+    act(c_big, c_rest, 1.0, BIG)
     cp(c_pm, a("coli", 1, 2))
     ts(c_own, c_inv, c_inv, A.mult, -4.0, A.mult)
-    for o, x, c in ((c_col, c_inv, 0.2), (c_step, c_inv, 1.0 / 4096), (c_y, c_big, 4097.0), (c_round, c_big, 1.5 * 2 ** 35),
-                    (c_thr, c_big, 4096.0), (c_mid, c_big, 1024.0)):
-        ts(o, x, c, A.mult)
+    for o, x, c in [(c_col, c_inv, 0.2), (c_half, c_inv, 0.5), (c_y, c_big, 4097.0), (c_less, c_big, -1.0)] + [
+            (c_near[k], c_big, 4096.0 * (1.5 * 2 ** 23 - k)) for k in c_near]:
+        act(o, x, 0.0, c)
     for lo, n in ((16, 16), (32, 32), (64, 64), (128, 128), (256, 32), (288, 288)):
-        cp(a("cm", lo, lo + n), a("cm", 0, n))
+        act(a("cm", lo, lo + n), a("cm", 0, n))
     for name, c in (("nf", NOWHERE), ("inf", NOWHERE), ("pf", 0.0), ("sg", 0.0)):
-        ms(a(name, C, 384), c)
-    ms(a("f0"), 0.0)
-    ms(a("h0"), 0.0)
-    ms(a("turn", NONE, NONE + 8), 2047.0)
-    cp(a("eb", 3, 515, 4), a("ident"))
-    for b in range(4):
-        quant(tile_e(b)[0], tile_e(b)[1], a("eb", 3 - b, 515 - b))
+        act(a(name, C, 384), a("ones", 0, 96), 0.0, c)
+    for buf, n, runs in (("f0", 4, 54), ("s0", 5, 6)):
+        act(step(buf, 0, 0, runs, n), a("ones", 0, runs), 0.0, 0.0)
+        act(step(buf, 2, 0, runs, n), a("ones", 0, runs), 0.0, c_half)
+        act(step(buf, 3, 0, runs, n), a("ones", 0, runs), 0.0, 2.0)
+    act(step("s0", 4, 0, 6, 5), a("ones", 0, 6), 0.0, 1.0)
+    act(step("s1", 4, 0, 3, 5), a("ones", 0, 3), 0.0, 5.0 * C)
+    act(step("s1", 4, 3, 6, 5), a("ones", 0, 3), 0.0, 0.0)
+    act(step("h0", 0, 0, 18, 2), a("ones", 0, 18), 0.0, 0.0)
+    act(step("four", 0, 0, 18), a("ones", 0, 18), 0.0, -1e9)
+    for k in range(1, 4):
+        act(step("four", k, 0, 18), a("ones", 0, 18), 0.0, 0.0)
+    act(a("turn", NONE, NONE + 8), a("ones", 0, 8), 0.0, 2047.0)
     cp(a("tw16", 0, 60), a("twb", 0, 60))
     cp(a("uoff"), a("uoi"))
     ts(a("vw"), a("c16"), c_pm, A.add)
-    sc(a("tfn", 192, 960), ind(a("inttab"), a("tw16", 12, 60)))
-    cp(a("tfn", 0, 192), ind(a("inttab"), a("tw16", 0, 12)))
+    for lo, hi in TFN:
+        act(a("tfn", 16 * lo, 16 * hi), ind(a("inttab"), a("tw16", lo, hi)))
     quant(a("uq"), a("us"), a("ub"))
     pick_u(0, 128)
     state(0, 0)
@@ -408,17 +544,18 @@ def rank_program(g, core, T, topo):
     for k in range(3):
         scan(a("so", C * k, C * k + C), a("tfn", k, 3 * C, 3))
     scan(a("so", 3 * C, 960), a("tfn", 3 * C, 960))
-    ts(a("tb"), ends("so", 0, 60), c_inv, A.mult)
-    column(a("e54"), ends("so", 0, 54))
+    act(a("tb"), ends("so", 0, 60), 0.0, c_inv)
+    ts(a("k1"), a("twb", 0, 54), 1.0 / 3, A.mult, -1.0 / 3, A.add)
+    ts(a("k2"), a("twb", 0, 54), -2.0 * C, A.add)
+    tt(a("lb"), a("k1"), a("k2"), A.max)
+    cp(a("eg"), a("lb"))
     for k in range(3):
         act(a("lab", 18 * k, 18 * k + 18), a("vw"), float(k), 5.0)
         act(a("v5", 18 * k, 18 * k + 18), a("vw"), 0.0, 5.0)
-        ms(a("kap", 18 * k, 18 * k + 18), float(k))
     keys()
-    for k, c in enumerate((2.0, 0.0, 1.0, 2.0, 0.0)):
-        act(a("turn", k, NONE, 5), a("base"), c, 1.0)
-    act(a("two", 0, 2 * C, 2), a("base", 0, C), -1e29, 0.0)
-    act(a("two", 1, 2 * C, 2), a("base", 0, C), 0.0, 0.0)
+    slots(a("tb", 54, 60))
+    ms(a("two", 0, 2 * C, 2), -1e29)
+    ms(a("two", 1, 2 * C, 2), 0.0)
     pick_u(128, 256)
     pick_u(256, 384)
     quant(a("vq"), a("vs"), a("vb"))
@@ -432,155 +569,168 @@ def rank_program(g, core, T, topo):
         send([(nxt, "low", fp, sx[0], T[ls][:, C:2 * C]), (prv, "high", fn, sx[0], T[ls][:, 0:C])], [sx])
         send([(prv, "all", fn, u8, T[lq][:, 0:C].bitcast(dt.uint8))], [qx])
 
-        sc(a("bits", 16 * SPLIT, 864), ind(a("sg"), a("e54", SPLIT, 54)))
-        cp(a("bits", 0, 16 * SPLIT), ind(a("sg"), a("e54", 0, SPLIT)))
+        act(a("bits", 16 * SPLIT, 864), ind(a("sg"), a("eg", SPLIT, 54)), only="s")
+        cp(a("bits", 0, 16 * SPLIT), ind(a("sg"), a("eg", 0, SPLIT)))
         scan(a("sbo"), a("sg", 0, C))
-        ts(a("own"), ends("sbo", 0, 18), c_own, A.mult)
-        scan(a("sb", 0, 16 * SPLIT), a("bits", 0, 16 * SPLIT))
-        scan(a("sb", 16 * SPLIT, 864), a("bits", 16 * SPLIT, 864))
+        act(a("own"), ends("sbo", 0, 18), 0.0, c_own)
+        if t:
+            scan(a("sb", 0, 16 * SPLIT), a("bits", 0, 16 * SPLIT))
+            scan(a("sb", 16 * SPLIT, 864), a("bits", 16 * SPLIT, 864))
+        else:
+            for k in range(3):
+                scan(a("sb", C * k, C * k + C), a("bits", k, 864, 3))
         for b in range(4):
             mm(bank(4 + b), tile_e(b)[0], tile_e(b)[1], qx, sx)
-            act(a("dw", 384 * b, 384 * b + C), bank(4 + b), 0.0, 0.015625)
-            sc(a("du", C * b, C * b + C), bank(4 + b))
+            act(a("du", C * b, C * b + C), bank(4 + b))
+            act(a("dw", 384 * b, 384 * b + C), a("du", C * b, C * b + C), 0.0, 0.015625)
         for h in (1, 0):
             for b in range(4):
                 bk = bank(b + 4 * (1 - h))
                 mm(bk, tile_e(b)[0], tile_e(b)[1], a(lq, C * h, C * h + C), a(ls, C * h, C * h + C),
-                   [(fp, from_prv) if h else (fn, from_nxt)] if b == 0 else (),
+                   [(fp, from_prv) if h else (fn, from_nxt)],
                    [(big, (LAG_A if h else LAG_B) + (LAG_1 if t == 0 else 0))])
                 act(a("dn", 576 * b + C * h, 576 * b + C * h + C), bk, 0.0, 0.015625)
         for h in range(2):
             for b in range(4):
-                mm(bank(4 * h + b, H), tile_e(b)[0], tile_e(b)[1], half("qx%d" % t, h), half("sx%d" % t, h), stop=False)
+                mm(hbank(4 * h + b, h), tile_e(b)[0], tile_e(b)[1], half("qx%d" % t, h), half("sx%d" % t, h), stop=False)
         for k in range(3):
-            tt(a("w", 18 * k, 18 * k + 18), ends("sb", 18 * k, 18 * k + 18), a("own"), A.mult)
-        for s_ in range(3):
-            tt(a("key", s_, 162, 3), a("w"), a("kk", 54 * s_, 54 * s_ + 54), A.mult)
-        tt(a("k1"), a("key", 0, 54), a("key", 54, 108), A.max)
-        tt(a("k2"), a("key", 108, 162), a("dfl"), A.max)
-        tt(a("best"), a("k1"), a("k2"), A.max)
-        ts(a("idx"), a("best", 0, 54, 3), 4095, A.bitwise_and)
-        ts(a("lb", 0, 18), a("best", 0, 54, 3), 2047, A.bitwise_and)
-        for s_ in (1, 2):
-            ts(a("lb", 18 * s_, 18 * s_ + 18), a("best", s_, 54, 3), 2, A.logical_shift_right, 2047, A.bitwise_and)
-            ts(a("ki", 18 * s_ - 18, 18 * s_), a("best", s_, 54, 3), 3, A.bitwise_and)
+            lo, hi = 18 * k, 18 * k + 18
+            tt(a("w", lo, hi), ends("sb", lo, hi), a("own"), A.mult)
+            if t:
+                tt(a("ko", lo, hi), a("kk", lo, hi), a("own"), A.mult)
+                tt(step("kq", k + 1, 0, 18), ends("sb", lo, hi), a("ko", lo, hi), A.mult)
+            else:
+                tt(step("kq", k + 1, 0, 18), a("w", lo, hi), a("kk", lo, hi), A.mult)
+        scan(a("bq"), a("kq"), a("four"), A.add, A.max)
+        ts(a("idx"), step("bq", 3, 0, 18), 4095, A.bitwise_and)
+        ts(a("lb", 0, 18), step("bq", 3, 0, 18), 2047, A.bitwise_and)
         ts(a("offn"), a("idx"), float(NONE), A.min, 2.0, A.add)
         cp(a("offa"), a("lb", 0, 18))
-        ts(a("offp"), a("lb", 18, 36), 1.0, A.add)
-        ts(a("e2", 0, 18), a("lb", 0, 18), 0.2, A.mult, -0.2, A.add)
+        column(a("e2", 0, 18), a("lb", 0, 18))
+        for s_ in (1, 2):
+            tt(a("key", s_ - 1, 108, 2), a("w"), a("kk", 54 * s_, 54 * s_ + 54), A.mult)
+        tt(a("k1", 0, 36), a("key", 0, 36), a("key", 36, 72), A.max)
+        tt(a("k2", 0, 36), a("key", 72, 108), a("dfl"), A.max)
+        tt(a("best"), a("k1", 0, 36), a("k2", 0, 36), A.max)
+        for s_, lo in ((1, 36), (2, 18)):
+            ts(a("lb", lo, lo + 18), a("best", s_ - 1, 36, 2), 2, A.logical_shift_right, 2047, A.bitwise_and)
+            ts(a("kap", 18 * s_, 18 * s_ + 18), a("best", s_ - 1, 36, 2), 3, A.bitwise_and)
+        ts(a("offp"), a("lb", 36, 54), 1.0, A.add)
+        column(a("e2", 18, 36), a("lb", 18, 36))
         act(a("nf", 0, C), ind(a("turn"), a("offn")), 0.0, 4096.0)
-        cp(a("af"), ind(a("turn"), a("offa")))
-        sc(a("pf", 0, C), ind(a("turn"), a("offp")))
+        ops[act(a("af"), ind(a("turn"), a("offa")))]["lean"] = -1e4
+        act(a("pf", 0, C), ind(a("turn"), a("offp")))
         tt(a("inf", 0, C), ind(a("nf"), a("e2", 0, 18)), a("af"), A.add)
-        cp(a("gf", 864, 960), ind(a("inf"), a("esl")))
-        sc(a("bo"), ind(a("pf"), a("e2", 0, 18)))
-        sc(a("gf", 0, C), ind(a("inf"), a("e2", 0, 18)))
-        cp(a("kap", 18, 54), a("ki"))
-        tt(a("ks"), a("ki", 0, 18), a("ki", 18, 36), A.add)
-        ts(a("kap", 0, 18), a("ks"), -1.0, A.mult, 3.0, A.add)
-        tt(a("lab", 18, 36), a("ki", 0, 18), a("v5", 0, 18), A.add)
-        if more:
-            tt(a("lab", 0, 18), a("kap", 0, 18), a("v5", 0, 18), A.add)
-            tt(a("lab", 36, 54), a("ki", 18, 36), a("v5", 0, 18), A.add)
-        ts(a("thr"), a("lab", 18, 36), c_thr, A.mult, c_mid, A.add)
-        ts(odd("f1", 0, 18), a("lb", 0, 18), c_big, A.mult)
-        ts(a("yy", 0, 18), a("lb", 0, 18), c_y, A.mult)
-        ts(odd("h1", 0, 36), a("lb", 18, 54), c_big, A.mult)
-        tt(even("h1", 0, 18), odd("h1", 18, 36), odd("h1", 0, 18), A.subtract)
-
-        def moved(lo, hi):
-            tt(even("f1", lo, hi), ends("so", lo, hi), a("yy", lo, hi), A.subtract)
-            near(odd("f0", lo, hi), even("f1", lo, hi))
-            scan(a("fo", 2 * lo, 2 * hi), a("f1", 2 * lo, 2 * hi), a("f0", 2 * lo, 2 * hi))
-
+        tt(a("gf", 864, 960), ind(a("inf"), a("esl")), a("ys"), A.subtract)
         scan(a("so", 864, 960), a("gf", 864, 960))
-        moved(54, 60)
-        ea, eb_ = a("esend", 8 * t, 8 * t + 3), a("esend", 8 * t + 4, 8 * t + 7)
-        column(ea, odd("fo", 54, 57), float(C))
-        column(eb_, odd("fo", 57, 60))
+        act(step("s1", 0, 0, 6, 5), ends("so", 54, 60))
+        moved("s0", "s1", 0, 6, ends("so", 54, 60), 5)
+        scan(a("sn"), a("s1"), a("s0"))
+        column(a("esend", 8 * t, 8 * t + 6), step("sn", 4, 0, 6, 5))
+        ea, eb_ = a("esend", 8 * t, 8 * t + 3), a("esend", 8 * t + 3, 8 * t + 6)
         small = send([(nxt, "low", lst, ea[0], T[lst][:, 3:6]), (prv, "high", lst, eb_[0], T[lst][:, 0:3])], [ea, eb_])
         if t == 0:
             iota(a("otab", 0, 5 * C), [[3, C], [1, 5]], 0, 0, True)
             iota(a("otab", 5 * C, NONE), [[1, 2 * S], [0, 5]], 3 * C, 0, True)
-        scan(a("si"), a("inf", 0, C))
-        scan(a("sp"), a("bo"))
-        tt(a("zf"), ends("si", 0, 18), a("thr"), A.subtract)
-        tt(even("h1", 18, 36), ends("sp", 0, 18), odd("h1", 18, 36), A.subtract)
-        near(odd("h0", 0, 18), a("zf"))
-        near(odd("h0", 18, 36), a("zf"))
-        scan(a("ho"), a("h1"), a("h0"))
-        column(a("e2", 18, 54), odd("ho", 0, 36))
-        ts(a("yy", 18, 54), odd("ho", 0, 36), 4097.0, A.mult)
-        cp(odd("f1", 18, 54), odd("ho", 0, 36))
-        sc(a("gf", 2 * C, 3 * C), ind(a("inf"), a("e2", 36, 54)))
-        cp(a("gf", C, 2 * C), ind(a("inf"), a("e2", 18, 36)))
-        for k in range(3):
+        act(a("bo"), ind(a("pf"), a("e2", 0, 18)))
+        ts(step("f1", 1, 0, 36), a("lb", 0, 36), c_big, A.mult, c_less, A.add)
+        ts(a("yy", 0, 36), a("lb", 0, 36), c_y, A.mult)
+        ts(step("h1", 1, 0, 18, 2), a("lb", 36, 54), c_big, A.mult)
+
+        def read(k):
+            lo, hi = 18 * k, 18 * k + 18
+            act(a("gf", C * k, C * k + C), ind(a("inf"), a("e2", lo, hi)))
             scan(a("so", C * k, C * k + C), a("gf", C * k, C * k + C))
-        moved(0, 54)
-        column(a("e54"), odd("fo", 0, 54))
-        ts(a("nd"), even("f1", 0, 60), c_step, A.mult)
-        ts(a("e1"), a("nd"), -1.0, A.is_equal, -1.0, A.mult)
-        ts(a("e2f"), a("nd"), 2.0, A.is_equal, 2.0, A.mult)
-        act(a("val"), odd("fo", 0, 60), 0.0, c_inv)
-        tt(a("cor"), a("e1"), a("e2f"), A.add)
-        tt(a("tb"), a("val"), a("cor"), A.add)
+            tt(step("f1", 0, lo, hi), ends("so", lo, hi), a("yy", lo, hi), A.subtract)
+
+        def go(lo, hi):
+            moved("f0", "f1", lo, hi, step("f1", 0, lo, hi))
+            scan(a("fo", 4 * lo, 4 * hi), a("f1", 4 * lo, 4 * hi), a("f0", 4 * lo, 4 * hi))
+            column(a("e54", lo, hi), step("fo", 3, lo, hi))
+
+        read(0)
+        read(1)
+        go(0, 36)
+        flips, third_ = step("h0", 1, 0, 18, 2), step("ho", 1, 0, 18, 2)
+        near(a("fa", 0, 18), step("f1", 0, 0, 18), 1)
+        near(a("fa", 18, 36), step("f1", 0, 0, 18), -2)
+        tt(flips, a("fa", 0, 18), a("fa", 18, 36), A.add)
+        scan(a("sp"), a("bo"))
+        tt(step("h1", 0, 0, 18, 2), ends("sp", 0, 18), step("h1", 1, 0, 18, 2), A.subtract)
+        scan(a("ho"), a("h1"), a("h0"))
+        ts(a("e2", 36, 54), third_, c_col, A.mult, -0.2, A.add)
+        act(a("yy", 36, 54), third_, 0.0, 4097.0)
+        act(step("f1", 1, 36, 54), third_, c_less, 1.0)
+        read(2)
+        go(36, 54)
+        new = [step("fo", 3, 18 * k, 18 * k + 18) for k in range(3)]
+        act(a("tb", 0, 18), new[0])
+        tt(a("dd", 0, 18), new[1], new[2], A.subtract)
+        tt(a("dd", 18, 36), a("dd", 0, 18), flips, A.mult)
+        tt(a("tb", 18, 36), new[2], a("dd", 18, 36), A.add)
+        tt(a("tb", 36, 54), new[1], a("dd", 18, 36), A.subtract)
+        tt(a("ks"), a("kap", 18, 36), a("kap", 36, 54), A.add)
+        ts(a("kap", 0, 18), a("ks"), -1.0, A.mult, 3.0, A.add)
         if more:
+            tt(a("lab"), a("kap"), a("v5"), A.add)
+            column(a("eg"), a("tb", 0, 54))
             keys()
+            slots(step("sn", 3, 0, 6, 5))
         else:
             for s_ in range(3):
                 ts(a("kk", 54 * s_, 54 * s_ + 54), a("kap"), float(s_), A.is_equal, 4096.0, A.mult)
                 tt(a("key", s_, 162, 3), a("kk", 54 * s_, 54 * s_ + 54), a("tb", 0, 54), A.add)
-            cp(a("oto", 54, 60), a("tb", 54, 60))
+            cp(a("oto", 54, 60), step("sn", 3, 0, 6, 5))
             tt(a("k1"), a("key", 0, 54), a("key", 54, 108), A.max)
             tt(a("k2"), a("k1"), a("key", 108, 162), A.max)
             for s_ in range(3):
                 ts(a("oto", 18 * s_, 18 * s_ + 18), a("k2", s_, 54, 3), -4096.0, A.add)
-                sc(a("otf", s_, 3 * C, 3), ind(a("otab"), a("oto", 18 * s_, 18 * s_ + 18)))
-            sc(a("otf", 3 * C, 960), ind(a("otab"), a("oto", 54, 60)))
-            dma("s", T.ot[:], T.otf[0:128:16, :], rd=[a("otf")])
+                act(a("otf", s_, 3 * C, 3), ind(a("otab"), a("oto", 18 * s_, 18 * s_ + 18)))
+            act(a("otf", 3 * C, 960), ind(a("otab"), a("oto", 54, 60)))
+            dma("s", T.ot[:], T.otf[0:128:16, :], rd=[a("otf")], lat=1500)
 
         def plane(b):
             return a("dw", 384 * b, 384 * b + 384)
 
-        def third(k):
-            return a("e54", 18 * k, 18 * k + 18)
-
-        gate = {q: [(small, LAG_L)] for q in "vs"}
         for b in range(4):
-            q = BORDER[b]
-            i = (cp if q == "v" else sc)(a("dw", 384 * b + C, 384 * b + 384), ind(a("dn", 576 * b, 576 * b + 576), a(lst, 0, 6)),
-                                         [(lst, lists_in)] if BORDER.index(q) == b else (), gate[q])
-            gate[q] = [(i, 0)]
-        for b in range(4):
-            g0, g1 = a("g0", C * b, C * b + C), a("g1", C * b, C * b + C)
-            if WAYS[b] < 3:
-                (cp if WAYS[b] == 1 else sc)(g0, ind(plane(b), third(0)))
-                tt(g1, ind(plane(b), third(1)), g0, A.max)
-            else:
-                lo, hi = 2 * C * b, 2 * C * b + 2 * C
-                for k in range(2):
-                    sc(a("gi", lo + k, hi, 2), ind(plane(b), third(k)))
-                scan(a("go", lo, hi), a("gi", lo, hi), a("two"), A.add, A.max)
-                g1 = a("go", lo + 1, hi, 2)
-            tt(a("mt", b, 4 * C, 4), ind(plane(b), third(2)), g1, A.max)
-        for h in range(2):
-            quant(half("mq", h), half("ms", h), a("mt", 4 * H * h, 4 * H * h + 4 * H))
+            act(a("dw", 384 * b + C, 384 * b + 384), ind(a("dn", 576 * b, 576 * b + 576), a(lst, 0, 6)),
+                pre=[(lst, lists_in)], after=[(small, LAG_L)])
+        for p_, (c0, c1) in enumerate(PARTS):
+            third = [a("e54", 18 * k + c0 // 16, 18 * k + c1 // 16) for k in range(3)]
             for b in range(4):
-                mm(bank(4 * h + b, H), a("wq", 128 * b, 128 * b + 128), a("wsc", 128 * b, 128 * b + 128),
+                g0, g1 = a("g0", C * b + c0, C * b + c1), a("g1", C * b + c0, C * b + c1)
+                if WAYS[p_][b] < 3:
+                    act(g0, ind(plane(b), third[0]))
+                    tt(g1, ind(plane(b), third[1]), g0, A.max)
+                else:
+                    lo, hi = 2 * (C * b + c0), 2 * (C * b + c1)
+                    for k in range(2):
+                        act(a("gi", lo + k, hi, 2), ind(plane(b), third[k]))
+                    scan(a("go", lo, hi), a("gi", lo, hi), a("two", 0, hi - lo), A.add, A.max)
+                    g1 = a("go", lo + 1, hi, 2)
+                tt(a("mt", 4 * c0 + b, 4 * c1, 4), ind(plane(b), third[2]), g1, A.max)
+        for h in range(2):
+            quant(half("mq", h), half("ms", h), half("mt", h, 0, 4))
+            for b in range(4):
+                mm(hbank(4 * h + b, h), a("wq", 128 * b, 128 * b + 128), a("wsc", 128 * b, 128 * b + 128),
                    half("mq", h), half("ms", h), start=False)
         for h in range(2):
             for b in range(4):
-                tt(a("xt", 4 * H * h + b, 4 * H * h + 4 * H, 4), bank(4 * h + b, H),
-                   a("du", C * b + H * h, C * b + H * h + H), A.max)
+                tt(a("xt", 4 * CUT[h] + b, 4 * CUT[h + 1], 4), hbank(4 * h + b, h), half("du", h, C * b), A.max)
         state(t + 1, 0)
         state(t + 1, 1)
 
     qx, sx = a("qx%d" % R), a("sx%d" % R)
-    sc(half("yb", 0), bank(0, H))
-    cp(half("yb", 1), bank(1, H))
+    for h in range(2):
+        act(half("yb", h), hbank(h, h))
     dma("y", T.oc[:], qx[0].bitcast(dt.uint8), rd=[qx])
-    dma("s", T.y[:], T.yb[:], rd=[a("yb")])
+    dma("y", T.y[:], T.yb[:], rd=[a("yb")])
     for k in range(4):
-        dma("y", T.osc[4 * k:4 * k + 4, :], T["sx%d" % R][32 * k:32 * k + 4, :], rd=[sx])
-    emit(g, T, order(ops))
+        dma("s", T.osc[4 * k:4 * k + 4, :], T["sx%d" % R][32 * k:32 * k + 4, :], rd=[sx], lat=1200)
+    if "order" not in PLAN:
+        PLAN["order"] = order(ops)
+    turns, queues = PLAN["order"]
+    for o, q in zip(ops, queues):
+        o["q"], o["fn"] = q, o["ways"][q][0]
+    emit(g, T, [ops[i] for i in turns])
     g.wait_ge(T.sem.sent, sent[0])

@@ -11,26 +11,34 @@ FP8 = "float8_e4m3fn_x4"
 BIG = float(2 ** 50)
 NONE = 1920
 NOWHERE = 2047 * 4096.0
-SPLIT = 20
+SPLIT = ((0, 22), (22, 42), (42, 54))
 TFN = ((0, 20), (20, 40), (40, 60))
-TURNS = 3
-WAKE, LAG_A, LAG_B, LAG_L, LAG_1 = 200, 4500, 6500, 1600, 1500
-PASSES, HEAT, SOFT, JUMP, LEAN, EARLY, SEED, PLAN = 60000, 20.0, 0.3, 0.6, 400.0, 9000, 1, {}
+SIGNED = 2
+TURNS = 2
+WAKE, LAG_A, LAG_B, LAG_L, LAG_1 = 200, 2800, 4800, 1500, 2500
+SLOW = {LAG_A: 3600, LAG_B: 5800, LAG_L: 2500}
+SWEEPS = ((12000, 8000, 60.0), (8000, 7000, 25.0), (10000, 6000, 10.0), (7000, 3500, 4.0))
+SOFT, JUMP, TRADE, LEAN, SEED, PLAN = 0.4, 0.65, 0.2, 400.0, 73, {}
+FIRST = ("twb", "ub", "xin", "r16", "base", "ones", "eb", "uoi", "inttab", "tw16", "tfn", "uoff", "uq", "uq2", "us2",
+         "qx0", "ps", "sg", "r16b", "c0", "c1", "cm", "so", "k1", "k2", "lb", "eg", "coli", "c16", "col", "lab", "tb",
+         "low", "pr", "kk")
+ON_VECTOR = (("inttab", 0), ("inttab", 864), ("tfn", 0), ("cm", 16), ("cm", 32), ("cm", 48), ("cm", 64), ("cm", 128),
+             ("tb", 0), ("pr", 0))
 
 SCRATCH = {"ps": ("psum", [128, 4096], "float32")}
 for _d, _bufs in (
     ("bfloat16", {"xin": 4 * C, "xt": 4 * C, "mt": 4 * C, "ub": 512, "vb": 512, "eb": 520, "ones": 128,
-                  "cm": 576, "sb": 864, "sbo": C, "sg": 384, "bits": 864, "dw": 4 * 384, "du": 4 * C,
-                  "dn": 4 * 576, "g0": 4 * C, "g1": 4 * C, "gi": 8 * C, "go": 8 * C, "two": 2 * C}),
-    ("float32", {"c0": 16, "c1": 16, "col": 16, "vw": 18, "base": 384, "inttab": 960, "turn": 1928, "otab": 1920,
-                 "tfn": 960, "otf": 960, "so": 960, "sp": C, "own": 18, "w": 54, "pr": 54, "lab": 54, "v5": 54,
-                 "af": C, "nf": 384, "pf": 384, "inf": 384, "bo": C, "gf": 960, "yb": C, "kk": 162, "ko": 54,
-                 "kq": 72, "four": 72, "dfl": 36, "f0": 216, "f1": 216, "fo": 216, "h0": 36, "h1": 36, "ho": 36,
-                 "s0": 30, "s1": 30, "sn": 30, "yy": 54, "ys": 96, "tb": 60, "t4": 54, "tk": 90, "low": 54, "fa": 36,
+                  "cm": 384, "sb": 864, "sbo": C, "sg": 384, "bits": 864, "dw": 4 * 384, "du": 4 * C,
+                  "dn": 4 * 576, "g0": 4 * C, "g1": 4 * C, "gi": 8 * C, "go": 8 * C, "two": 320}),
+    ("float32", {"c0": 16, "c1": 16, "col": 16, "row": 8, "base": 390, "inttab": 960, "turn": 1960, "otab": 1920,
+                 "tfn": 960, "otf": 960, "so": 960, "sp": C, "own": 54, "w": 54, "pr": 54, "lab": 54, "v5": 54,
+                 "af": C, "nf": 384, "pf": 384, "inf": 384, "bo": C, "gf": 960, "yb": C, "kk": 162, "ko": 162,
+                 "kq": 216, "four": 72, "f0": 216, "f1": 216, "fo": 216, "h0": 54, "h1": 54, "ho": 54,
+                 "s0": 30, "s1": 30, "sn": 30, "yy": 54, "ys": 96, "tb": 60, "t4": 54, "tk": 90, "low": 54,
                  "ks": 18, "dd": 36}),
-    ("int32", {"twb": 64, "r16": 16, "r16b": 16, "coli": 8, "c16": 18, "uoi": 24, "key": 162, "k1": 54, "k2": 54,
-               "best": 36, "bq": 72, "lb": 54, "idx": 18, "kap": 54}),
-    ("uint16", {"tw16": 64, "uoff": 24, "offn": 18, "offa": 18, "offp": 18, "e2": 54, "e54": 54, "eg": 54, "esl": 6,
+    ("int32", {"twb": 64, "r16": 16, "r16b": 16, "coli": 8, "c16": 54, "uoi": 24, "key": 162, "k1": 54, "k2": 54,
+               "bq": 216, "lb": 54, "idx": 18, "kap": 54}),
+    ("uint16", {"tw16": 64, "uoff": 24, "offn": 18, "offp": 18, "e2": 54, "e54": 54, "eg": 60,
                 "osl": 6, "oto": 60, "esend": 24}),
     (FP8, {"wq": 512, "uq": 128, "uq2": 384, "vq": 128, "eq": 512, "mq": C}),
     ("uint8", {"wsc": 512, "us": 128, "us2": 384, "vs": 128, "es": 512, "ms": C}),
@@ -45,7 +53,7 @@ for _t in range(R):
     SCRATCH["ls%d" % _t] = ("sbuf", [128, 2 * C], "uint8")
     SCRATCH["lst%d" % _t] = ("sbuf", [128, 8], "uint16")
 
-POOL = {"v": 48, "s": 36, "t": 24, "g": 10}
+POOL = {"v": 48, "s": 36, "t": 24, "g": 14}
 NDMA = 16
 SEMAPHORES = (["%s%d" % (q, i) for q in POOL for i in range(POOL[q])] + ["d%d" % i for i in range(NDMA)]
               + ["%s%d" % (n, t) for n in ("fp", "fn", "lst") for t in range(R)] + ["sent"])
@@ -98,6 +106,11 @@ def order(ops):
         dep.append([(j, d[j]) for j in d if j not in reach])
         for j, w in dep[i]:
             back[j].append((i, w))
+    slow = [[(j, SLOW.get(w, w) if ops[j]["kind"] == "remote" else w) for j, w in dep[i]] for i in range(n)]
+    cases = [(dep, back), (slow, [[] for _ in ops])]
+    for i in range(n):
+        for j, w in slow[i]:
+            cases[1][1][j].append((i, w))
     lat = [o["lat"] for o in ops]
     ways = [sorted((q, o["ways"][q][1]) for q in o["ways"]) for o in ops]
     cost = [dict(w) for w in ways]
@@ -130,34 +143,129 @@ def order(ops):
                     ready.append(j)
         return end, queue
 
-    def run(lines):
-        end, why, left, after, soon, took = [0] * n, [None] * n, [len(e) for e in dep], [None] * n, [0] * n, [0] * n
-        for q in lines:
-            line = lines[q]
-            for k in range(len(line)):
-                took[line[k]] = cost[line[k]][q]
-                if k:
-                    after[line[k - 1]] = line[k]
-                    left[line[k]] += 1
-        ready, done = [i for i in range(n) if left[i] == 0], 0
-        while ready:
-            i = ready.pop()
-            done += 1
-            e = end[i] = soon[i] + took[i]
-            for j, w in back[i]:
-                if e + w > soon[j]:
-                    soon[j], why[j] = e + w, i
-                left[j] -= 1
-                if not left[j]:
-                    ready.append(j)
-            j = after[i]
-            if j is not None:
-                if e > soon[j]:
-                    soon[j], why[j] = e, -1 - i
-                left[j] -= 1
-                if not left[j]:
-                    ready.append(j)
-        return (end, why, soon) if done == n else None
+    price = {q: [c.get(q, 0) for c in cost] for q in "vstgy"}
+
+    def run(lines, users, waits, soonest, opens, tail, most):
+        end, why, left, soon = [0] * n, [None] * n, waits[:], soonest[:]
+        state, moved = [[lines[q], 0, len(lines[q]), opens[q], None, price[q]] for q in lines if lines[q]], True
+        while moved:
+            moved = False
+            for x in state:
+                line, k, size, e, before, took = x
+                if k == size or left[line[k]]:
+                    continue
+                moved = True
+                while k < size:
+                    i = line[k]
+                    if left[i]:
+                        break
+                    if e > soon[i]:
+                        soon[i], why[i] = e, before
+                    else:
+                        e = soon[i]
+                    e = end[i] = e + took[i]
+                    if e + tail[i] > most:
+                        return None
+                    for j, w in users[i]:
+                        left[j] -= 1
+                        if e + w > soon[j]:
+                            soon[j], why[j] = e + w, i
+                    before = -1 - i
+                    k += 1
+                x[1], x[3], x[4] = k, e, before
+        return (end, why, soon) if all(x[1] == x[2] for x in state) else None
+
+    def whole(lines):
+        return run(lines, back, [len(e) for e in dep], [0] * n, {q: 0 for q in lines}, [0] * n, 1e9)
+
+    def stretch(lines, lo, hi, passes, heat):
+        soon = whole(lines)[2]
+        mine = [i for i in range(n) if lo <= soon[i] < hi]
+        free = [z for z in mine if ops[z]["q"][0] not in "tgy"]
+        if len(free) < 2:
+            return lines
+        inside = set(mine)
+        head = {q: [i for i in lines[q] if soon[i] < lo] for q in lines}
+        foot = {q: [i for i in lines[q] if soon[i] >= hi] for q in lines}
+        causes = [[x for x in e if x[0] in inside] for e in dep]
+        waits = [len(e) for e in causes]
+        frames = []
+        for ins, outs in cases:
+            end = run(lines, outs, [len(e) for e in ins], [0] * n, {q: 0 for q in lines}, [0] * n, 1e9)[0]
+            rest = run({q: lines[q][::-1] for q in lines}, ins, [len(e) for e in outs], lat, {q: 0 for q in lines},
+                       [0] * n, 1e9)[0]
+            users = [[x for x in e if x[0] in inside] for e in outs]
+            tail = [max([lat[i]] + [w + rest[j] for j, w in outs[i] if j not in inside]) for i in range(n)]
+            reach = tail[:]
+            for i in sorted(mine, key=lambda z: -soon[z]):
+                reach[i] = max([tail[i]] + [w + min(cost[j].values()) + reach[j] for j, w in users[i]])
+            frame = (users, [max([0] + [end[j] + w for j, w in e if j not in inside]) for e in ins],
+                     {q: end[head[q][-1]] if head[q] else 0 for q in lines}, reach, tail,
+                     {q: rest[foot[q][0]] if foot[q] else 0 for q in lines}, [z for z in mine if tail[z]])
+            if any(dep[i] != slow[i] for i in mine) or not frames:
+                frames.append(frame)
+        users, soonest = frames[0][:2]
+        now, top, trial = None, None, {q: [i for i in lines[q] if i in inside] for q in lines}
+        dice, bell = rng.random_sample((passes, 7)).tolist(), rng.normal(0.0, 100.0, passes).tolist()
+        for turn in range(passes):
+            d = dice[turn]
+            slack = -heat * (1 - turn / passes) * math.log(1 - d[0])
+            seen = []
+            for k, (outs, first, opens, reach, tail, shuts, outer) in enumerate(frames):
+                got = run(trial, outs, waits, first, opens, reach, now[5][k] + 2 * slack + 200 if now else 1e9)
+                if not got:
+                    break
+                end = got[0]
+                seen.append(max([(end[z] + tail[z], z) for z in outer]
+                                + [(end[trial[q][-1]] + shuts[q], trial[q][-1]) for q in trial if trial[q]]) + got)
+            else:
+                worth = sum(x[0] for x in seen) / len(seen) + SOFT * sum(seen[0][2]) / len(mine)
+                if now is None or worth <= now[0] + slack:
+                    held = []
+                    for total, i, end, why, soon in seen:
+                        while why[i] is not None:
+                            j = why[i]
+                            if j < 0:
+                                j = -1 - j
+                                if ops[i]["q"][0] not in "tgy":
+                                    held.append((i, j))
+                            i = j
+                    now = (worth, trial, held, seen[0][4], seen[0][2], [x[0] for x in seen])
+                    if top is None or worth < top[0]:
+                        top = (worth, trial)
+            trial = dict(now[1])
+            how = int(8 * d[1])
+            if how < 5 and now[2]:
+                i, j = now[2][int(len(now[2]) * d[2])]
+                x = (i, j)[how % 2]
+            else:
+                i, x = None, free[int(len(free) * d[2])]
+            q = "v" if x in now[1]["v"] else "s"
+            line = list(trial[q])
+            k = line.index(x)
+            del line[k]
+            trial[q] = line
+            if len(cost[x]) > 1 and d[3] < TRADE:
+                other = list(trial["s" if q == "v" else "v"])
+                near = [z for z in other if len(cost[z]) > 1 and abs(now[3][z] - now[3][x]) < 1200]
+                if near:
+                    z = near[int(len(near) * d[4])]
+                    other[other.index(z)] = x
+                    trial["s" if q == "v" else "v"], x = other, z
+            elif ops[x]["kind"] == "op" and d[3] < JUMP:
+                q = "sv"[int(2 * d[4])] if len(cost[x]) > 1 else q
+                first = max([soonest[x]] + [now[4][z] + w for z, w in causes[x]])
+                last = min([hi] + [now[3][z] - w for z, w in users[x]]) - cost[x][q]
+                line, at = list(trial[q]), first + (last - first) * d[5] ** 2 + bell[turn]
+                k = 0
+                while k < len(line) and now[3][line[k]] < at:
+                    k += 1
+                trial[q] = line
+            else:
+                far = 1 + int(-2.0 * math.log(1 - d[6]))
+                k = min(max(k - far if x == i or how == 6 else k + far, 0), len(line))
+            line.insert(k, x)
+        return {q: head[q] + top[1][q] + foot[q] for q in lines}
 
     key, best = [0] * n, None
     for i in range(n - 1, -1, -1):
@@ -165,64 +273,21 @@ def order(ops):
     for turn in range(4):
         end, queue = place(key, dep, back, [0] * n, ways)
         late = place([-e for e in end], back, dep, lat, [[x] for x in queue])[0]
-        key = [-late[i] - ops[i].get("early", 0) for i in range(n)]
+        key = [ops[i]["first"] - 1e6 if "first" in ops[i] else -late[i] for i in range(n)]
         if turn == 1 or (turn > 1 and max(end) < best[0]):
             best = (max(end), end, queue)
     lines = {q: [i for i in sorted(range(n), key=lambda z: best[1][z]) if best[2][i][0] == q] for q in "vstgy"}
-    tails = [i for i in range(n) if not back[i]]
-    rng, now, top, trial = np.random.RandomState(SEED), None, None, lines
-    for turn in range(PASSES):
-        got = run(trial)
-        if got:
-            end, why, soon = got
-            i = max(tails, key=lambda z: end[z] + lat[z])
-            total = end[i] + lat[i]
-            worth = total + SOFT * sum(end) / n
-            if now is None or worth <= now[0] - HEAT * (1 - turn / PASSES) * math.log(1 - rng.random_sample()):
-                held = []
-                while i is not None:
-                    j = why[i]
-                    if j is not None and j < 0:
-                        j = -1 - j
-                        if ops[i]["q"][0] not in "tgy":
-                            held.append((i, j))
-                    i = j
-                now = (worth, trial, held, soon, end)
-                if top is None or total < top[0]:
-                    top = (total, trial, end, soon)
-        trial = dict(now[1])
-        how = rng.randint(8)
-        if how < 6 and now[2]:
-            i, j = now[2][rng.randint(len(now[2]))]
-            x = (i, j)[how % 2]
-        else:
-            x = rng.randint(n)
-            if ops[x]["q"][0] in "tgy":
-                continue
-        q = "v" if x in now[1]["v"] else "s"
-        line = list(trial[q])
-        k = line.index(x)
-        del line[k]
-        trial[q] = line
-        if ops[x]["kind"] == "op" and rng.random_sample() < JUMP:
-            q = "sv"[rng.randint(2)] if len(cost[x]) > 1 else q
-            lo = max([0] + [now[4][z] + w for z, w in dep[x]])
-            hi = min([now[0]] + [now[3][z] - w for z, w in back[x]]) - cost[x][q]
-            line, at = list(trial[q]), lo + (hi - lo) * rng.random_sample() ** 2 + rng.normal(0.0, 100.0)
-            k = 0
-            while k < len(line) and now[3][line[k]] < at:
-                k += 1
-            trial[q] = line
-        else:
-            far = 1 + int(rng.exponential(2.0))
-            k = min(max(k - far if (how < 6 and x == i) or how == 6 else k + far, 0), len(line))
-        line.insert(k, x)
-    PLAN["total"] = top[0]
+    rng = np.random.RandomState(SEED)
+    for wide, passes, heat in SWEEPS:
+        for lo in range(-wide // 2, int(best[0]), wide // 2):
+            lines = stretch(lines, lo, lo + wide, passes, heat)
+    end, why, soon = whole(lines)
+    PLAN["total"] = max(end[i] + lat[i] for i in range(n))
     queue = [None] * n
-    for q in top[1]:
-        for i in top[1][q]:
+    for q in lines:
+        for i in lines[q]:
             queue[i] = q
-    return sorted(range(n), key=lambda i: (top[3][i], top[2][i])), queue
+    return sorted(range(n), key=lambda i: (soon[i], end[i])), queue
 
 
 def emit(g, T, ops):
@@ -416,13 +481,15 @@ def rank_program(g, core, T, topo):
             sent[0] += len(en)
             tr.append(RemoteDMATransfer(dst_ids=[DstId(rid=rid, pnc=pid)], dma_engine_mask=sum(1 << e for e in en),
                                         remote_sem=T.sem[sem], src=s_, dst=d_))
-        return rec("g", lambda e: e.remote_dma_fused(tr, local_sem=T.sem.sent), rd, [], 300, kind="remote")
+        return rec("g", lambda e: e.remote_dma_fused(tr, local_sem=T.sem.sent), rd, [],
+                   300 if sent[0] > len(en) else 300 + LAG_1, kind="remote")
 
-    from_prv = len(part(prv, core, "all")) + len(part(prv, core, "low"))
-    from_nxt = len(part(nxt, core, "all")) + len(part(nxt, core, "high"))
+    from_prv = 2 * len(part(prv, core, "all"))
+    from_nxt = 2 * len(part(nxt, core, "all"))
     lists_in = len(part(prv, core, "low")) + len(part(nxt, core, "high"))
 
-    c_big, c_less, c_inv, c_half, c_own, c_col, c_y, c_pm, c_last, c_rest = [a("col", i, i + 1) for i in range(10)]
+    (c_big, c_inv, c_half, c_own, c_col, c_pm, c_last, c_rest, c_y,
+     c_less) = [a("col", i, i + 1) for i in range(10)]
     c_near = {k: a("col", 13 + k, 14 + k) for k in range(-2, 3)}
 
     def column(o, x):
@@ -446,10 +513,9 @@ def rank_program(g, core, T, topo):
         act(step("kq", 0, 0, 18), a("tb", 0, 18), 2048.0, 1.0)
         for s_ in (1, 2):
             tt(a("kk", 54 * s_, 54 * s_ + 54), a("pr"), a("tk", 18 * s_, 18 * s_ + 54), A.add)
-            act(a("dfl", s_ - 1, 36, 2), a("tk", 18 * s_, 18 * s_ + 18))
+        act(step("kq", 0, 18, 54), a("tk", 18, 54))
 
     def slots(x):
-        column(a("esl"), x)
         ts(a("osl"), x, 1.0, A.add)
         act(a("ys"), ind(a("turn"), a("osl")), 0.0, 4097.0)
         act(step("s1", 1, 0, 6, 5), x, c_less, c_big)
@@ -473,31 +539,46 @@ def rank_program(g, core, T, topo):
         else:
             mm(hbank(h, h), a("vq"), a("vs"), q_, s_)
 
-    dma("y", T.twb[:, 0:60], T.tw[:], wr=[a("twb")], lat=1500)
-    dma("s", T.ub[:], T.u[:], wr=[a("ub")], lat=2200)
-    dma("y", T.xin[:], T.x[:], wr=[a("xin")], lat=2800)
+    dma("y", T.twb[:, 0:60], T.tw[:], wr=[a("twb")], lat=1300)
+    dma("s", T.ub[:], T.u[:], wr=[a("ub")], lat=1600)
+    dma("y", T.xin[:], T.x[:], wr=[a("xin")], lat=2400)
     dma("y", T.wq[:].bitcast(dt.uint8), T.wc[:], rd=[a("xin")], wr=[a("wq")], lat=4000)
     dma("y", T.wsc[:], T.ws[:], wr=[a("wsc")], lat=4000)
     dma("y", T.vb[:], T.v[:], wr=[a("vb")], lat=4500)
-    first = len(ops)
     ms(a("ones"), 1.0)
     ms(a("eb"), 0.0)
     iota(a("r16"), [[1, 16]], 128, -1)
-    iota(a("base"), [[5, 384]], 0, 0, True)
+    iota(a("base"), [[5, 390]], 0, 0, True)
     rec("g", lambda e: e.affine_select(T.eb[:, 3:515:4], T.ones[:], [[-1, 128]], A.is_equal, 0.0, 0, 1),
         [a("ones")], [a("eb", 3, 515, 4)], 400)
     for b in range(4):
         quant(tile_e(b)[0], tile_e(b)[1], a("eb", 3 - b, 515 - b))
-    for o in ops[first:]:
-        o["early"] = EARLY
     iota(a("uoi"), [[1, 3], [16, 8]], 0, 0)
-    iota(a("c16"), [[16, 18]], 0, 0)
+    iota(a("c16"), [[1, 3], [80, 18]], 0, 0)
     iota(a("kap"), [[1, 3], [0, 18]], 0, 0)
-    for k, c in enumerate((2, 0, 1, 2, 0)):
-        if k < TURNS:
-            iota(a("turn", k, NONE, 5), [[5, 384]], c, 0, True)
-        else:
-            act(a("turn", k, NONE, 5), a("base"), float(c), 1.0)
+    iota(a("row", 0, 5), [[-1, 5]], 3 * 2 ** 22 + 2, 0, True)
+    iota(a("row", 5, 7), [[-4098, 2]], 4097, 0, True)
+
+    def turns(lo, hi):
+        for k in range(lo, hi):
+            iota(a("turn", k, 1950, 5), [[5, 390]], (2, 0, 1, 2, 0)[k], 0, True)
+
+    def fill(o, c):
+        act(o, a("ones", 0, o[2]), 0.0, float(c))
+
+    turns(0, TURNS)
+    fill(step("s1", 4, 0, 3, 5), 5 * C)
+    fill(step("s1", 4, 3, 6, 5), 0)
+
+    fill(a("turn", 1950), 2047 + 30)
+    for name, c in (("nf", NOWHERE), ("inf", NOWHERE), ("pf", 0)):
+        fill(a(name, C, 384), c)
+    for k, c in ((0, 0), (3, 2), (4, 1)):
+        fill(step("s0", k, 0, 6, 5), c)
+    for k in range(TURNS, 5):
+        act(a("turn", k, 1950, 5), a("base"), (2.0, 0.0, 1.0, 2.0, 0.0)[k], 1.0)
+    ms(a("four"), 0.0)
+    ms(step("four", 0, 0, 18), -1e9)
     for k in range(3):
         act(a("inttab", k, 3 * C, 3), a("base", 0, C), float(k), 1.0)
     act(a("inttab", 3 * C, 960), a("base", C, 384))
@@ -511,30 +592,19 @@ def rank_program(g, core, T, topo):
     tt(a("cm", 0, 16), a("c0"), a("c1"), A.max)
     act(c_inv, c_last, 1.0 / BIG, 1.0)
     act(c_big, c_rest, 1.0, BIG)
-    cp(c_pm, a("coli", 1, 2))
+    ts(c_pm, a("coli", 1, 2), 5.0, A.mult)
     ts(c_own, c_inv, c_inv, A.mult, -4.0, A.mult)
-    for o, x, c in [(c_col, c_inv, 0.2), (c_half, c_inv, 0.5), (c_y, c_big, 4097.0), (c_less, c_big, -1.0)] + [
-            (c_near[k], c_big, 4096.0 * (1.5 * 2 ** 23 - k)) for k in c_near]:
-        act(o, x, 0.0, c)
-    for lo, n in ((16, 16), (32, 32), (64, 64), (128, 128), (256, 32), (288, 288)):
+    act(c_col, c_inv, 0.0, 0.2)
+    act(c_half, c_inv, 0.0, 0.5)
+    ts(a("col", 11, 16), a("row", 0, 5), 4096.0, A.mult, c_big, A.mult)
+    act(a("col", 8, 10), a("row", 5, 7), 0.0, c_big)
+    for lo, n in ((16, 16), (32, 16), (48, 16), (64, 64), (128, 64), (192, 64), (256, 64), (320, 64)):
         act(a("cm", lo, lo + n), a("cm", 0, n))
-    for name, c in (("nf", NOWHERE), ("inf", NOWHERE), ("pf", 0.0), ("sg", 0.0)):
-        act(a(name, C, 384), a("ones", 0, 96), 0.0, c)
+    act(a("sg", C, 384), a("ones", 0, 96), 0.0, 0.0)
     for buf, n, runs in (("f0", 4, 54), ("s0", 5, 6)):
-        act(step(buf, 0, 0, runs, n), a("ones", 0, runs), 0.0, 0.0)
         act(step(buf, 2, 0, runs, n), a("ones", 0, runs), 0.0, c_half)
-        act(step(buf, 3, 0, runs, n), a("ones", 0, runs), 0.0, 2.0)
-    act(step("s0", 4, 0, 6, 5), a("ones", 0, 6), 0.0, 1.0)
-    act(step("s1", 4, 0, 3, 5), a("ones", 0, 3), 0.0, 5.0 * C)
-    act(step("s1", 4, 3, 6, 5), a("ones", 0, 3), 0.0, 0.0)
-    act(step("h0", 0, 0, 18, 2), a("ones", 0, 18), 0.0, 0.0)
-    act(step("four", 0, 0, 18), a("ones", 0, 18), 0.0, -1e9)
-    for k in range(1, 4):
-        act(step("four", k, 0, 18), a("ones", 0, 18), 0.0, 0.0)
-    act(a("turn", NONE, NONE + 8), a("ones", 0, 8), 0.0, 2047.0)
     cp(a("tw16", 0, 60), a("twb", 0, 60))
     cp(a("uoff"), a("uoi"))
-    ts(a("vw"), a("c16"), c_pm, A.add)
     for lo, hi in TFN:
         act(a("tfn", 16 * lo, 16 * hi), ind(a("inttab"), a("tw16", lo, hi)))
     quant(a("uq"), a("us"), a("ub"))
@@ -548,17 +618,19 @@ def rank_program(g, core, T, topo):
     ts(a("k1"), a("twb", 0, 54), 1.0 / 3, A.mult, -1.0 / 3, A.add)
     ts(a("k2"), a("twb", 0, 54), -2.0 * C, A.add)
     tt(a("lb"), a("k1"), a("k2"), A.max)
-    cp(a("eg"), a("lb"))
-    for k in range(3):
-        act(a("lab", 18 * k, 18 * k + 18), a("vw"), float(k), 5.0)
-        act(a("v5", 18 * k, 18 * k + 18), a("vw"), 0.0, 5.0)
+    cp(a("eg", 0, 54), a("lb"))
+    column(a("eg", 54, 60), a("tb", 54, 60))
+    ts(a("lab"), a("c16"), c_pm, A.add)
+    tt(a("v5"), a("lab"), a("kap"), A.subtract)
     keys()
+    for o in ops:
+        name, lo = o["w"][0][:2]
+        if name in FIRST and (name, lo) != ("sg", C):
+            o["first"] = FIRST.index(name)
+            o["lean"] = -1e4 if (name, lo) in ON_VECTOR else 1e4
     slots(a("tb", 54, 60))
-    ms(a("two", 0, 2 * C, 2), -1e29)
-    ms(a("two", 1, 2 * C, 2), 0.0)
-    pick_u(128, 256)
-    pick_u(256, 384)
-    quant(a("vq"), a("vs"), a("vb"))
+    ms(a("two"), 0.0)
+    ms(a("two", 0, 320, 2), -1e29)
 
     for t in range(R):
         more = t < R - 1
@@ -566,62 +638,63 @@ def rank_program(g, core, T, topo):
         lq, ls, lst, fp, fn = "lq%d" % t, "ls%d" % t, "lst%d" % t, "fp%d" % t, "fn%d" % t
         u8 = qx[0].bitcast(dt.uint8)
         big = send([(nxt, "all", fp, u8, T[lq][:, C:2 * C].bitcast(dt.uint8))], [qx])
-        send([(nxt, "low", fp, sx[0], T[ls][:, C:2 * C]), (prv, "high", fn, sx[0], T[ls][:, 0:C])], [sx])
+        send([(nxt, "all", fp, sx[0], T[ls][:, C:2 * C])], [sx])
         send([(prv, "all", fn, u8, T[lq][:, 0:C].bitcast(dt.uint8))], [qx])
+        send([(prv, "all", fn, sx[0], T[ls][:, 0:C])], [sx])
+        if t == 0:
+            iota(a("h0"), [[0, 18], [1, 3]], 0, 0, True)
+            for k in (0, 3):
+                iota(step("f0", k, 0, 54), [[0, 54]], 2 * k // 3, 0, True)
 
-        act(a("bits", 16 * SPLIT, 864), ind(a("sg"), a("eg", SPLIT, 54)), only="s")
-        cp(a("bits", 0, 16 * SPLIT), ind(a("sg"), a("eg", 0, SPLIT)))
+        for k, (lo, hi) in enumerate(SPLIT):
+            ops[act(a("bits", 16 * lo, 16 * hi), ind(a("sg"), a("eg", lo, hi)))]["lean"] = 1e4 if k else -1e4
+            if t:
+                scan(a("sb", 16 * lo, 16 * hi), a("bits", 16 * lo, 16 * hi))
         scan(a("sbo"), a("sg", 0, C))
-        act(a("own"), ends("sbo", 0, 18), 0.0, c_own)
-        if t:
-            scan(a("sb", 0, 16 * SPLIT), a("bits", 0, 16 * SPLIT))
-            scan(a("sb", 16 * SPLIT, 864), a("bits", 16 * SPLIT, 864))
-        else:
+        for k in range(3):
+            act(a("own", 18 * k, 18 * k + 18), ends("sbo", 0, 18), 0.0, c_own)
+        if not t:
             for k in range(3):
                 scan(a("sb", C * k, C * k + C), a("bits", k, 864, 3))
         for b in range(4):
             mm(bank(4 + b), tile_e(b)[0], tile_e(b)[1], qx, sx)
-            act(a("du", C * b, C * b + C), bank(4 + b))
-            act(a("dw", 384 * b, 384 * b + C), a("du", C * b, C * b + C), 0.0, 0.015625)
+            act(a("dw", 384 * b, 384 * b + C), bank(4 + b), 0.0, 0.015625)
+            ops[act(a("du", C * b, C * b + C), a("dw", 384 * b, 384 * b + C), 0.0, 64.0, after=[(big, 0)])]["lean"] = 1e4
         for h in (1, 0):
             for b in range(4):
                 bk = bank(b + 4 * (1 - h))
                 mm(bk, tile_e(b)[0], tile_e(b)[1], a(lq, C * h, C * h + C), a(ls, C * h, C * h + C),
                    [(fp, from_prv) if h else (fn, from_nxt)],
-                   [(big, (LAG_A if h else LAG_B) + (LAG_1 if t == 0 else 0))])
+                   [(big, LAG_A if h else LAG_B)])
                 act(a("dn", 576 * b + C * h, 576 * b + C * h + C), bk, 0.0, 0.015625)
         for h in range(2):
             for b in range(4):
                 mm(hbank(4 * h + b, h), tile_e(b)[0], tile_e(b)[1], half("qx%d" % t, h), half("sx%d" % t, h), stop=False)
-        for k in range(3):
-            lo, hi = 18 * k, 18 * k + 18
-            tt(a("w", lo, hi), ends("sb", lo, hi), a("own"), A.mult)
-            if t:
-                tt(a("ko", lo, hi), a("kk", lo, hi), a("own"), A.mult)
-                tt(step("kq", k + 1, 0, 18), ends("sb", lo, hi), a("ko", lo, hi), A.mult)
-            else:
-                tt(step("kq", k + 1, 0, 18), a("w", lo, hi), a("kk", lo, hi), A.mult)
-        scan(a("bq"), a("kq"), a("four"), A.add, A.max)
+        if not t or SIGNED < 3:
+            tt(a("w"), ends("sb", 0, 54), a("own"), A.mult)
+        for s_ in range(3):
+            ahead = t and s_ < SIGNED
+            if ahead:
+                tt(a("ko", 54 * s_, 54 * s_ + 54), a("kk", 54 * s_, 54 * s_ + 54), a("own"), A.mult)
+            for k in range(3):
+                lo, hi, at = 18 * k, 18 * k + 18, 54 * s_ + 18 * k
+                tt(step("kq", k + 1, 18 * s_, 18 * s_ + 18), ends("sb", lo, hi) if ahead else a("w", lo, hi),
+                   a("ko" if ahead else "kk", at, at + 18), A.mult)
+            scan(a("bq", 72 * s_, 72 * s_ + 72), a("kq", 72 * s_, 72 * s_ + 72), a("four"), A.add, A.max)
         ts(a("idx"), step("bq", 3, 0, 18), 4095, A.bitwise_and)
         ts(a("lb", 0, 18), step("bq", 3, 0, 18), 2047, A.bitwise_and)
-        ts(a("offn"), a("idx"), float(NONE), A.min, 2.0, A.add)
-        cp(a("offa"), a("lb", 0, 18))
+        ts(a("offn"), a("idx"), float(NONE), A.min)
         column(a("e2", 0, 18), a("lb", 0, 18))
-        for s_ in (1, 2):
-            tt(a("key", s_ - 1, 108, 2), a("w"), a("kk", 54 * s_, 54 * s_ + 54), A.mult)
-        tt(a("k1", 0, 36), a("key", 0, 36), a("key", 36, 72), A.max)
-        tt(a("k2", 0, 36), a("key", 72, 108), a("dfl"), A.max)
-        tt(a("best"), a("k1", 0, 36), a("k2", 0, 36), A.max)
         for s_, lo in ((1, 36), (2, 18)):
-            ts(a("lb", lo, lo + 18), a("best", s_ - 1, 36, 2), 2, A.logical_shift_right, 2047, A.bitwise_and)
-            ts(a("kap", 18 * s_, 18 * s_ + 18), a("best", s_ - 1, 36, 2), 3, A.bitwise_and)
+            ts(a("lb", lo, lo + 18), step("bq", 3, 18 * s_, 18 * s_ + 18), 2, A.logical_shift_right, 2047, A.bitwise_and)
+        ts(a("kap", 18, 54), step("bq", 3, 18, 54), 3, A.bitwise_and)
         ts(a("offp"), a("lb", 36, 54), 1.0, A.add)
         column(a("e2", 18, 36), a("lb", 18, 36))
-        act(a("nf", 0, C), ind(a("turn"), a("offn")), 0.0, 4096.0)
-        ops[act(a("af"), ind(a("turn"), a("offa")))]["lean"] = -1e4
+        act(a("nf", 0, C), ind(a("turn", 32), a("offn")), -30 * 4096.0, 4096.0)
+        ops[act(a("af"), ind(a("turn"), a("offn")))]["lean"] = -1e4
         act(a("pf", 0, C), ind(a("turn"), a("offp")))
         tt(a("inf", 0, C), ind(a("nf"), a("e2", 0, 18)), a("af"), A.add)
-        tt(a("gf", 864, 960), ind(a("inf"), a("esl")), a("ys"), A.subtract)
+        tt(a("gf", 864, 960), ind(a("inf"), a("eg", 54, 60)), a("ys"), A.subtract)
         scan(a("so", 864, 960), a("gf", 864, 960))
         act(step("s1", 0, 0, 6, 5), ends("so", 54, 60))
         moved("s0", "s1", 0, 6, ends("so", 54, 60), 5)
@@ -635,7 +708,7 @@ def rank_program(g, core, T, topo):
         act(a("bo"), ind(a("pf"), a("e2", 0, 18)))
         ts(step("f1", 1, 0, 36), a("lb", 0, 36), c_big, A.mult, c_less, A.add)
         ts(a("yy", 0, 36), a("lb", 0, 36), c_y, A.mult)
-        ts(step("h1", 1, 0, 18, 2), a("lb", 36, 54), c_big, A.mult)
+        ts(step("h1", 2, 0, 18, 3), a("lb", 36, 54), c_big, A.mult)
 
         def read(k):
             lo, hi = 18 * k, 18 * k + 18
@@ -651,12 +724,11 @@ def rank_program(g, core, T, topo):
         read(0)
         read(1)
         go(0, 36)
-        flips, third_ = step("h0", 1, 0, 18, 2), step("ho", 1, 0, 18, 2)
-        near(a("fa", 0, 18), step("f1", 0, 0, 18), 1)
-        near(a("fa", 18, 36), step("f1", 0, 0, 18), -2)
-        tt(flips, a("fa", 0, 18), a("fa", 18, 36), A.add)
+        flips, third_ = step("ho", 1, 0, 18, 3), step("ho", 2, 0, 18, 3)
+        near(step("h1", 0, 0, 18, 3), step("f1", 0, 0, 18), 1)
+        near(step("h1", 1, 0, 18, 3), step("f1", 0, 0, 18), -2)
         scan(a("sp"), a("bo"))
-        tt(step("h1", 0, 0, 18, 2), ends("sp", 0, 18), step("h1", 1, 0, 18, 2), A.subtract)
+        tt(step("h0", 2, 0, 18, 3), ends("sp", 0, 18), step("h1", 2, 0, 18, 3), A.subtract)
         scan(a("ho"), a("h1"), a("h0"))
         ts(a("e2", 36, 54), third_, c_col, A.mult, -0.2, A.add)
         act(a("yy", 36, 54), third_, 0.0, 4097.0)
@@ -664,22 +736,29 @@ def rank_program(g, core, T, topo):
         read(2)
         go(36, 54)
         new = [step("fo", 3, 18 * k, 18 * k + 18) for k in range(3)]
-        act(a("tb", 0, 18), new[0])
-        tt(a("dd", 0, 18), new[1], new[2], A.subtract)
-        tt(a("dd", 18, 36), a("dd", 0, 18), flips, A.mult)
-        tt(a("tb", 18, 36), new[2], a("dd", 18, 36), A.add)
-        tt(a("tb", 36, 54), new[1], a("dd", 18, 36), A.subtract)
         tt(a("ks"), a("kap", 18, 36), a("kap", 36, 54), A.add)
         ts(a("kap", 0, 18), a("ks"), -1.0, A.mult, 3.0, A.add)
+
+        def swap(o1, o2, x1, x2):
+            tt(a("dd", 0, 18), x1, x2, A.subtract)
+            tt(a("dd", 18, 36), a("dd", 0, 18), flips, A.mult)
+            tt(o1, x2, a("dd", 18, 36), A.add)
+            tt(o2, x1, a("dd", 18, 36), A.subtract)
+
         if more:
+            act(a("tb", 0, 18), new[0])
+            act(a("tb", 54, 60), step("sn", 3, 0, 6, 5))
+            swap(a("tb", 18, 36), a("tb", 36, 54), new[1], new[2])
             tt(a("lab"), a("kap"), a("v5"), A.add)
-            column(a("eg"), a("tb", 0, 54))
+            column(a("eg"), a("tb"))
             keys()
             slots(step("sn", 3, 0, 6, 5))
         else:
+            cp(a("lab", 0, 18), a("kap", 0, 18))
+            swap(a("lab", 18, 36), a("lab", 36, 54), a("kap", 18, 36), a("kap", 36, 54))
             for s_ in range(3):
-                ts(a("kk", 54 * s_, 54 * s_ + 54), a("kap"), float(s_), A.is_equal, 4096.0, A.mult)
-                tt(a("key", s_, 162, 3), a("kk", 54 * s_, 54 * s_ + 54), a("tb", 0, 54), A.add)
+                ts(a("kk", 54 * s_, 54 * s_ + 54), a("lab"), float(s_), A.is_equal, 4096.0, A.mult)
+                tt(a("key", s_, 162, 3), a("kk", 54 * s_, 54 * s_ + 54), step("fo", 3, 0, 54), A.add)
             cp(a("oto", 54, 60), step("sn", 3, 0, 6, 5))
             tt(a("k1"), a("key", 0, 54), a("key", 54, 108), A.max)
             tt(a("k2"), a("k1"), a("key", 108, 162), A.max)
@@ -687,7 +766,7 @@ def rank_program(g, core, T, topo):
                 ts(a("oto", 18 * s_, 18 * s_ + 18), a("k2", s_, 54, 3), -4096.0, A.add)
                 act(a("otf", s_, 3 * C, 3), ind(a("otab"), a("oto", 18 * s_, 18 * s_ + 18)))
             act(a("otf", 3 * C, 960), ind(a("otab"), a("oto", 54, 60)))
-            dma("s", T.ot[:], T.otf[0:128:16, :], rd=[a("otf")], lat=1500)
+            dma("y", T.ot[:], T.otf[0:128:16, :], rd=[a("otf")], lat=1500)
 
         def plane(b):
             return a("dw", 384 * b, 384 * b + 384)
@@ -709,6 +788,12 @@ def rank_program(g, core, T, topo):
                     scan(a("go", lo, hi), a("gi", lo, hi), a("two", 0, hi - lo), A.add, A.max)
                     g1 = a("go", lo + 1, hi, 2)
                 tt(a("mt", 4 * c0 + b, 4 * c1, 4), ind(plane(b), third[2]), g1, A.max)
+        if more:
+            pick_u(128 * t + 128, 128 * t + 256)
+            ops[-2]["after"], ops[-1]["after"] = [(small, 0)], [(small, 0)]
+        if t == 1:
+            quant(a("vq"), a("vs"), a("vb"))
+            ops[-1]["after"] = [(big, 500)]
         for h in range(2):
             quant(half("mq", h), half("ms", h), half("mt", h, 0, 4))
             for b in range(4):
@@ -723,8 +808,8 @@ def rank_program(g, core, T, topo):
     qx, sx = a("qx%d" % R), a("sx%d" % R)
     for h in range(2):
         act(half("yb", h), hbank(h, h))
-    dma("y", T.oc[:], qx[0].bitcast(dt.uint8), rd=[qx])
-    dma("y", T.y[:], T.yb[:], rd=[a("yb")])
+    dma("y", T.oc[:], qx[0].bitcast(dt.uint8), rd=[qx], lat=1500)
+    dma("y", T.y[:], T.yb[:], rd=[a("yb")], lat=1500)
     for k in range(4):
         dma("s", T.osc[4 * k:4 * k + 4, :], T["sx%d" % R][32 * k:32 * k + 4, :], rd=[sx], lat=1200)
     if "order" not in PLAN:

import math
import numpy as np
from concourse.bass import DstId, RemoteDMATransfer
from concourse.mybir import dt, AluOpType, ActivationFunctionType

C, S, R = 288, 48, 3
CUT = (0, 160, C)
PARTS = ((0, 160), (160, C))
WAYS = ((3, 3, 2, 2), (3, 3, 3, 3))
FP8 = "float8_e4m3fn_x4"
BIG = float(2 ** 50)
NONE = 1920
NOWHERE = 2047 * 4096.0
SPLIT = ((0, 22), (22, 42), (42, 54))
TFN = ((0, 20), (20, 40), (40, 60))
SIGNED = 2
TURNS = 2
WAKE, LAG_A, LAG_B, LAG_L, LAG_1 = 200, 2800, 4800, 1500, 2500
SLOW = {LAG_A: 3600, LAG_B: 5800, LAG_L: 2500}
SWEEPS = ((12000, 8000, 60.0), (8000, 7000, 25.0), (10000, 6000, 10.0), (7000, 3500, 4.0))
SOFT, JUMP, TRADE, LEAN, SEED, PLAN = 0.4, 0.65, 0.2, 400.0, 73, {}
FIRST = ("twb", "ub", "xin", "r16", "base", "ones", "eb", "uoi", "inttab", "tw16", "tfn", "uoff", "uq", "uq2", "us2",
         "qx0", "ps", "sg", "r16b", "c0", "c1", "cm", "so", "k1", "k2", "lb", "eg", "coli", "c16", "col", "lab", "tb",
         "low", "pr", "kk")
ON_VECTOR = (("inttab", 0), ("inttab", 864), ("tfn", 0), ("cm", 16), ("cm", 32), ("cm", 48), ("cm", 64), ("cm", 128),
             ("tb", 0), ("pr", 0))

SCRATCH = {"ps": ("psum", [128, 4096], "float32")}
for _d, _bufs in (
    ("bfloat16", {"xin": 4 * C, "xt": 4 * C, "mt": 4 * C, "ub": 512, "vb": 512, "eb": 520, "ones": 128,
                  "cm": 384, "sb": 864, "sbo": C, "sg": 384, "bits": 864, "dw": 4 * 384, "du": 4 * C,
                  "dn": 4 * 576, "g0": 4 * C, "g1": 4 * C, "gi": 8 * C, "go": 8 * C, "two": 320}),
    ("float32", {"c0": 16, "c1": 16, "col": 16, "row": 8, "base": 390, "inttab": 960, "turn": 1960, "otab": 1920,
                 "tfn": 960, "otf": 960, "so": 960, "sp": C, "own": 54, "w": 54, "pr": 54, "lab": 54, "v5": 54,
                 "af": C, "nf": 384, "pf": 384, "inf": 384, "bo": C, "gf": 960, "yb": C, "kk": 162, "ko": 162,
                 "kq": 216, "four": 72, "f0": 216, "f1": 216, "fo": 216, "h0": 54, "h1": 54, "ho": 54,
                 "s0": 30, "s1": 30, "sn": 30, "yy": 54, "ys": 96, "tb": 60, "t4": 54, "tk": 90, "low": 54,
                 "ks": 18, "dd": 36}),
    ("int32", {"twb": 64, "r16": 16, "r16b": 16, "coli": 8, "c16": 54, "uoi": 24, "key": 162, "k1": 54, "k2": 54,
               "bq": 216, "lb": 54, "idx": 18, "kap": 54}),
    ("uint16", {"tw16": 64, "uoff": 24, "offn": 18, "offp": 18, "e2": 54, "e54": 54, "eg": 60,
                "osl": 6, "oto": 60, "esend": 24}),
    (FP8, {"wq": 512, "uq": 128, "uq2": 384, "vq": 128, "eq": 512, "mq": C}),
    ("uint8", {"wsc": 512, "us": 128, "us2": 384, "vs": 128, "es": 512, "ms": C}),
):
    for _n in _bufs:
        SCRATCH[_n] = ("sbuf", [128, _bufs[_n]], _d)
for _t in range(R + 1):
    SCRATCH["qx%d" % _t] = ("sbuf", [128, C], FP8)
    SCRATCH["sx%d" % _t] = ("sbuf", [128, C], "uint8")
for _t in range(R):
    SCRATCH["lq%d" % _t] = ("sbuf", [128, 2 * C], FP8)
    SCRATCH["ls%d" % _t] = ("sbuf", [128, 2 * C], "uint8")
    SCRATCH["lst%d" % _t] = ("sbuf", [128, 8], "uint16")

POOL = {"v": 48, "s": 36, "t": 24, "g": 14}
NDMA = 16
SEMAPHORES = (["%s%d" % (q, i) for q in POOL for i in range(POOL[q])] + ["d%d" % i for i in range(NDMA)]
              + ["%s%d" % (n, t) for n in ("fp", "fn", "lst") for t in range(R)] + ["sent"])

A = AluOpType
F = ActivationFunctionType


def meet(a, b):
    if a[0] != b[0] or a[2] <= b[1] or b[2] <= a[1]:
        return False
    return not (a[3] > 1 and a[3] == b[3] and (a[1] - b[1]) % a[3] != 0)


def clash(x, o):
    if o["kind"] == "remote":
        return False
    if any(meet(a, b) for a in x["r"] + x["w"] for b in o["w"]) or any(meet(a, b) for a in x["w"] for b in o["r"]):
        return True
    return o["q"] != x["q"] and any(a[0] == "ps" and meet(a, b) for a in x["r"] for b in o["r"])


def clashes(ops):
    seen, out = {}, []
    for i, x in enumerate(ops):
        names = {z[0] for z in x["r"] + x["w"]}
        near = set()
        for name in names:
            near.update(seen.setdefault(name, []))
            seen[name].append(i)
        out.append(sorted(j for j in near if clash(x, ops[j])))
    return out


def order(ops):
    n = len(ops)
    dep, back, last = [], [[] for _ in ops], {}
    must = clashes(ops)
    for i, x in enumerate(ops):
        d = {j: ops[j]["lat"] + WAKE for j in must[i]}
        for j, w in x["after"]:
            d[j] = max(d.get(j, 0), w)
        if x["q"] in "tgy":
            if x["q"] in last:
                d.setdefault(last[x["q"]], 0)
            last[x["q"]] = i
        reach = set()
        for j in d:
            reach.update(k for k, w in dep[j] if d.get(k, 0) <= WAKE)
        dep.append([(j, d[j]) for j in d if j not in reach])
        for j, w in dep[i]:
            back[j].append((i, w))
    slow = [[(j, SLOW.get(w, w) if ops[j]["kind"] == "remote" else w) for j, w in dep[i]] for i in range(n)]
    cases = [(dep, back), (slow, [[] for _ in ops])]
    for i in range(n):
        for j, w in slow[i]:
            cases[1][1][j].append((i, w))
    lat = [o["lat"] for o in ops]
    ways = [sorted((q, o["ways"][q][1]) for q in o["ways"]) for o in ops]
    cost = [dict(w) for w in ways]
    lean = [o.get("lean", LEAN) for o in ops]

    def place(key, edges, users, soonest, ways):
        end, queue, busy = [0] * n, [None] * n, {q: [] for q in "vstgy"}
        left = [len(e) for e in edges]
        ready = [i for i in range(n) if left[i] == 0]
        while ready:
            i = min(ready, key=lambda z: key[z])
            ready.remove(i)
            soon = max([soonest[i]] + [end[j] + w for j, w in edges[i]])
            pick = None
            for q, c in ways[i]:
                line, at = busy[q], soon
                k = len(line)
                while k and line[k - 1][1] > at:
                    k -= 1
                while k < len(line) and line[k][0] < at + c:
                    at = max(at, line[k][1])
                    k += 1
                if pick is None or at + c + lean[i] < pick[0]:
                    pick = (at + c, at, q, k)
            busy[pick[2]].insert(pick[3], (pick[1], pick[0]))
            end[i], queue[i] = pick[0], (pick[2], pick[0] - pick[1])
            for j, w in users[i]:
                left[j] -= 1
                if left[j] == 0:
                    ready.append(j)
        return end, queue

    price = {q: [c.get(q, 0) for c in cost] for q in "vstgy"}

    def run(lines, users, waits, soonest, opens, tail, most):
        end, why, left, soon = [0] * n, [None] * n, waits[:], soonest[:]
        state, moved = [[lines[q], 0, len(lines[q]), opens[q], None, price[q]] for q in lines if lines[q]], True
        while moved:
            moved = False
            for x in state:
                line, k, size, e, before, took = x
                if k == size or left[line[k]]:
                    continue
                moved = True
                while k < size:
                    i = line[k]
                    if left[i]:
                        break
                    if e > soon[i]:
                        soon[i], why[i] = e, before
                    else:
                        e = soon[i]
                    e = end[i] = e + took[i]
                    if e + tail[i] > most:
                        return None
                    for j, w in users[i]:
                        left[j] -= 1
                        if e + w > soon[j]:
                            soon[j], why[j] = e + w, i
                    before = -1 - i
                    k += 1
                x[1], x[3], x[4] = k, e, before
        return (end, why, soon) if all(x[1] == x[2] for x in state) else None

    def whole(lines):
        return run(lines, back, [len(e) for e in dep], [0] * n, {q: 0 for q in lines}, [0] * n, 1e9)

    def stretch(lines, lo, hi, passes, heat):
        soon = whole(lines)[2]
        mine = [i for i in range(n) if lo <= soon[i] < hi]
        free = [z for z in mine if ops[z]["q"][0] not in "tgy"]
        if len(free) < 2:
            return lines
        inside = set(mine)
        head = {q: [i for i in lines[q] if soon[i] < lo] for q in lines}
        foot = {q: [i for i in lines[q] if soon[i] >= hi] for q in lines}
        causes = [[x for x in e if x[0] in inside] for e in dep]
        waits = [len(e) for e in causes]
        frames = []
        for ins, outs in cases:
            end = run(lines, outs, [len(e) for e in ins], [0] * n, {q: 0 for q in lines}, [0] * n, 1e9)[0]
            rest = run({q: lines[q][::-1] for q in lines}, ins, [len(e) for e in outs], lat, {q: 0 for q in lines},
                       [0] * n, 1e9)[0]
            users = [[x for x in e if x[0] in inside] for e in outs]
            tail = [max([lat[i]] + [w + rest[j] for j, w in outs[i] if j not in inside]) for i in range(n)]
            reach = tail[:]
            for i in sorted(mine, key=lambda z: -soon[z]):
                reach[i] = max([tail[i]] + [w + min(cost[j].values()) + reach[j] for j, w in users[i]])
            frame = (users, [max([0] + [end[j] + w for j, w in e if j not in inside]) for e in ins],
                     {q: end[head[q][-1]] if head[q] else 0 for q in lines}, reach, tail,
                     {q: rest[foot[q][0]] if foot[q] else 0 for q in lines}, [z for z in mine if tail[z]])
            if any(dep[i] != slow[i] for i in mine) or not frames:
                frames.append(frame)
        users, soonest = frames[0][:2]
        now, top, trial = None, None, {q: [i for i in lines[q] if i in inside] for q in lines}
        dice, bell = rng.random_sample((passes, 7)).tolist(), rng.normal(0.0, 100.0, passes).tolist()
        for turn in range(passes):
            d = dice[turn]
            slack = -heat * (1 - turn / passes) * math.log(1 - d[0])
            seen = []
            for k, (outs, first, opens, reach, tail, shuts, outer) in enumerate(frames):
                got = run(trial, outs, waits, first, opens, reach, now[5][k] + 2 * slack + 200 if now else 1e9)
                if not got:
                    break
                end = got[0]
                seen.append(max([(end[z] + tail[z], z) for z in outer]
                                + [(end[trial[q][-1]] + shuts[q], trial[q][-1]) for q in trial if trial[q]]) + got)
            else:
                worth = sum(x[0] for x in seen) / len(seen) + SOFT * sum(seen[0][2]) / len(mine)
                if now is None or worth <= now[0] + slack:
                    held = []
                    for total, i, end, why, soon in seen:
                        while why[i] is not None:
                            j = why[i]
                            if j < 0:
                                j = -1 - j
                                if ops[i]["q"][0] not in "tgy":
                                    held.append((i, j))
                            i = j
                    now = (worth, trial, held, seen[0][4], seen[0][2], [x[0] for x in seen])
                    if top is None or worth < top[0]:
                        top = (worth, trial)
            trial = dict(now[1])
            how = int(8 * d[1])
            if how < 5 and now[2]:
                i, j = now[2][int(len(now[2]) * d[2])]
                x = (i, j)[how % 2]
            else:
                i, x = None, free[int(len(free) * d[2])]
            q = "v" if x in now[1]["v"] else "s"
            line = list(trial[q])
            k = line.index(x)
            del line[k]
            trial[q] = line
            if len(cost[x]) > 1 and d[3] < TRADE:
                other = list(trial["s" if q == "v" else "v"])
                near = [z for z in other if len(cost[z]) > 1 and abs(now[3][z] - now[3][x]) < 1200]
                if near:
                    z = near[int(len(near) * d[4])]
                    other[other.index(z)] = x
                    trial["s" if q == "v" else "v"], x = other, z
            elif ops[x]["kind"] == "op" and d[3] < JUMP:
                q = "sv"[int(2 * d[4])] if len(cost[x]) > 1 else q
                first = max([soonest[x]] + [now[4][z] + w for z, w in causes[x]])
                last = min([hi] + [now[3][z] - w for z, w in users[x]]) - cost[x][q]
                line, at = list(trial[q]), first + (last - first) * d[5] ** 2 + bell[turn]
                k = 0
                while k < len(line) and now[3][line[k]] < at:
                    k += 1
                trial[q] = line
            else:
                far = 1 + int(-2.0 * math.log(1 - d[6]))
                k = min(max(k - far if x == i or how == 6 else k + far, 0), len(line))
            line.insert(k, x)
        return {q: head[q] + top[1][q] + foot[q] for q in lines}

    key, best = [0] * n, None
    for i in range(n - 1, -1, -1):
        key[i] = min([-lat[i]] + [key[j] - w for j, w in back[i]]) - ways[i][0][1]
    for turn in range(4):
        end, queue = place(key, dep, back, [0] * n, ways)
        late = place([-e for e in end], back, dep, lat, [[x] for x in queue])[0]
        key = [ops[i]["first"] - 1e6 if "first" in ops[i] else -late[i] for i in range(n)]
        if turn == 1 or (turn > 1 and max(end) < best[0]):
            best = (max(end), end, queue)
    lines = {q: [i for i in sorted(range(n), key=lambda z: best[1][z]) if best[2][i][0] == q] for q in "vstgy"}
    rng = np.random.RandomState(SEED)
    for wide, passes, heat in SWEEPS:
        for lo in range(-wide // 2, int(best[0]), wide // 2):
            lines = stretch(lines, lo, lo + wide, passes, heat)
    end, why, soon = whole(lines)
    PLAN["total"] = max(end[i] + lat[i] for i in range(n))
    queue = [None] * n
    for q in lines:
        for i in lines[q]:
            queue[i] = q
    return sorted(range(n), key=lambda i: (soon[i], end[i])), queue


def emit(g, T, ops):
    Q = {"v": g.vector, "s": g.scalar, "t": g.tensor, "g": g, "y": g.sync}
    n = len(ops)
    known = {q: set() for q in Q}
    closure, waits, first, before, prev = [], [], {}, {}, {}
    must = clashes(ops)
    for i in range(n):
        q = ops[i]["q"]
        k = known[q]
        need = [j for j in must[i] if j not in k]
        keep = [j for j in need if not any(j in closure[x] for x in need if x != j)]
        for j in keep:
            k |= closure[j]
            k.add(j)
            first.setdefault(j, i)
        waits.append(keep)
        closure.append(set(k))
        before[i] = prev.get(q)
        prev[q] = i
    group = {}
    for i in sorted(first):
        j = before[i]
        if ops[i]["kind"] == "op" and j in group and ops[j]["kind"] == "op" and first[j] == first[i]:
            group[i] = group[j]
            group[i].append(i)
        else:
            group[i] = [i]
    known = {q: set() for q in Q}
    closure = []
    last = {q: [None] * POOL[q] for q in POOL}
    count = {q: [0] * POOL[q] for q in POOL}
    tag, ndma, stores, arrived = {}, [0], [], set()

    def learn(k, j):
        for x in group[j]:
            k |= closure[x]
            k.add(x)

    for i in range(n):
        o = ops[i]
        q = o["q"]
        k = known[q]
        ws = []
        for j in waits[i]:
            if j not in k:
                ws.append(j)
                learn(k, j)
        if o["kind"] == "dma":
            tag[i] = ("d%d" % ndma[0], 16)
            ndma[0] += 1
            if i not in first:
                stores.append((q, tag[i]))
        elif i in first and group[i][0] == i:
            free = [s for s in range(POOL[q]) if last[q][s] is None or last[q][s] in k]
            if free:
                s = min(free, key=lambda z: -1 if last[q][z] is None else last[q][z])
            else:
                s = min(range(POOL[q]), key=lambda z: last[q][z])
                ws.append(last[q][s])
                learn(k, last[q][s])
            last[q][s] = group[i][-1]
            count[q][s] += len(group[i])
            for x in group[i]:
                tag[x] = ("%s%d" % (q, s), count[q][s])
        for name, val in o["pre"]:
            if (q, name) not in arrived:
                arrived.add((q, name))
                Q[q].wait_ge(T.sem[name], val)
        for j in ws:
            Q[q].wait_ge(T.sem[tag[j][0]], tag[j][1])
        closure.append(set(k))
        ins = o["fn"](Q[q])
        if i in tag:
            ins.then_inc(T.sem[tag[i][0]], 16 if o["kind"] == "dma" else 1)
    for q, (name, val) in stores:
        Q[q].wait_ge(T.sem[name], val)


def rank_program(g, core, T, topo):
    rank = T.rank_of(core)
    if rank is None:
        return
    nr = len(T.cores)
    nxt, prv = T.cores[(rank + 1) % nr], T.cores[(rank - 1) % nr]
    ops = []
    sent = [0]

    def a(name, lo=0, hi=None, st=1):
        if hi is None:
            hi = SCRATCH[name][1][1]
        ap = T[name][:, lo:hi] if st == 1 else T[name][:, lo:hi:st]
        if name == "ps":
            return (ap, [("ps", lo // 512 * 512, lo // 512 * 512 + 512, 1)], hi - lo)
        return (ap, [(name, lo, hi, st)], len(range(lo, hi, st)))

    def ends(name, lo, hi):
        return a(name, 16 * lo + 15, 16 * hi, 16)

    def step(buf, k, lo, hi, n=4):
        return a(buf, n * lo + k, n * hi, n)

    def bank(b, n=C):
        return a("ps", 512 * b, 512 * b + n)

    def half(name, h, at=0, n=1):
        return a(name, at + n * CUT[h], at + n * CUT[h + 1])

    def hbank(b, h):
        return bank(b, CUT[h + 1] - CUT[h])

    def ind(win, off):
        return (win[0].indirect(off[0]), win[1] + off[1], -1)

    def rec(q, fn, rd, wr, cost, kind="op", pre=(), after=(), lat=0):
        r = []
        for x in rd:
            if isinstance(x, tuple):
                r += x[1]
                if x[2] < 0:
                    cost = 60 + 1.3 * wr[0][2]
        w = []
        for x in wr:
            w += x[1]
        ops.append({"q": q, "ways": {q: (fn, max(cost, 55))}, "r": r, "w": w, "kind": kind, "pre": list(pre),
                    "after": list(after), "lat": lat})
        return len(ops) - 1

    def val(x):
        return x[0] if isinstance(x, tuple) else x

    def per(*xs):
        return 0.42 if all(SCRATCH[x[1][0][0]][2] == "bfloat16" for x in xs) else 0.83

    def act(o, x, bias=0.0, scale=1.0, pre=(), after=(), only=None):
        i = rec("s", lambda e: e.activation(o[0], x[0], F.Identity, bias=val(bias), scale=val(scale)), [x, bias, scale],
                [o], 60 + o[2] * 0.83, pre=pre, after=after)
        if only != "s":
            plain = bias == 0.0 and scale == 1.0
            fn = ((lambda e: e.tensor_copy(o[0], x[0])) if plain
                  else (lambda e: e.tensor_scalar(o[0], x[0], val(scale), val(bias), A.mult, A.add)))
            ops[i]["ways"]["v"] = (fn, 50 + 1.3 * o[2] if x[2] < 0 else max(55, o[2] * per(o, x)))
            ops[i]["q"] = "e%d" % i
        return i

    def tt(o, x, y, op):
        rec("v", lambda e: e.tensor_tensor(o[0], x[0], y[0], op), [x, y], [o], o[2] * (0.83 if x[1][0][0] == "ps" else 1.66))

    def ts(o, x, s1, op0, s2=None, op1=None):
        if op1 is None:
            rec("v", lambda e: e.tensor_scalar(o[0], x[0], val(s1), None, op0), [x, s1], [o], o[2] * per(o, x))
        else:
            rec("v", lambda e: e.tensor_scalar(o[0], x[0], val(s1), val(s2), op0, op1), [x, s1, s2], [o], o[2] * per(o, x))

    def cp(o, x):
        rec("v", lambda e: e.tensor_copy(o[0], x[0]), [x], [o], o[2] * per(o, x))

    def ms(o, c):
        rec("v", lambda e: e.memset(o[0], c), [], [o], o[2] * per(o))

    def scan(o, x, m=None, op0=A.mult, op1=A.add):
        m = m or a("cm", 0, o[2])
        rec("v", lambda e: e.tensor_tensor_scan(o[0], m[0], x[0], 0.0, op0, op1), [m, x], [o], o[2] * per(o, x, m))

    def quant(q, s, x):
        rec("v", lambda e: e.quantize_mx(q[0], s[0], x[0]), [x], [q, s], 12 + 0.22 * x[2])

    def mm(o, wq, wsc, xq, xs, pre=(), after=(), start=True, stop=True):
        rec("t", lambda e: e.matmul_mx(o[0], wq[0], wsc[0], xq[0], xs[0], start, stop), [wq, wsc, xq, xs], [o],
            10 + 0.6 * o[2], pre=pre, after=after)

    def dma(q, o, x, rd=(), wr=(), lat=2000):
        rec(q, lambda e: e.dma_start(o, x), list(rd), list(wr), 100, kind="dma", lat=lat)

    def iota(o, pattern, base, cmul, small=False):
        if small:
            rec("g", lambda e: e.iota(o[0], pattern, base, cmul, allow_small_or_imprecise_dtypes=True), [], [o], 130 + 1.7 * o[2])
        else:
            rec("g", lambda e: e.iota(o[0], pattern, base, cmul), [], [o], 130 + 1.7 * o[2])

    def part(src, dst, which):
        en = topo.engines(src, dst)
        return en if which == "all" else en[:len(en) // 2] if which == "low" else en[len(en) // 2:]

    def send(pieces, rd):
        tr = []
        for dst, which, sem, s_, d_ in pieces:
            rid, pid = topo.addr(dst)[:2]
            en = part(core, dst, which)
            sent[0] += len(en)
            tr.append(RemoteDMATransfer(dst_ids=[DstId(rid=rid, pnc=pid)], dma_engine_mask=sum(1 << e for e in en),
                                        remote_sem=T.sem[sem], src=s_, dst=d_))
        return rec("g", lambda e: e.remote_dma_fused(tr, local_sem=T.sem.sent), rd, [],
                   300 if sent[0] > len(en) else 300 + LAG_1, kind="remote")

    from_prv = 2 * len(part(prv, core, "all"))
    from_nxt = 2 * len(part(nxt, core, "all"))
    lists_in = len(part(prv, core, "low")) + len(part(nxt, core, "high"))

    (c_big, c_inv, c_half, c_own, c_col, c_pm, c_last, c_rest, c_y,
     c_less) = [a("col", i, i + 1) for i in range(10)]
    c_near = {k: a("col", 13 + k, 14 + k) for k in range(-2, 3)}

    def column(o, x):
        ts(o, x, 0.2, A.mult, -0.2, A.add)

    def near(o, z, k, op=A.is_equal):
        ts(o, z, c_near[k], A.add, c_near[0], op)

    def moved(m, x, lo, hi, z, n=4):
        near(step(m, 1, lo, hi, n), z, 0)
        near(step(x, 2, lo, hi, n), z, 2)
        near(step(x, 3, lo, hi, n), z, -1, A.not_equal)

    def keys():
        tt(a("low"), a("lab"), a("tb", 0, 54), A.min)
        act(a("pr"), a("low"), (5 * C + 1) * 8192.0, -8192.0)
        act(a("t4"), a("tb", 0, 54), 0.0, 4.0)
        tt(a("tk", 0, 54), a("t4"), a("kap"), A.add)
        act(a("tk", 54, 90), a("tk", 0, 36))
        tt(a("kk", 0, 54), a("pr"), a("tb", 0, 54), A.add)
        act(step("kq", 0, 0, 18), a("tb", 0, 18), 2048.0, 1.0)
        for s_ in (1, 2):
            tt(a("kk", 54 * s_, 54 * s_ + 54), a("pr"), a("tk", 18 * s_, 18 * s_ + 54), A.add)
        act(step("kq", 0, 18, 54), a("tk", 18, 54))

    def slots(x):
        ts(a("osl"), x, 1.0, A.add)
        act(a("ys"), ind(a("turn"), a("osl")), 0.0, 4097.0)
        act(step("s1", 1, 0, 6, 5), x, c_less, c_big)

    def pick_u(lo, hi):
        o = a("uoff", lo // 16, hi // 16)
        rec("v", lambda e: e.tensor_copy(T.uq2[:, lo:hi].bitcast(dt.uint32), T.uq[:, 0:128].bitcast(dt.uint32).indirect(o[0])),
            [a("uq"), o], [a("uq2", lo, hi)], 60 + 1.3 * (hi - lo))
        x = ind(a("us"), o)
        rec("s", lambda e: e.activation(T.us2[:, lo:hi], x[0], F.Copy), [x], [a("us2", lo, hi)], 0)

    def tile_e(b):
        return a("eq", 128 * b, 128 * b + 128), a("es", 128 * b, 128 * b + 128)

    def state(t, h):
        q_, s_ = half("qx%d" % t, h), half("sx%d" % t, h)
        quant(q_, s_, half("xt" if t else "xin", h, 0, 4))
        if t < R:
            mm(hbank(h, h), a("uq2", 128 * t, 128 * t + 128), a("us2", 128 * t, 128 * t + 128), q_, s_)
            ts(half("sg", h), hbank(h, h), 0.0, A.is_gt, 0.5, A.subtract)
        else:
            mm(hbank(h, h), a("vq"), a("vs"), q_, s_)

    dma("y", T.twb[:, 0:60], T.tw[:], wr=[a("twb")], lat=1300)
    dma("s", T.ub[:], T.u[:], wr=[a("ub")], lat=1600)
    dma("y", T.xin[:], T.x[:], wr=[a("xin")], lat=2400)
    dma("y", T.wq[:].bitcast(dt.uint8), T.wc[:], rd=[a("xin")], wr=[a("wq")], lat=4000)
    dma("y", T.wsc[:], T.ws[:], wr=[a("wsc")], lat=4000)
    dma("y", T.vb[:], T.v[:], wr=[a("vb")], lat=4500)
    ms(a("ones"), 1.0)
    ms(a("eb"), 0.0)
    iota(a("r16"), [[1, 16]], 128, -1)
    iota(a("base"), [[5, 390]], 0, 0, True)
    rec("g", lambda e: e.affine_select(T.eb[:, 3:515:4], T.ones[:], [[-1, 128]], A.is_equal, 0.0, 0, 1),
        [a("ones")], [a("eb", 3, 515, 4)], 400)
    for b in range(4):
        quant(tile_e(b)[0], tile_e(b)[1], a("eb", 3 - b, 515 - b))
    iota(a("uoi"), [[1, 3], [16, 8]], 0, 0)
    iota(a("c16"), [[1, 3], [80, 18]], 0, 0)
    iota(a("kap"), [[1, 3], [0, 18]], 0, 0)
    iota(a("row", 0, 5), [[-1, 5]], 3 * 2 ** 22 + 2, 0, True)
    iota(a("row", 5, 7), [[-4098, 2]], 4097, 0, True)

    def turns(lo, hi):
        for k in range(lo, hi):
            iota(a("turn", k, 1950, 5), [[5, 390]], (2, 0, 1, 2, 0)[k], 0, True)

    def fill(o, c):
        act(o, a("ones", 0, o[2]), 0.0, float(c))

    turns(0, TURNS)
    fill(step("s1", 4, 0, 3, 5), 5 * C)
    fill(step("s1", 4, 3, 6, 5), 0)

    fill(a("turn", 1950), 2047 + 30)
    for name, c in (("nf", NOWHERE), ("inf", NOWHERE), ("pf", 0)):
        fill(a(name, C, 384), c)
    for k, c in ((0, 0), (3, 2), (4, 1)):
        fill(step("s0", k, 0, 6, 5), c)
    for k in range(TURNS, 5):
        act(a("turn", k, 1950, 5), a("base"), (2.0, 0.0, 1.0, 2.0, 0.0)[k], 1.0)
    ms(a("four"), 0.0)
    ms(step("four", 0, 0, 18), -1e9)
    for k in range(3):
        act(a("inttab", k, 3 * C, 3), a("base", 0, C), float(k), 1.0)
    act(a("inttab", 3 * C, 960), a("base", C, 384))
    ts(a("r16b"), a("r16"), 15, A.bitwise_and)
    ts(a("coli", 0, 1), a("r16", 0, 1), -1.0, A.mult, 128.0, A.add)
    ts(a("c0"), a("r16b"), 0.0, A.not_equal)
    ts(a("c1"), a("r16b"), 1.0, A.is_equal, BIG, A.mult)
    ts(c_last, a("r16b", 0, 1), 1.0, A.is_equal)
    ts(c_rest, a("r16b", 0, 1), 1.0, A.not_equal)
    ts(a("coli", 1, 2), a("coli", 0, 1), 15, A.bitwise_and)
    tt(a("cm", 0, 16), a("c0"), a("c1"), A.max)
    act(c_inv, c_last, 1.0 / BIG, 1.0)
    act(c_big, c_rest, 1.0, BIG)
    ts(c_pm, a("coli", 1, 2), 5.0, A.mult)
    ts(c_own, c_inv, c_inv, A.mult, -4.0, A.mult)
    act(c_col, c_inv, 0.0, 0.2)
    act(c_half, c_inv, 0.0, 0.5)
    ts(a("col", 11, 16), a("row", 0, 5), 4096.0, A.mult, c_big, A.mult)
    act(a("col", 8, 10), a("row", 5, 7), 0.0, c_big)
    for lo, n in ((16, 16), (32, 16), (48, 16), (64, 64), (128, 64), (192, 64), (256, 64), (320, 64)):
        act(a("cm", lo, lo + n), a("cm", 0, n))
    act(a("sg", C, 384), a("ones", 0, 96), 0.0, 0.0)
    for buf, n, runs in (("f0", 4, 54), ("s0", 5, 6)):
        act(step(buf, 2, 0, runs, n), a("ones", 0, runs), 0.0, c_half)
    cp(a("tw16", 0, 60), a("twb", 0, 60))
    cp(a("uoff"), a("uoi"))
    for lo, hi in TFN:
        act(a("tfn", 16 * lo, 16 * hi), ind(a("inttab"), a("tw16", lo, hi)))
    quant(a("uq"), a("us"), a("ub"))
    pick_u(0, 128)
    state(0, 0)
    state(0, 1)
    for k in range(3):
        scan(a("so", C * k, C * k + C), a("tfn", k, 3 * C, 3))
    scan(a("so", 3 * C, 960), a("tfn", 3 * C, 960))
    act(a("tb"), ends("so", 0, 60), 0.0, c_inv)
    ts(a("k1"), a("twb", 0, 54), 1.0 / 3, A.mult, -1.0 / 3, A.add)
    ts(a("k2"), a("twb", 0, 54), -2.0 * C, A.add)
    tt(a("lb"), a("k1"), a("k2"), A.max)
    cp(a("eg", 0, 54), a("lb"))
    column(a("eg", 54, 60), a("tb", 54, 60))
    ts(a("lab"), a("c16"), c_pm, A.add)
    tt(a("v5"), a("lab"), a("kap"), A.subtract)
    keys()
    for o in ops:
        name, lo = o["w"][0][:2]
        if name in FIRST and (name, lo) != ("sg", C):
            o["first"] = FIRST.index(name)
            o["lean"] = -1e4 if (name, lo) in ON_VECTOR else 1e4
    slots(a("tb", 54, 60))
    ms(a("two"), 0.0)
    ms(a("two", 0, 320, 2), -1e29)

    for t in range(R):
        more = t < R - 1
        qx, sx = a("qx%d" % t), a("sx%d" % t)
        lq, ls, lst, fp, fn = "lq%d" % t, "ls%d" % t, "lst%d" % t, "fp%d" % t, "fn%d" % t
        u8 = qx[0].bitcast(dt.uint8)
        big = send([(nxt, "all", fp, u8, T[lq][:, C:2 * C].bitcast(dt.uint8))], [qx])
        send([(nxt, "all", fp, sx[0], T[ls][:, C:2 * C])], [sx])
        send([(prv, "all", fn, u8, T[lq][:, 0:C].bitcast(dt.uint8))], [qx])
        send([(prv, "all", fn, sx[0], T[ls][:, 0:C])], [sx])
        if t == 0:
            iota(a("h0"), [[0, 18], [1, 3]], 0, 0, True)
            for k in (0, 3):
                iota(step("f0", k, 0, 54), [[0, 54]], 2 * k // 3, 0, True)

        for k, (lo, hi) in enumerate(SPLIT):
            ops[act(a("bits", 16 * lo, 16 * hi), ind(a("sg"), a("eg", lo, hi)))]["lean"] = 1e4 if k else -1e4
            if t:
                scan(a("sb", 16 * lo, 16 * hi), a("bits", 16 * lo, 16 * hi))
        scan(a("sbo"), a("sg", 0, C))
        for k in range(3):
            act(a("own", 18 * k, 18 * k + 18), ends("sbo", 0, 18), 0.0, c_own)
        if not t:
            for k in range(3):
                scan(a("sb", C * k, C * k + C), a("bits", k, 864, 3))
        for b in range(4):
            mm(bank(4 + b), tile_e(b)[0], tile_e(b)[1], qx, sx)
            act(a("dw", 384 * b, 384 * b + C), bank(4 + b), 0.0, 0.015625)
            ops[act(a("du", C * b, C * b + C), a("dw", 384 * b, 384 * b + C), 0.0, 64.0, after=[(big, 0)])]["lean"] = 1e4
        for h in (1, 0):
            for b in range(4):
                bk = bank(b + 4 * (1 - h))
                mm(bk, tile_e(b)[0], tile_e(b)[1], a(lq, C * h, C * h + C), a(ls, C * h, C * h + C),
                   [(fp, from_prv) if h else (fn, from_nxt)],
                   [(big, LAG_A if h else LAG_B)])
                act(a("dn", 576 * b + C * h, 576 * b + C * h + C), bk, 0.0, 0.015625)
        for h in range(2):
            for b in range(4):
                mm(hbank(4 * h + b, h), tile_e(b)[0], tile_e(b)[1], half("qx%d" % t, h), half("sx%d" % t, h), stop=False)
        if not t or SIGNED < 3:
            tt(a("w"), ends("sb", 0, 54), a("own"), A.mult)
        for s_ in range(3):
            ahead = t and s_ < SIGNED
            if ahead:
                tt(a("ko", 54 * s_, 54 * s_ + 54), a("kk", 54 * s_, 54 * s_ + 54), a("own"), A.mult)
            for k in range(3):
                lo, hi, at = 18 * k, 18 * k + 18, 54 * s_ + 18 * k
                tt(step("kq", k + 1, 18 * s_, 18 * s_ + 18), ends("sb", lo, hi) if ahead else a("w", lo, hi),
                   a("ko" if ahead else "kk", at, at + 18), A.mult)
            scan(a("bq", 72 * s_, 72 * s_ + 72), a("kq", 72 * s_, 72 * s_ + 72), a("four"), A.add, A.max)
        ts(a("idx"), step("bq", 3, 0, 18), 4095, A.bitwise_and)
        ts(a("lb", 0, 18), step("bq", 3, 0, 18), 2047, A.bitwise_and)
        ts(a("offn"), a("idx"), float(NONE), A.min)
        column(a("e2", 0, 18), a("lb", 0, 18))
        for s_, lo in ((1, 36), (2, 18)):
            ts(a("lb", lo, lo + 18), step("bq", 3, 18 * s_, 18 * s_ + 18), 2, A.logical_shift_right, 2047, A.bitwise_and)
        ts(a("kap", 18, 54), step("bq", 3, 18, 54), 3, A.bitwise_and)
        ts(a("offp"), a("lb", 36, 54), 1.0, A.add)
        column(a("e2", 18, 36), a("lb", 18, 36))
        act(a("nf", 0, C), ind(a("turn", 32), a("offn")), -30 * 4096.0, 4096.0)
        ops[act(a("af"), ind(a("turn"), a("offn")))]["lean"] = -1e4
        act(a("pf", 0, C), ind(a("turn"), a("offp")))
        tt(a("inf", 0, C), ind(a("nf"), a("e2", 0, 18)), a("af"), A.add)
        tt(a("gf", 864, 960), ind(a("inf"), a("eg", 54, 60)), a("ys"), A.subtract)
        scan(a("so", 864, 960), a("gf", 864, 960))
        act(step("s1", 0, 0, 6, 5), ends("so", 54, 60))
        moved("s0", "s1", 0, 6, ends("so", 54, 60), 5)
        scan(a("sn"), a("s1"), a("s0"))
        column(a("esend", 8 * t, 8 * t + 6), step("sn", 4, 0, 6, 5))
        ea, eb_ = a("esend", 8 * t, 8 * t + 3), a("esend", 8 * t + 3, 8 * t + 6)
        small = send([(nxt, "low", lst, ea[0], T[lst][:, 3:6]), (prv, "high", lst, eb_[0], T[lst][:, 0:3])], [ea, eb_])
        if t == 0:
            iota(a("otab", 0, 5 * C), [[3, C], [1, 5]], 0, 0, True)
            iota(a("otab", 5 * C, NONE), [[1, 2 * S], [0, 5]], 3 * C, 0, True)
        act(a("bo"), ind(a("pf"), a("e2", 0, 18)))
        ts(step("f1", 1, 0, 36), a("lb", 0, 36), c_big, A.mult, c_less, A.add)
        ts(a("yy", 0, 36), a("lb", 0, 36), c_y, A.mult)
        ts(step("h1", 2, 0, 18, 3), a("lb", 36, 54), c_big, A.mult)

        def read(k):
            lo, hi = 18 * k, 18 * k + 18
            act(a("gf", C * k, C * k + C), ind(a("inf"), a("e2", lo, hi)))
            scan(a("so", C * k, C * k + C), a("gf", C * k, C * k + C))
            tt(step("f1", 0, lo, hi), ends("so", lo, hi), a("yy", lo, hi), A.subtract)

        def go(lo, hi):
            moved("f0", "f1", lo, hi, step("f1", 0, lo, hi))
            scan(a("fo", 4 * lo, 4 * hi), a("f1", 4 * lo, 4 * hi), a("f0", 4 * lo, 4 * hi))
            column(a("e54", lo, hi), step("fo", 3, lo, hi))

        read(0)
        read(1)
        go(0, 36)
        flips, third_ = step("ho", 1, 0, 18, 3), step("ho", 2, 0, 18, 3)
        near(step("h1", 0, 0, 18, 3), step("f1", 0, 0, 18), 1)
        near(step("h1", 1, 0, 18, 3), step("f1", 0, 0, 18), -2)
        scan(a("sp"), a("bo"))
        tt(step("h0", 2, 0, 18, 3), ends("sp", 0, 18), step("h1", 2, 0, 18, 3), A.subtract)
        scan(a("ho"), a("h1"), a("h0"))
        ts(a("e2", 36, 54), third_, c_col, A.mult, -0.2, A.add)
        act(a("yy", 36, 54), third_, 0.0, 4097.0)
        act(step("f1", 1, 36, 54), third_, c_less, 1.0)
        read(2)
        go(36, 54)
        new = [step("fo", 3, 18 * k, 18 * k + 18) for k in range(3)]
        tt(a("ks"), a("kap", 18, 36), a("kap", 36, 54), A.add)
        ts(a("kap", 0, 18), a("ks"), -1.0, A.mult, 3.0, A.add)

        def swap(o1, o2, x1, x2):
            tt(a("dd", 0, 18), x1, x2, A.subtract)
            tt(a("dd", 18, 36), a("dd", 0, 18), flips, A.mult)
            tt(o1, x2, a("dd", 18, 36), A.add)
            tt(o2, x1, a("dd", 18, 36), A.subtract)

        if more:
            act(a("tb", 0, 18), new[0])
            act(a("tb", 54, 60), step("sn", 3, 0, 6, 5))
            swap(a("tb", 18, 36), a("tb", 36, 54), new[1], new[2])
            tt(a("lab"), a("kap"), a("v5"), A.add)
            column(a("eg"), a("tb"))
            keys()
            slots(step("sn", 3, 0, 6, 5))
        else:
            cp(a("lab", 0, 18), a("kap", 0, 18))
            swap(a("lab", 18, 36), a("lab", 36, 54), a("kap", 18, 36), a("kap", 36, 54))
            for s_ in range(3):
                ts(a("kk", 54 * s_, 54 * s_ + 54), a("lab"), float(s_), A.is_equal, 4096.0, A.mult)
                tt(a("key", s_, 162, 3), a("kk", 54 * s_, 54 * s_ + 54), step("fo", 3, 0, 54), A.add)
            cp(a("oto", 54, 60), step("sn", 3, 0, 6, 5))
            tt(a("k1"), a("key", 0, 54), a("key", 54, 108), A.max)
            tt(a("k2"), a("k1"), a("key", 108, 162), A.max)
            for s_ in range(3):
                ts(a("oto", 18 * s_, 18 * s_ + 18), a("k2", s_, 54, 3), -4096.0, A.add)
                act(a("otf", s_, 3 * C, 3), ind(a("otab"), a("oto", 18 * s_, 18 * s_ + 18)))
            act(a("otf", 3 * C, 960), ind(a("otab"), a("oto", 54, 60)))
            dma("y", T.ot[:], T.otf[0:128:16, :], rd=[a("otf")], lat=1500)

        def plane(b):
            return a("dw", 384 * b, 384 * b + 384)

        for b in range(4):
            act(a("dw", 384 * b + C, 384 * b + 384), ind(a("dn", 576 * b, 576 * b + 576), a(lst, 0, 6)),
                pre=[(lst, lists_in)], after=[(small, LAG_L)])
        for p_, (c0, c1) in enumerate(PARTS):
            third = [a("e54", 18 * k + c0 // 16, 18 * k + c1 // 16) for k in range(3)]
            for b in range(4):
                g0, g1 = a("g0", C * b + c0, C * b + c1), a("g1", C * b + c0, C * b + c1)
                if WAYS[p_][b] < 3:
                    act(g0, ind(plane(b), third[0]))
                    tt(g1, ind(plane(b), third[1]), g0, A.max)
                else:
                    lo, hi = 2 * (C * b + c0), 2 * (C * b + c1)
                    for k in range(2):
                        act(a("gi", lo + k, hi, 2), ind(plane(b), third[k]))
                    scan(a("go", lo, hi), a("gi", lo, hi), a("two", 0, hi - lo), A.add, A.max)
                    g1 = a("go", lo + 1, hi, 2)
                tt(a("mt", 4 * c0 + b, 4 * c1, 4), ind(plane(b), third[2]), g1, A.max)
        if more:
            pick_u(128 * t + 128, 128 * t + 256)
            ops[-2]["after"], ops[-1]["after"] = [(small, 0)], [(small, 0)]
        if t == 1:
            quant(a("vq"), a("vs"), a("vb"))
            ops[-1]["after"] = [(big, 500)]
        for h in range(2):
            quant(half("mq", h), half("ms", h), half("mt", h, 0, 4))
            for b in range(4):
                mm(hbank(4 * h + b, h), a("wq", 128 * b, 128 * b + 128), a("wsc", 128 * b, 128 * b + 128),
                   half("mq", h), half("ms", h), start=False)
        for h in range(2):
            for b in range(4):
                tt(a("xt", 4 * CUT[h] + b, 4 * CUT[h + 1], 4), hbank(4 * h + b, h), half("du", h, C * b), A.max)
        state(t + 1, 0)
        state(t + 1, 1)

    qx, sx = a("qx%d" % R), a("sx%d" % R)
    for h in range(2):
        act(half("yb", h), hbank(h, h))
    dma("y", T.oc[:], qx[0].bitcast(dt.uint8), rd=[qx], lat=1500)
    dma("y", T.y[:], T.yb[:], rd=[a("yb")], lat=1500)
    for k in range(4):
        dma("s", T.osc[4 * k:4 * k + 4, :], T["sx%d" % R][32 * k:32 * k + 4, :], rd=[sx], lat=1200)
    if "order" not in PLAN:
        PLAN["order"] = order(ops)
    turns, queues = PLAN["order"]
    for o, q in zip(ops, queues):
        o["q"], o["fn"] = q, o["ways"][q][0]
    emit(g, T, [ops[i] for i in turns])
    g.wait_ge(T.sem.sent, sent[0])
